import numpy as np
import ml_dtypes


def mxq(x, axis, fmt="e4m3"):
    dtype, down = {"e4m3": (ml_dtypes.float8_e4m3fn, 7), "e5m2": (ml_dtypes.float8_e5m2, 14)}[fmt]
    v = np.moveaxis(np.asarray(x, np.float32).astype(ml_dtypes.bfloat16).astype(np.float64), axis, -1)
    blocks = v.reshape(v.shape[:-1] + (-1, 32))
    amax = np.abs(blocks).max(-1, keepdims=True)
    byte = np.maximum(np.where(amax > 0, np.frexp(amax)[1] - 1 + 127, 0) - down, 1)
    scale = np.exp2(byte - 127.0)
    codes = (blocks / scale).astype(np.float32).astype(dtype).astype(np.float64)
    return np.moveaxis((codes * scale).reshape(v.shape), -1, axis)


WIDE = False


def mx_kscale(k):
    if not WIDE:
        return np.ones(k)
    levels = np.array([10, -10, 5, -5, 0])
    if k % 512:
        return np.exp2(np.random.permutation(np.resize(levels, k // 32))).repeat(32)
    a = np.empty((k // 512, 16))
    for p in range(k // 512):
        a[p, :8] = np.random.permutation(np.resize(levels, 8))
        for g in range(8):
            far = levels[np.abs(levels - a[p, g]) >= 10]
            a[p, g + 8] = far[np.random.randint(len(far))]
    return np.exp2(a.ravel()).repeat(32)


def f64(x):
    return np.asarray(x).astype(np.float64)


def striped(idx):
    return np.tile(np.asarray(idx).reshape(-1, 16).T, (8, 1)).astype(np.uint16)


def unstriped(offs):
    return offs[:16].T.reshape(-1).astype(np.int64)


E2M1 = np.array([0.0, 0.5, 1.0, 1.5, 2.0, 3.0, 4.0, 6.0, -0.0, -0.5, -1.0, -1.5, -2.0, -3.0, -4.0, -6.0])


def pack_weight(w, fmt):
    k, n = w.shape
    w = f64(np.asarray(w, np.float32).astype(ml_dtypes.bfloat16)).reshape(k // 32, 32, n)
    amax = np.abs(w).max(1)
    if fmt == "e4m3":
        byte = np.frexp(amax)[1] - 1 + 127 - 7
    else:
        mant, ex = np.frexp(amax / 6.0)
        byte = np.where(mant > 0.5, ex, ex - 1) + 127
    byte = np.clip(np.where(amax > 0, byte, 1), 1, 254)
    scaled = (w * np.exp2(127.0 - byte)[:, None, :]).reshape(k, n).astype(np.float32)
    by_word = np.ascontiguousarray(scaled.reshape(k // 512, 128, 4, n).transpose(0, 1, 3, 2))
    if fmt == "e4m3":
        words = by_word.astype(ml_dtypes.float8_e4m3fn).view(np.uint8)
    else:
        c = by_word.astype(ml_dtypes.float4_e2m1fn).view(np.uint8) & 0xF
        words = (c[..., 0::2] | (c[..., 1::2] << 4)).reshape(k // 512, 128, 2 * n)
    return np.ascontiguousarray(words), np.ascontiguousarray(byte.astype(np.uint8).reshape(k // 512, 16, n))


def unpack_weight(words, scales, fmt):
    g, _, n = scales.shape
    words = np.ascontiguousarray(words).reshape(g, 128, n, -1)
    if fmt == "e4m3":
        vals = words.view(ml_dtypes.float8_e4m3fn).astype(np.float64)
    else:
        nib = np.empty((g, 128, n, 4), np.uint8)
        nib[..., 0::2] = words & 0xF
        nib[..., 1::2] = words >> 4
        vals = E2M1[nib]
    vals = vals * np.repeat(np.exp2(scales.astype(np.float64) - 127.0), 8, axis=1)[..., None]
    return vals.transpose(0, 1, 3, 2).reshape(g * 512, n)


def bf(x):
    return np.asarray(x, np.float32).astype(ml_dtypes.bfloat16)


def planes(Y):
    r, m = Y.shape
    b = f64(bf(Y)).reshape(r // 32, 32, m)
    amax = np.abs(b).max(1)
    byte = np.clip(np.where(amax > 0, np.frexp(amax)[1] - 1 + 127 - 7, 1), 1, 254)
    codes = (b * np.exp2(127.0 - byte)[:, None, :]).reshape(r, m).astype(np.float32).astype(ml_dtypes.float8_e4m3fn).view(np.uint8)
    words = codes.reshape(r // 512, 128, 4, m).transpose(0, 1, 3, 2)
    return np.ascontiguousarray(words), np.ascontiguousarray(byte.astype(np.uint8).reshape(r // 512, 16, m))


D, T, J, I, E = 512, 2048, 512, 512, 512


def setup_inputs():
    n = np.random.standard_normal
    idx = np.random.permutation(T)[:I]
    idx2 = np.random.permutation(T)[:J]
    fd = mx_kscale(D)
    fj = mx_kscale(J)
    tj = np.ones(T)
    tj[idx2] = fj
    ekeyp = pack_weight(n((D, T)) * 0.5 / np.sqrt(D) * fd[:, None], "e4m3")
    keysp = pack_weight(n((D, T)) / fd[:, None], "e4m3")
    return {
        "ekey_words": ekeyp[0],
        "ekey_scales": ekeyp[1],
        "keys_words": keysp[0],
        "keys_scales": keysp[1],
        "fac": (np.random.uniform(0.5, 2.0, (J, 1)) * fj[:, None]).astype(np.float32),
        "evals": (n((E, T)) * 4.0 / tj).astype(np.float32),
        "vals": (n((E, T)) * 0.3).astype(np.float32),
        "offs": striped(idx),
        "offs2": striped(idx2),
    }


def reference(ekey_words, ekey_scales, keys_words, keys_scales, fac, evals, vals, offs, offs2):
    idx = unstriped(offs)
    idx2 = unstriped(offs2)
    ekeyu = unpack_weight(ekey_words, ekey_scales, "e4m3")
    keysu = unpack_weight(keys_words, keys_scales, "e4m3")
    ekeyidx2g = ekeyu[:, idx2]
    keysidxg = keysu[:, idx]
    a = ekeyidx2g.T @ keysidxg
    p = np.exp(a - np.max(a, axis=1, keepdims=True))
    w = p * f64(fac) / np.sum(p, axis=1, keepdims=True)
    vt = f64(evals)[:, idx2].T
    vtq = mxq(vt, 0, "e4m3")
    wq = mxq(w, 0, "e4m3")
    o = vtq.T @ wq
    y = f64(vals)[:, idx] + o
    words, scales = planes(y)
    return y, words, scales

@@ -1,0 +1,164 @@
+from contextlib import ExitStack
+
+import concourse.mybir as mybir
+from concourse.masks import make_identity
+
+D, T, J, I, E = 512, 2048, 512, 512, 512
+FLOPS = 2 * D * J * I + 2 * J * E * I
+
+F32 = mybir.dt.float32
+BF16 = mybir.dt.bfloat16
+I32 = mybir.dt.int32
+U32 = mybir.dt.uint32
+U16 = mybir.dt.uint16
+U8 = mybir.dt.uint8
+FP8X4 = mybir.dt.float8_e4m3fn_x4
+ALU = mybir.AluOpType
+ACT = mybir.ActivationFunctionType
+AXIS = mybir.AxisListType
+
+P = 128
+PACK = 4
+QUADS = 4
+HALF = I // 2
+KEPT_ROW = 4
+
+
+def tile_attend_softmerge_pl_kernel(tc, ekey_words, ekey_scales, keys_words, keys_scales, fac, evals, vals, offs, offs2, out_0, out_1, out_2):
+    nc = tc.nc
+    with ExitStack() as ctx:
+        held = ctx.enter_context(tc.tile_pool(name="held", bufs=1))
+        ring = ctx.enter_context(tc.tile_pool(name="ring", bufs=4))
+        psum = ctx.enter_context(tc.psum_pool(name="psum", bufs=4))
+
+        def sbuf(name, shape, dtype):
+            return held.tile(shape, dtype, name=name, align_bytes=64)
+
+        def window(dtype):
+            return ring.tile([P, T], dtype, name="window", align_bytes=64)
+
+        kept_list = held.tile([P, I // 16], U16, name="kept_list")
+        evicted_list = held.tile([P, J // 16], U16, name="evicted_list")
+
+        ekey_byte_pool = window(U8)
+        ekey_word_pool = window(U32)
+        keys_word_pool = window(U32)
+        keys_byte_pool = window(U8)
+        nc.vector.memset(ekey_byte_pool[:].bitcast(I32), 0)
+        nc.vector.memset(keys_byte_pool[:].bitcast(I32), 0)
+
+        nc.sync.dma_start(evicted_list[:], offs2)
+        nc.sync.dma_start(kept_list[:], offs)
+        nc.sync.dma_start(ekey_word_pool[:].bitcast(I32), ekey_words[0].rearrange("p n t -> p (n t)").bitcast(I32))
+        nc.sync.dma_start(keys_word_pool[:].bitcast(I32), keys_words[0].rearrange("p n t -> p (n t)").bitcast(I32))
+        for q in range(QUADS):
+            nc.scalar.dma_start(ekey_byte_pool[32 * q : 32 * q + 4, :].bitcast(I32), ekey_scales[0, 4 * q : 4 * q + 4, :].bitcast(I32))
+        for q in range(QUADS):
+            row = 32 * q + KEPT_ROW
+            nc.scalar.dma_start(keys_byte_pool[row : row + 4, :].bitcast(I32), keys_scales[0, 4 * q : 4 * q + 4, :].bitcast(I32))
+        fac_sb = sbuf("fac_sb", [P, PACK], F32)
+        nc.gpsimd.dma_start(fac_sb[:], fac.rearrange("(p t) o -> p (t o)", t=PACK))
+
+        evals_rows = evals.rearrange("(p t) c -> p t c", t=PACK)
+        vals_rows = vals.rearrange("(p t) c -> p t c", t=PACK)
+        identity = sbuf("identity", [P, P], F32)
+        make_identity(nc, identity[:])
+
+        ekey_bytes = held.tile([P, J], U8, name="ekey_bytes", tag="ekey_gathered", align_bytes=64)
+        ekey_scale = sbuf("ekey_scale", [P, J], U8)
+        keys_scale = sbuf("keys_scale", [P, I], U8)
+        keys_codes = sbuf("keys_codes", [P, I], U32)
+        nc.vector.tensor_copy(ekey_bytes[:], ekey_byte_pool[:].indirect(evicted_list[:]))
+        nc.vector.tensor_copy(ekey_scale[:].rearrange("p (t s) -> p t s", t=PACK), ekey_bytes[:].rearrange("p (s t) -> p t s", t=PACK))
+        ekey_codes = held.tile([P, J], U32, name="ekey_codes", tag="ekey_gathered", align_bytes=64)
+        nc.vector.tensor_copy(ekey_codes[:].rearrange("p (t s) -> p s t", t=PACK), ekey_word_pool[:].indirect(evicted_list[:]))
+        nc.vector.tensor_copy(keys_codes[:], keys_word_pool[:].indirect(kept_list[:]))
+        nc.vector.tensor_copy(keys_scale[:], keys_byte_pool[:].indirect(kept_list[:]))
+
+        evals_pool = []
+        for t in range(PACK):
+            evals_pool.append(window(F32))
+            nc.sync.dma_start(evals_pool[t][:], evals_rows[:, t, :])
+
+        neg_max = sbuf("neg_max", [P, PACK], F32)
+        row_sum = sbuf("row_sum", [P, PACK], F32)
+        inv_sum = sbuf("inv_sum", [P, PACK], F32)
+        factor = sbuf("factor", [P, PACK], F32)
+        prob = sbuf("prob", [P, PACK, I], F32)
+        w_rows = sbuf("w_rows", [P, PACK, I], BF16)
+        for t in range(PACK):
+            cols = slice(t * P, (t + 1) * P)
+            score = psum.tile([P, I], F32, name="score", tag="product")
+            nc.tensor.matmul_mx(score[:], lhsT=ekey_codes[:, cols].bitcast(FP8X4), lhsT_scale=ekey_scale[:, cols],
+                                rhs=keys_codes[:].bitcast(FP8X4), rhs_scale=keys_scale[KEPT_ROW:P, :], start=True, stop=True)
+            nc.vector.tensor_reduce(neg_max[:, t : t + 1], score[:], AXIS.X, ALU.max, negate=True)
+            nc.scalar.activation(prob[:, t, :], score[:], ACT.Exp, bias=neg_max[:, t : t + 1], accum_out=row_sum[:, t : t + 1])
+        for pair in (slice(0, 2), slice(2, 4)):
+            nc.vector.reciprocal(inv_sum[:, pair], row_sum[:, pair])
+            nc.vector.tensor_tensor(factor[:, pair], inv_sum[:, pair], fac_sb[:, pair], ALU.mult)
+        for t in range(PACK):
+            nc.scalar.activation(w_rows[:, t, :], prob[:, t, :], ACT.Copy, scale=factor[:, t : t + 1])
+        w_grouped = sbuf("w_grouped", [P, I, PACK], BF16)
+        nc.scalar.copy(w_grouped[:], w_rows[:].rearrange("p t i -> p i t"))
+        w_codes = sbuf("w_codes", [P, I], U32)
+        w_scale = sbuf("w_scale", [P, I], U8)
+        nc.vector.quantize_mx(w_codes[:].bitcast(FP8X4), w_scale[:], w_grouped[:].rearrange("p i t -> p (i t)"))
+
+        vt_codes = []
+        vt_scale = []
+        for t in range(PACK):
+            picked = sbuf("evals_picked%d" % t, [P, J], BF16)
+            nc.vector.tensor_copy(picked[:], evals_pool[t][:].indirect(evicted_list[:]))
+            pairs = picked[:].bitcast(F32)
+            turned = psum.tile([P, 2, P], F32, name="turned", tag="turned")
+            for u in range(2):
+                nc.tensor.transpose(turned[:, u, :], pairs[:, u : J // 2 : 2], identity[:])
+            vt_grouped = sbuf("vt_grouped%d" % t, [P, P * PACK], BF16)
+            nc.scalar.copy(vt_grouped[:].bitcast(F32).rearrange("p (e u) -> p e u", u=2), turned[:].rearrange("p u e -> p e u"))
+            vt_codes.append(sbuf("vt_codes%d" % t, [P, P], U32))
+            vt_scale.append(sbuf("vt_scale%d" % t, [P, P], U8))
+            nc.vector.quantize_mx(vt_codes[t][:].bitcast(FP8X4), vt_scale[t][:], vt_grouped[:])
+
+        vals_pool = []
+        for t in range(PACK):
+            vals_pool.append(window(F32))
+            nc.sync.dma_start(vals_pool[t][:], vals_rows[:, t, :])
+
+        merged = []
+        for t in range(PACK):
+            product = psum.tile([P, I], F32, name="merged", tag="product")
+            nc.tensor.matmul_mx(product[:], lhsT=vt_codes[t][:].bitcast(FP8X4), lhsT_scale=vt_scale[t][:],
+                                rhs=w_codes[:].bitcast(FP8X4), rhs_scale=w_scale[:], start=True, stop=True)
+            merged.append(product)
+
+        out_rows = out_0.rearrange("(p t) i -> p t i", t=PACK)
+        y_low = sbuf("y_low", [P, 2, I], F32)
+        y_high = sbuf("y_high", [P, 2, I], F32)
+        y_grouped = sbuf("y_grouped", [P, I, PACK], BF16)
+        y_codes = sbuf("y_codes", [P, I], U32)
+        y_scale = sbuf("y_scale", [P, I], U8)
+        for t in range(PACK - 1):
+            kept = sbuf("kept%d" % t, [P, I], F32)
+            y_t = (y_low, y_high)[t // 2][:, t % 2, :]
+            nc.vector.tensor_copy(kept[:], vals_pool[t][:].indirect(kept_list[:]))
+            nc.vector.tensor_tensor(y_t, merged[t][:], kept[:], ALU.add)
+            nc.sync.dma_start(out_rows[:, t, :], y_t)
+            if t == 1:
+                nc.scalar.copy(y_grouped[:, :, 0:2], y_low[:].rearrange("p t i -> p i t"))
+        last = PACK - 1
+        kept = sbuf("kept_last", [P, I], F32)
+        words_out = out_1[0].rearrange("p n t -> p (n t)").bitcast(I32)
+        halves = (slice(0, HALF), slice(HALF, I))
+        for h, cols in enumerate(halves):
+            nc.vector.tensor_copy(kept[:, cols], vals_pool[last][:].indirect(kept_list[:, h * HALF // 16 : (h + 1) * HALF // 16]))
+        for h, cols in enumerate(halves):
+            nc.vector.tensor_tensor(y_high[:, 1, cols], merged[last][:, cols], kept[:, cols], ALU.add)
+        nc.scalar.copy(y_grouped[:, halves[0], 2:4], y_high[:, :, halves[0]].rearrange("p t i -> p i t"))
+        nc.vector.tensor_copy(y_grouped[:, halves[1], 2:4], y_high[:, :, halves[1]].rearrange("p t i -> p i t"))
+        nc.sync.dma_start(out_rows[:, last, :], y_high[:, 1, :])
+        for cols in halves:
+            nc.vector.quantize_mx(y_codes[:, cols].bitcast(FP8X4), y_scale[:, cols], y_grouped[:, cols, :].rearrange("p i t -> p (i t)"))
+            nc.sync.dma_start(words_out[:, cols], y_codes[:, cols].bitcast(I32))
+        for q in range(QUADS):
+            queue = (nc.sync, nc.scalar)[q % 2]
+            queue.dma_start(out_2[0, 4 * q : 4 * q + 4, :].bitcast(I32), y_scale[32 * q : 32 * q + 4, :].bitcast(I32))

@@ -22,28 +22,29 @@ PACK = 4
 QUADS = 4
 HALF = I // 2
 KEPT_ROW = 4
+LANE_KIB = 11
 
 
 def tile_attend_softmerge_pl_kernel(tc, ekey_words, ekey_scales, keys_words, keys_scales, fac, evals, vals, offs, offs2, out_0, out_1, out_2):
     nc = tc.nc
     with ExitStack() as ctx:
         held = ctx.enter_context(tc.tile_pool(name="held", bufs=1))
-        ring = ctx.enter_context(tc.tile_pool(name="ring", bufs=4))
+        shared = ctx.enter_context(tc.tile_pool(name="shared", bufs=1))
         psum = ctx.enter_context(tc.psum_pool(name="psum", bufs=4))
 
         def sbuf(name, shape, dtype):
             return held.tile(shape, dtype, name=name, align_bytes=64)
 
-        def window(dtype):
-            return ring.tile([P, T], dtype, name="window", align_bytes=64)
+        def placed(name, shape, dtype, lane, kib):
+            return shared.tile(shape, dtype, name=name, align_bytes=64, offset=(lane * LANE_KIB + kib) * 1024)
 
         kept_list = held.tile([P, I // 16], U16, name="kept_list")
         evicted_list = held.tile([P, J // 16], U16, name="evicted_list")
 
-        ekey_byte_pool = window(U8)
-        ekey_word_pool = window(U32)
-        keys_word_pool = window(U32)
-        keys_byte_pool = window(U8)
+        ekey_byte_pool = placed("ekey_byte_pool", [P, T], U8, 1, 0)
+        ekey_word_pool = placed("ekey_word_pool", [P, T], U32, 0, 0)
+        keys_word_pool = placed("keys_word_pool", [P, T], U32, 2, 0)
+        keys_byte_pool = placed("keys_byte_pool", [P, T], U8, 3, 0)
         nc.vector.memset(ekey_byte_pool[:].bitcast(I32), 0)
         nc.vector.memset(keys_byte_pool[:].bitcast(I32), 0)
 
@@ -55,8 +56,8 @@ def tile_attend_softmerge_pl_kernel(tc, ekey_words, ekey_scales, keys_words, key
             nc.scalar.dma_start(ekey_byte_pool[32 * q : 32 * q + 4, :].bitcast(I32), ekey_scales[0, 4 * q : 4 * q + 4, :].bitcast(I32))
         for q in range(QUADS):
             row = 32 * q + KEPT_ROW
-            nc.scalar.dma_start(keys_byte_pool[row : row + 4, :].bitcast(I32), keys_scales[0, 4 * q : 4 * q + 4, :].bitcast(I32))
-        fac_sb = sbuf("fac_sb", [P, PACK], F32)
+            (nc.scalar, nc.gpsimd)[q // 2].dma_start(keys_byte_pool[row : row + 4, :].bitcast(I32), keys_scales[0, 4 * q : 4 * q + 4, :].bitcast(I32))
+        fac_sb = placed("fac_sb", [P, PACK], F32, 4, 2)
         nc.gpsimd.dma_start(fac_sb[:], fac.rearrange("(p t) o -> p (t o)", t=PACK))
 
         evals_rows = evals.rearrange("(p t) c -> p t c", t=PACK)
@@ -64,25 +65,24 @@ def tile_attend_softmerge_pl_kernel(tc, ekey_words, ekey_scales, keys_words, key
         identity = sbuf("identity", [P, P], F32)
         make_identity(nc, identity[:])
 
-        ekey_bytes = held.tile([P, J], U8, name="ekey_bytes", tag="ekey_gathered", align_bytes=64)
+        ekey_bytes = placed("ekey_bytes", [P, J], U8, 0, 0)
+        ekey_codes = sbuf("ekey_codes", [P, J], U32)
         ekey_scale = sbuf("ekey_scale", [P, J], U8)
-        keys_scale = sbuf("keys_scale", [P, I], U8)
-        keys_codes = sbuf("keys_codes", [P, I], U32)
-        nc.vector.tensor_copy(ekey_bytes[:], ekey_byte_pool[:].indirect(evicted_list[:]))
-        nc.vector.tensor_copy(ekey_scale[:].rearrange("p (t s) -> p t s", t=PACK), ekey_bytes[:].rearrange("p (s t) -> p t s", t=PACK))
-        ekey_codes = held.tile([P, J], U32, name="ekey_codes", tag="ekey_gathered", align_bytes=64)
+        keys_scale = placed("keys_scale", [P, I], U8, 2, 0)
+        keys_codes = placed("keys_codes", [P, I], U32, 0, 1)
         nc.vector.tensor_copy(ekey_codes[:].rearrange("p (t s) -> p s t", t=PACK), ekey_word_pool[:].indirect(evicted_list[:]))
+        nc.vector.tensor_copy(ekey_bytes[:], ekey_byte_pool[:].indirect(evicted_list[:]))
         nc.vector.tensor_copy(keys_codes[:], keys_word_pool[:].indirect(kept_list[:]))
+        nc.vector.tensor_copy(ekey_scale[:].rearrange("p (t s) -> p t s", t=PACK), ekey_bytes[:].rearrange("p (s t) -> p t s", t=PACK))
         nc.vector.tensor_copy(keys_scale[:], keys_byte_pool[:].indirect(kept_list[:]))
 
         evals_pool = []
         for t in range(PACK):
-            evals_pool.append(window(F32))
+            evals_pool.append(placed("evals_pool%d" % t, [P, T], F32, t, (3, 0, 1, 0)[t]))
             nc.sync.dma_start(evals_pool[t][:], evals_rows[:, t, :])
 
         neg_max = sbuf("neg_max", [P, PACK], F32)
         row_sum = sbuf("row_sum", [P, PACK], F32)
-        inv_sum = sbuf("inv_sum", [P, PACK], F32)
         factor = sbuf("factor", [P, PACK], F32)
         prob = sbuf("prob", [P, PACK, I], F32)
         w_rows = sbuf("w_rows", [P, PACK, I], BF16)
@@ -93,9 +93,11 @@ def tile_attend_softmerge_pl_kernel(tc, ekey_words, ekey_scales, keys_words, key
                                 rhs=keys_codes[:].bitcast(FP8X4), rhs_scale=keys_scale[KEPT_ROW:P, :], start=True, stop=True)
             nc.vector.tensor_reduce(neg_max[:, t : t + 1], score[:], AXIS.X, ALU.max, negate=True)
             nc.scalar.activation(prob[:, t, :], score[:], ACT.Exp, bias=neg_max[:, t : t + 1], accum_out=row_sum[:, t : t + 1])
-        for pair in (slice(0, 2), slice(2, 4)):
-            nc.vector.reciprocal(inv_sum[:, pair], row_sum[:, pair])
-            nc.vector.tensor_tensor(factor[:, pair], inv_sum[:, pair], fac_sb[:, pair], ALU.mult)
+        for h in range(2):
+            pair = slice(2 * h, 2 * h + 2)
+            inv_sum = placed("inv_sum%d" % h, [P, 2], F32, 4, h)
+            nc.vector.reciprocal(inv_sum[:], row_sum[:, pair])
+            nc.vector.tensor_tensor(factor[:, pair], inv_sum[:], fac_sb[:, pair], ALU.mult)
         for t in range(PACK):
             nc.scalar.activation(w_rows[:, t, :], prob[:, t, :], ACT.Copy, scale=factor[:, t : t + 1])
         w_grouped = sbuf("w_grouped", [P, I, PACK], BF16)
@@ -107,7 +109,7 @@ def tile_attend_softmerge_pl_kernel(tc, ekey_words, ekey_scales, keys_words, key
         vt_codes = []
         vt_scale = []
         for t in range(PACK):
-            picked = sbuf("evals_picked%d" % t, [P, J], BF16)
+            picked = placed("evals_picked%d" % t, [P, J], BF16, *((4, 0), (4, 1), (4, 2), (1, 0))[t])
             nc.vector.tensor_copy(picked[:], evals_pool[t][:].indirect(evicted_list[:]))
             pairs = picked[:].bitcast(F32)
             turned = psum.tile([P, 2, P], F32, name="turned", tag="turned")
@@ -121,7 +123,7 @@ def tile_attend_softmerge_pl_kernel(tc, ekey_words, ekey_scales, keys_words, key
 
         vals_pool = []
         for t in range(PACK):
-            vals_pool.append(window(F32))
+            vals_pool.append(placed("vals_pool%d" % t, [P, T], F32, t, (3, 1, 3, 0)[t]))
             nc.sync.dma_start(vals_pool[t][:], vals_rows[:, t, :])
 
         merged = []
@@ -137,22 +139,25 @@ def tile_attend_softmerge_pl_kernel(tc, ekey_words, ekey_scales, keys_words, key
         y_grouped = sbuf("y_grouped", [P, I, PACK], BF16)
         y_codes = sbuf("y_codes", [P, I], U32)
         y_scale = sbuf("y_scale", [P, I], U8)
-        for t in range(PACK - 1):
-            kept = sbuf("kept%d" % t, [P, I], F32)
+        kept = placed("kept", [P, I], F32, 2, 1)
+        nc.vector.tensor_copy(kept[:], vals_pool[0][:].indirect(kept_list[:]))
+        nc.vector.tensor_tensor(y_low[:, 0, :], merged[0][:], kept[:], ALU.add)
+        nc.sync.dma_start(out_rows[:, 0, :], y_low[:, 0, :])
+        merged_sb = sbuf("merged_sb", [P, PACK - 1, I], F32)
+        for t in range(1, PACK):
+            nc.scalar.copy(merged_sb[:, t - 1, :], merged[t][:])
+        for t in (1, 2):
             y_t = (y_low, y_high)[t // 2][:, t % 2, :]
-            nc.vector.tensor_copy(kept[:], vals_pool[t][:].indirect(kept_list[:]))
-            nc.vector.tensor_tensor(y_t, merged[t][:], kept[:], ALU.add)
+            nc.vector.tensor_tensor(y_t, vals_pool[t][:].indirect(kept_list[:]), merged_sb[:, t - 1, :], ALU.add)
             nc.sync.dma_start(out_rows[:, t, :], y_t)
             if t == 1:
                 nc.scalar.copy(y_grouped[:, :, 0:2], y_low[:].rearrange("p t i -> p i t"))
         last = PACK - 1
-        kept = sbuf("kept_last", [P, I], F32)
         words_out = out_1[0].rearrange("p n t -> p (n t)").bitcast(I32)
         halves = (slice(0, HALF), slice(HALF, I))
         for h, cols in enumerate(halves):
-            nc.vector.tensor_copy(kept[:, cols], vals_pool[last][:].indirect(kept_list[:, h * HALF // 16 : (h + 1) * HALF // 16]))
-        for h, cols in enumerate(halves):
-            nc.vector.tensor_tensor(y_high[:, 1, cols], merged[last][:, cols], kept[:, cols], ALU.add)
+            nc.vector.tensor_tensor(y_high[:, 1, cols], vals_pool[last][:].indirect(kept_list[:, h * HALF // 16 : (h + 1) * HALF // 16]),
+                                    merged_sb[:, last - 1, cols], ALU.add)
         nc.scalar.copy(y_grouped[:, halves[0], 2:4], y_high[:, :, halves[0]].rearrange("p t i -> p i t"))
         nc.vector.tensor_copy(y_grouped[:, halves[1], 2:4], y_high[:, :, halves[1]].rearrange("p t i -> p i t"))
         nc.sync.dma_start(out_rows[:, last, :], y_high[:, 1, :])

@@ -45,8 +45,8 @@ def tile_attend_softmerge_pl_kernel(tc, ekey_words, ekey_scales, keys_words, key
         ekey_word_pool = placed("ekey_word_pool", [P, T], U32, 0, 0)
         keys_word_pool = placed("keys_word_pool", [P, T], U32, 2, 0)
         keys_byte_pool = placed("keys_byte_pool", [P, T], U8, 3, 0)
-        nc.vector.memset(ekey_byte_pool[:].bitcast(I32), 0)
         nc.vector.memset(keys_byte_pool[:].bitcast(I32), 0)
+        nc.vector.memset(ekey_byte_pool[:].bitcast(I32), 0)
 
         nc.sync.dma_start(evicted_list[:], offs2)
         nc.sync.dma_start(kept_list[:], offs)
@@ -56,7 +56,7 @@ def tile_attend_softmerge_pl_kernel(tc, ekey_words, ekey_scales, keys_words, key
             nc.scalar.dma_start(ekey_byte_pool[32 * q : 32 * q + 4, :].bitcast(I32), ekey_scales[0, 4 * q : 4 * q + 4, :].bitcast(I32))
         for q in range(QUADS):
             row = 32 * q + KEPT_ROW
-            (nc.scalar, nc.gpsimd)[q // 2].dma_start(keys_byte_pool[row : row + 4, :].bitcast(I32), keys_scales[0, 4 * q : 4 * q + 4, :].bitcast(I32))
+            (nc.gpsimd if q else nc.scalar).dma_start(keys_byte_pool[row : row + 4, :].bitcast(I32), keys_scales[0, 4 * q : 4 * q + 4, :].bitcast(I32))
         fac_sb = placed("fac_sb", [P, PACK], F32, 4, 2)
         nc.gpsimd.dma_start(fac_sb[:], fac.rearrange("(p t) o -> p (t o)", t=PACK))
 
@@ -78,12 +78,12 @@ def tile_attend_softmerge_pl_kernel(tc, ekey_words, ekey_scales, keys_words, key
 
         evals_pool = []
         for t in range(PACK):
-            evals_pool.append(placed("evals_pool%d" % t, [P, T], F32, t, (3, 0, 1, 0)[t]))
+            evals_pool.append(placed("evals_pool%d" % t, [P, T], F32, *((5, 0), (0, 3), (1, 0), (2, 1))[t]))
             nc.sync.dma_start(evals_pool[t][:], evals_rows[:, t, :])
 
         neg_max = sbuf("neg_max", [P, PACK], F32)
         row_sum = sbuf("row_sum", [P, PACK], F32)
-        factor = sbuf("factor", [P, PACK], F32)
+        factor = sbuf("factor", [P, 2], F32)
         prob = sbuf("prob", [P, PACK, I], F32)
         w_rows = sbuf("w_rows", [P, PACK, I], BF16)
         for t in range(PACK):
@@ -93,13 +93,15 @@ def tile_attend_softmerge_pl_kernel(tc, ekey_words, ekey_scales, keys_words, key
                                 rhs=keys_codes[:].bitcast(FP8X4), rhs_scale=keys_scale[KEPT_ROW:P, :], start=True, stop=True)
             nc.vector.tensor_reduce(neg_max[:, t : t + 1], score[:], AXIS.X, ALU.max, negate=True)
             nc.scalar.activation(prob[:, t, :], score[:], ACT.Exp, bias=neg_max[:, t : t + 1], accum_out=row_sum[:, t : t + 1])
-        for h in range(2):
-            pair = slice(2 * h, 2 * h + 2)
-            inv_sum = placed("inv_sum%d" % h, [P, 2], F32, 4, h)
-            nc.vector.reciprocal(inv_sum[:], row_sum[:, pair])
-            nc.vector.tensor_tensor(factor[:, pair], inv_sum[:], fac_sb[:, pair], ALU.mult)
-        for t in range(PACK):
+        inv_low = placed("inv_low", [P, 2], F32, 4, 0)
+        nc.vector.reciprocal(inv_low[:], row_sum[:, 0:2])
+        nc.vector.tensor_tensor(factor[:], inv_low[:], fac_sb[:, 0:2], ALU.mult)
+        inv_high = placed("inv_high", [P, 2], F32, 4, 1)
+        nc.vector.reciprocal(inv_high[:], row_sum[:, 2:4])
+        for t in (0, 1):
             nc.scalar.activation(w_rows[:, t, :], prob[:, t, :], ACT.Copy, scale=factor[:, t : t + 1])
+        for t in (2, 3):
+            nc.vector.tensor_scalar(w_rows[:, t, :], prob[:, t, :], inv_high[:, t - 2 : t - 1], fac_sb[:, t : t + 1], ALU.mult, ALU.mult)
         w_grouped = sbuf("w_grouped", [P, I, PACK], BF16)
         nc.scalar.copy(w_grouped[:], w_rows[:].rearrange("p t i -> p i t"))
         w_codes = sbuf("w_codes", [P, I], U32)
@@ -109,7 +111,7 @@ def tile_attend_softmerge_pl_kernel(tc, ekey_words, ekey_scales, keys_words, key
         vt_codes = []
         vt_scale = []
         for t in range(PACK):
-            picked = placed("evals_picked%d" % t, [P, J], BF16, *((4, 0), (4, 1), (4, 2), (1, 0))[t])
+            picked = placed("evals_picked%d" % t, [P, J], BF16, *((3, 0), (4, 0), (4, 1), (4, 2))[t])
             nc.vector.tensor_copy(picked[:], evals_pool[t][:].indirect(evicted_list[:]))
             pairs = picked[:].bitcast(F32)
             turned = psum.tile([P, 2, P], F32, name="turned", tag="turned")
@@ -123,7 +125,7 @@ def tile_attend_softmerge_pl_kernel(tc, ekey_words, ekey_scales, keys_words, key
 
         vals_pool = []
         for t in range(PACK):
-            vals_pool.append(placed("vals_pool%d" % t, [P, T], F32, t, (3, 1, 3, 0)[t]))
+            vals_pool.append(placed("vals_pool%d" % t, [P, T], F32, *((3, 1), (5, 0), (0, 3), (1, 0))[t]))
             nc.sync.dma_start(vals_pool[t][:], vals_rows[:, t, :])
 
         merged = []
@@ -139,16 +141,12 @@ def tile_attend_softmerge_pl_kernel(tc, ekey_words, ekey_scales, keys_words, key
         y_grouped = sbuf("y_grouped", [P, I, PACK], BF16)
         y_codes = sbuf("y_codes", [P, I], U32)
         y_scale = sbuf("y_scale", [P, I], U8)
-        kept = placed("kept", [P, I], F32, 2, 1)
-        nc.vector.tensor_copy(kept[:], vals_pool[0][:].indirect(kept_list[:]))
-        nc.vector.tensor_tensor(y_low[:, 0, :], merged[0][:], kept[:], ALU.add)
-        nc.sync.dma_start(out_rows[:, 0, :], y_low[:, 0, :])
-        merged_sb = sbuf("merged_sb", [P, PACK - 1, I], F32)
-        for t in range(1, PACK):
-            nc.scalar.copy(merged_sb[:, t - 1, :], merged[t][:])
-        for t in (1, 2):
+        merged_sb = sbuf("merged_sb", [P, PACK, I], F32)
+        for t in range(PACK):
+            nc.scalar.copy(merged_sb[:, t, :], merged[t][:])
+        for t in range(PACK - 1):
             y_t = (y_low, y_high)[t // 2][:, t % 2, :]
-            nc.vector.tensor_tensor(y_t, vals_pool[t][:].indirect(kept_list[:]), merged_sb[:, t - 1, :], ALU.add)
+            nc.vector.tensor_tensor(y_t, vals_pool[t][:].indirect(kept_list[:]), merged_sb[:, t, :], ALU.add)
             nc.sync.dma_start(out_rows[:, t, :], y_t)
             if t == 1:
                 nc.scalar.copy(y_grouped[:, :, 0:2], y_low[:].rearrange("p t i -> p i t"))
@@ -157,7 +155,7 @@ def tile_attend_softmerge_pl_kernel(tc, ekey_words, ekey_scales, keys_words, key
         halves = (slice(0, HALF), slice(HALF, I))
         for h, cols in enumerate(halves):
             nc.vector.tensor_tensor(y_high[:, 1, cols], vals_pool[last][:].indirect(kept_list[:, h * HALF // 16 : (h + 1) * HALF // 16]),
-                                    merged_sb[:, last - 1, cols], ALU.add)
+                                    merged_sb[:, last, cols], ALU.add)
         nc.scalar.copy(y_grouped[:, halves[0], 2:4], y_high[:, :, halves[0]].rearrange("p t i -> p i t"))
         nc.vector.tensor_copy(y_grouped[:, halves[1], 2:4], y_high[:, :, halves[1]].rearrange("p t i -> p i t"))
         nc.sync.dma_start(out_rows[:, last, :], y_high[:, 1, :])

@@ -22,7 +22,7 @@ PACK = 4
 QUADS = 4
 HALF = I // 2
 KEPT_ROW = 4
-LANE_KIB = 11
+LANE_KIB = 22
 
 
 def tile_attend_softmerge_pl_kernel(tc, ekey_words, ekey_scales, keys_words, keys_scales, fac, evals, vals, offs, offs2, out_0, out_1, out_2):
@@ -43,43 +43,80 @@ def tile_attend_softmerge_pl_kernel(tc, ekey_words, ekey_scales, keys_words, key
 
         ekey_byte_pool = placed("ekey_byte_pool", [P, T], U8, 1, 0)
         ekey_word_pool = placed("ekey_word_pool", [P, T], U32, 0, 0)
-        keys_word_pool = placed("keys_word_pool", [P, T], U32, 2, 0)
+        keys_word_pool = placed("keys_word_pool", [P, T], U32, 2, 7)
         keys_byte_pool = placed("keys_byte_pool", [P, T], U8, 3, 0)
-        nc.vector.memset(keys_byte_pool[:].bitcast(I32), 0)
         nc.vector.memset(ekey_byte_pool[:].bitcast(I32), 0)
+        nc.vector.memset(keys_byte_pool[:].bitcast(I32), 0)
 
         nc.sync.dma_start(evicted_list[:], offs2)
         nc.sync.dma_start(kept_list[:], offs)
         nc.sync.dma_start(ekey_word_pool[:].bitcast(I32), ekey_words[0].rearrange("p n t -> p (n t)").bitcast(I32))
-        nc.sync.dma_start(keys_word_pool[:].bitcast(I32), keys_words[0].rearrange("p n t -> p (n t)").bitcast(I32))
         for q in range(QUADS):
             nc.scalar.dma_start(ekey_byte_pool[32 * q : 32 * q + 4, :].bitcast(I32), ekey_scales[0, 4 * q : 4 * q + 4, :].bitcast(I32))
+        evals_rows = evals.rearrange("(p t) c -> p t c", t=PACK)
+        evals_pool = [sbuf("evals_pool0", [P, T], F32)]
+        nc.sync.dma_start(evals_pool[0][:], evals_rows[:, 0, :])
+        nc.sync.dma_start(keys_word_pool[:].bitcast(I32), keys_words[0].rearrange("p n t -> p (n t)").bitcast(I32))
         for q in range(QUADS):
             row = 32 * q + KEPT_ROW
-            (nc.gpsimd if q else nc.scalar).dma_start(keys_byte_pool[row : row + 4, :].bitcast(I32), keys_scales[0, 4 * q : 4 * q + 4, :].bitcast(I32))
-        fac_sb = placed("fac_sb", [P, PACK], F32, 4, 2)
-        nc.gpsimd.dma_start(fac_sb[:], fac.rearrange("(p t) o -> p (t o)", t=PACK))
+            (nc.scalar, nc.gpsimd)[q // 2].dma_start(keys_byte_pool[row : row + 4, :].bitcast(I32), keys_scales[0, 4 * q : 4 * q + 4, :].bitcast(I32))
 
-        evals_rows = evals.rearrange("(p t) c -> p t c", t=PACK)
-        vals_rows = vals.rearrange("(p t) c -> p t c", t=PACK)
+        fac_sb = placed("fac_sb", [P, PACK], F32, 4, 1)
+        nc.gpsimd.dma_start(fac_sb[:], fac.rearrange("(p t) o -> p (t o)", t=PACK))
         identity = sbuf("identity", [P, P], F32)
         make_identity(nc, identity[:])
+
+        vals_rows = vals.rearrange("(p t) c -> p t c", t=PACK)
 
         ekey_bytes = placed("ekey_bytes", [P, J], U8, 0, 0)
         ekey_codes = sbuf("ekey_codes", [P, J], U32)
         ekey_scale = sbuf("ekey_scale", [P, J], U8)
-        keys_scale = placed("keys_scale", [P, I], U8, 2, 0)
-        keys_codes = placed("keys_codes", [P, I], U32, 0, 1)
+        keys_scale = sbuf("keys_scale", [P, I], U8)
+        keys_codes = placed("keys_codes", [P, I], U32, 3, 0)
         nc.vector.tensor_copy(ekey_codes[:].rearrange("p (t s) -> p s t", t=PACK), ekey_word_pool[:].indirect(evicted_list[:]))
         nc.vector.tensor_copy(ekey_bytes[:], ekey_byte_pool[:].indirect(evicted_list[:]))
-        nc.vector.tensor_copy(keys_codes[:], keys_word_pool[:].indirect(kept_list[:]))
         nc.vector.tensor_copy(ekey_scale[:].rearrange("p (t s) -> p t s", t=PACK), ekey_bytes[:].rearrange("p (s t) -> p t s", t=PACK))
         nc.vector.tensor_copy(keys_scale[:], keys_byte_pool[:].indirect(kept_list[:]))
+        nc.vector.tensor_copy(keys_codes[:], keys_word_pool[:].indirect(kept_list[:]))
 
-        evals_pool = []
-        for t in range(PACK):
-            evals_pool.append(placed("evals_pool%d" % t, [P, T], F32, *((5, 0), (0, 3), (1, 0), (2, 1))[t]))
+
+        for t in range(1, PACK):
+            evals_pool.append(placed("evals_pool%d" % t, [P, T], F32, *((0, 3), (1, 0), (2, 0))[t - 1]))
             nc.sync.dma_start(evals_pool[t][:], evals_rows[:, t, :])
+
+        vals_pool = []
+        turned = []
+        vt_grouped = []
+        vt_codes = [sbuf("vt_codes%d" % t, [P, P], U32) for t in range(PACK)]
+        vt_scale = [sbuf("vt_scale%d" % t, [P, P], U8) for t in range(PACK)]
+
+        def load_vals(t):
+            vals_pool.append(placed("vals_pool%d" % t, [P, T], F32, *((2, 14), (3, 0), (0, 4), (1, 0))[t]))
+            nc.sync.dma_start(vals_pool[t][:], vals_rows[:, t, :])
+
+        def gather_and_turn(t):
+            picked = placed("evals_picked%d" % t, [P, J], BF16, *((4, 0), (0, 3), (4, 1))[t - 1])
+            nc.vector.tensor_copy(picked[:], evals_pool[t][:].indirect(evicted_list[:]))
+            turn(t, picked, "turned")
+
+        def turn(t, picked, banks):
+            pairs = picked[:].bitcast(F32)
+            turned.append(psum.tile([P, 2, P], F32, name="turned", tag=banks))
+            for u in range(2):
+                nc.tensor.transpose(turned[t][:, u, :], pairs[:, u : J // 2 : 2], identity[:])
+
+        def group_vt(t):
+            vt_grouped.append(sbuf("vt_grouped%d" % t, [P, P * PACK], BF16))
+            nc.scalar.copy(vt_grouped[t][:].bitcast(F32).rearrange("p (e u) -> p e u", u=2), turned[t][:].rearrange("p u e -> p e u"))
+
+        def quantise_vt(t):
+            nc.vector.quantize_mx(vt_codes[t][:].bitcast(FP8X4), vt_scale[t][:], vt_grouped[t][:])
+
+        load_vals(0)
+        evals_rounded = sbuf("evals_rounded", [P, T], BF16)
+        picked_first = sbuf("evals_picked0", [P, J], BF16)
+        nc.scalar.activation(evals_rounded[:], evals_pool[0][:], ACT.Copy)
+        nc.scalar.activation(picked_first[:], evals_rounded[:].indirect(evicted_list[:]), ACT.Copy)
 
         neg_max = sbuf("neg_max", [P, PACK], F32)
         row_sum = sbuf("row_sum", [P, PACK], F32)
@@ -93,60 +130,54 @@ def tile_attend_softmerge_pl_kernel(tc, ekey_words, ekey_scales, keys_words, key
                                 rhs=keys_codes[:].bitcast(FP8X4), rhs_scale=keys_scale[KEPT_ROW:P, :], start=True, stop=True)
             nc.vector.tensor_reduce(neg_max[:, t : t + 1], score[:], AXIS.X, ALU.max, negate=True)
             nc.scalar.activation(prob[:, t, :], score[:], ACT.Exp, bias=neg_max[:, t : t + 1], accum_out=row_sum[:, t : t + 1])
+        turn(0, picked_first, "product")
+        load_vals(1)
         inv_low = placed("inv_low", [P, 2], F32, 4, 0)
         nc.vector.reciprocal(inv_low[:], row_sum[:, 0:2])
         nc.vector.tensor_tensor(factor[:], inv_low[:], fac_sb[:, 0:2], ALU.mult)
-        inv_high = placed("inv_high", [P, 2], F32, 4, 1)
-        nc.vector.reciprocal(inv_high[:], row_sum[:, 2:4])
         for t in (0, 1):
             nc.scalar.activation(w_rows[:, t, :], prob[:, t, :], ACT.Copy, scale=factor[:, t : t + 1])
+        gather_and_turn(1)
+        load_vals(2)
+        inv_high = placed("inv_high", [P, 2], F32, 0, 3)
+        nc.vector.reciprocal(inv_high[:], row_sum[:, 2:4])
         for t in (2, 3):
             nc.vector.tensor_scalar(w_rows[:, t, :], prob[:, t, :], inv_high[:, t - 2 : t - 1], fac_sb[:, t : t + 1], ALU.mult, ALU.mult)
-        w_grouped = sbuf("w_grouped", [P, I, PACK], BF16)
+        w_grouped = placed("w_grouped", [P, I, PACK], BF16, 4, 2)
         nc.scalar.copy(w_grouped[:], w_rows[:].rearrange("p t i -> p i t"))
-        w_codes = sbuf("w_codes", [P, I], U32)
+
+        gather_and_turn(2)
+        load_vals(3)
+        gather_and_turn(3)
+        for t in range(PACK):
+            group_vt(t)
+        w_codes = placed("w_codes", [P, I], U32, 2, 0)
         w_scale = sbuf("w_scale", [P, I], U8)
         nc.vector.quantize_mx(w_codes[:].bitcast(FP8X4), w_scale[:], w_grouped[:].rearrange("p i t -> p (i t)"))
 
-        vt_codes = []
-        vt_scale = []
-        for t in range(PACK):
-            picked = placed("evals_picked%d" % t, [P, J], BF16, *((3, 0), (4, 0), (4, 1), (4, 2))[t])
-            nc.vector.tensor_copy(picked[:], evals_pool[t][:].indirect(evicted_list[:]))
-            pairs = picked[:].bitcast(F32)
-            turned = psum.tile([P, 2, P], F32, name="turned", tag="turned")
-            for u in range(2):
-                nc.tensor.transpose(turned[:, u, :], pairs[:, u : J // 2 : 2], identity[:])
-            vt_grouped = sbuf("vt_grouped%d" % t, [P, P * PACK], BF16)
-            nc.scalar.copy(vt_grouped[:].bitcast(F32).rearrange("p (e u) -> p e u", u=2), turned[:].rearrange("p u e -> p e u"))
-            vt_codes.append(sbuf("vt_codes%d" % t, [P, P], U32))
-            vt_scale.append(sbuf("vt_scale%d" % t, [P, P], U8))
-            nc.vector.quantize_mx(vt_codes[t][:].bitcast(FP8X4), vt_scale[t][:], vt_grouped[:])
-
-        vals_pool = []
-        for t in range(PACK):
-            vals_pool.append(placed("vals_pool%d" % t, [P, T], F32, *((3, 1), (5, 0), (0, 3), (1, 0))[t]))
-            nc.sync.dma_start(vals_pool[t][:], vals_rows[:, t, :])
-
         merged = []
         for t in range(PACK):
-            product = psum.tile([P, I], F32, name="merged", tag="product")
-            nc.tensor.matmul_mx(product[:], lhsT=vt_codes[t][:].bitcast(FP8X4), lhsT_scale=vt_scale[t][:],
+            quantise_vt(t)
+            merged.append(psum.tile([P, I], F32, name="merged", tag="product"))
+            nc.tensor.matmul_mx(merged[t][:], lhsT=vt_codes[t][:].bitcast(FP8X4), lhsT_scale=vt_scale[t][:],
                                 rhs=w_codes[:].bitcast(FP8X4), rhs_scale=w_scale[:], start=True, stop=True)
-            merged.append(product)
 
+        kept = placed("kept", [P, I], F32, 4, 2)
+        nc.vector.tensor_copy(kept[:], vals_pool[0][:].indirect(kept_list[:]))
         out_rows = out_0.rearrange("(p t) i -> p t i", t=PACK)
         y_low = sbuf("y_low", [P, 2, I], F32)
         y_high = sbuf("y_high", [P, 2, I], F32)
         y_grouped = sbuf("y_grouped", [P, I, PACK], BF16)
         y_codes = sbuf("y_codes", [P, I], U32)
         y_scale = sbuf("y_scale", [P, I], U8)
-        merged_sb = sbuf("merged_sb", [P, PACK, I], F32)
-        for t in range(PACK):
-            nc.scalar.copy(merged_sb[:, t, :], merged[t][:])
-        for t in range(PACK - 1):
+        nc.vector.tensor_tensor(y_low[:, 0, :], merged[0][:], kept[:], ALU.add)
+        nc.sync.dma_start(out_rows[:, 0, :], y_low[:, 0, :])
+        merged_sb = sbuf("merged_sb", [P, PACK - 1, I], F32)
+        for t in range(1, PACK):
+            nc.scalar.copy(merged_sb[:, t - 1, :], merged[t][:])
+        for t in (1, 2):
             y_t = (y_low, y_high)[t // 2][:, t % 2, :]
-            nc.vector.tensor_tensor(y_t, vals_pool[t][:].indirect(kept_list[:]), merged_sb[:, t, :], ALU.add)
+            nc.vector.tensor_tensor(y_t, vals_pool[t][:].indirect(kept_list[:]), merged_sb[:, t - 1, :], ALU.add)
             nc.sync.dma_start(out_rows[:, t, :], y_t)
             if t == 1:
                 nc.scalar.copy(y_grouped[:, :, 0:2], y_low[:].rearrange("p t i -> p i t"))
@@ -155,7 +186,7 @@ def tile_attend_softmerge_pl_kernel(tc, ekey_words, ekey_scales, keys_words, key
         halves = (slice(0, HALF), slice(HALF, I))
         for h, cols in enumerate(halves):
             nc.vector.tensor_tensor(y_high[:, 1, cols], vals_pool[last][:].indirect(kept_list[:, h * HALF // 16 : (h + 1) * HALF // 16]),
-                                    merged_sb[:, last, cols], ALU.add)
+                                    merged_sb[:, last - 1, cols], ALU.add)
         nc.scalar.copy(y_grouped[:, halves[0], 2:4], y_high[:, :, halves[0]].rearrange("p t i -> p i t"))
         nc.vector.tensor_copy(y_grouped[:, halves[1], 2:4], y_high[:, :, halves[1]].rearrange("p t i -> p i t"))
         nc.sync.dma_start(out_rows[:, last, :], y_high[:, 1, :])

@@ -45,8 +45,8 @@ def tile_attend_softmerge_pl_kernel(tc, ekey_words, ekey_scales, keys_words, key
         ekey_word_pool = placed("ekey_word_pool", [P, T], U32, 0, 0)
         keys_word_pool = placed("keys_word_pool", [P, T], U32, 2, 7)
         keys_byte_pool = placed("keys_byte_pool", [P, T], U8, 3, 0)
-        nc.vector.memset(ekey_byte_pool[:].bitcast(I32), 0)
         nc.vector.memset(keys_byte_pool[:].bitcast(I32), 0)
+        nc.vector.memset(ekey_byte_pool[:].bitcast(I32), 0)
 
         nc.sync.dma_start(evicted_list[:], offs2)
         nc.sync.dma_start(kept_list[:], offs)
@@ -61,8 +61,6 @@ def tile_attend_softmerge_pl_kernel(tc, ekey_words, ekey_scales, keys_words, key
             row = 32 * q + KEPT_ROW
             (nc.scalar, nc.gpsimd)[q // 2].dma_start(keys_byte_pool[row : row + 4, :].bitcast(I32), keys_scales[0, 4 * q : 4 * q + 4, :].bitcast(I32))
 
-        fac_sb = placed("fac_sb", [P, PACK], F32, 4, 1)
-        nc.gpsimd.dma_start(fac_sb[:], fac.rearrange("(p t) o -> p (t o)", t=PACK))
         identity = sbuf("identity", [P, P], F32)
         make_identity(nc, identity[:])
 
@@ -80,6 +78,8 @@ def tile_attend_softmerge_pl_kernel(tc, ekey_words, ekey_scales, keys_words, key
         nc.vector.tensor_copy(keys_codes[:], keys_word_pool[:].indirect(kept_list[:]))
 
 
+        fac_sb = placed("fac_sb", [P, PACK], F32, 0, 1)
+        nc.gpsimd.dma_start(fac_sb[:], fac.rearrange("(p t) o -> p (t o)", t=PACK))
         for t in range(1, PACK):
             evals_pool.append(placed("evals_pool%d" % t, [P, T], F32, *((0, 3), (1, 0), (2, 0))[t - 1]))
             nc.sync.dma_start(evals_pool[t][:], evals_rows[:, t, :])
@@ -95,7 +95,7 @@ def tile_attend_softmerge_pl_kernel(tc, ekey_words, ekey_scales, keys_words, key
             nc.sync.dma_start(vals_pool[t][:], vals_rows[:, t, :])
 
         def gather_and_turn(t):
-            picked = placed("evals_picked%d" % t, [P, J], BF16, *((4, 0), (0, 3), (4, 1))[t - 1])
+            picked = placed("evals_picked%d" % t, [P, J], BF16, *((4, 0), (0, 3), (0, 1))[t - 1])
             nc.vector.tensor_copy(picked[:], evals_pool[t][:].indirect(evicted_list[:]))
             turn(t, picked, "turned")
 

@@ -1,7 +1,6 @@
 from contextlib import ExitStack
 
 import concourse.mybir as mybir
-from concourse.masks import make_identity
 
 D, T, J, I, E = 512, 2048, 512, 512, 512
 FLOPS = 2 * D * J * I + 2 * J * E * I
@@ -22,7 +21,7 @@ PACK = 4
 QUADS = 4
 HALF = I // 2
 KEPT_ROW = 4
-LANE_KIB = 22
+KIB = 1024
 
 
 def tile_attend_softmerge_pl_kernel(tc, ekey_words, ekey_scales, keys_words, keys_scales, fac, evals, vals, offs, offs2, out_0, out_1, out_2):
@@ -35,67 +34,66 @@ def tile_attend_softmerge_pl_kernel(tc, ekey_words, ekey_scales, keys_words, key
         def sbuf(name, shape, dtype):
             return held.tile(shape, dtype, name=name, align_bytes=64)
 
-        def placed(name, shape, dtype, lane, kib):
-            return shared.tile(shape, dtype, name=name, align_bytes=64, offset=(lane * LANE_KIB + kib) * 1024)
+        def placed(name, shape, dtype, offset):
+            return shared.tile(shape, dtype, name=name, align_bytes=64, offset=offset)
 
         kept_list = held.tile([P, I // 16], U16, name="kept_list")
         evicted_list = held.tile([P, J // 16], U16, name="evicted_list")
-
-        ekey_byte_pool = placed("ekey_byte_pool", [P, T], U8, 1, 0)
-        ekey_word_pool = placed("ekey_word_pool", [P, T], U32, 0, 0)
-        keys_word_pool = placed("keys_word_pool", [P, T], U32, 2, 7)
-        keys_byte_pool = placed("keys_byte_pool", [P, T], U8, 3, 0)
-        nc.vector.memset(keys_byte_pool[:].bitcast(I32), 0)
-        nc.vector.memset(ekey_byte_pool[:].bitcast(I32), 0)
-
         nc.sync.dma_start(evicted_list[:], offs2)
         nc.sync.dma_start(kept_list[:], offs)
+
+        ekey_word_pool = sbuf("ekey_word_pool", [P, T], U32)
         nc.sync.dma_start(ekey_word_pool[:].bitcast(I32), ekey_words[0].rearrange("p n t -> p (n t)").bitcast(I32))
-        for q in range(QUADS):
-            nc.scalar.dma_start(ekey_byte_pool[32 * q : 32 * q + 4, :].bitcast(I32), ekey_scales[0, 4 * q : 4 * q + 4, :].bitcast(I32))
-        evals_rows = evals.rearrange("(p t) c -> p t c", t=PACK)
-        evals_pool = [sbuf("evals_pool0", [P, T], F32)]
-        nc.sync.dma_start(evals_pool[0][:], evals_rows[:, 0, :])
-        nc.sync.dma_start(keys_word_pool[:].bitcast(I32), keys_words[0].rearrange("p n t -> p (n t)").bitcast(I32))
-        for q in range(QUADS):
-            row = 32 * q + KEPT_ROW
-            (nc.scalar, nc.gpsimd)[q // 2].dma_start(keys_byte_pool[row : row + 4, :].bitcast(I32), keys_scales[0, 4 * q : 4 * q + 4, :].bitcast(I32))
 
+        ekey_byte_pool = placed("ekey_byte_pool", [P, T], U8, 74 * KIB)
+        keys_byte_pool = placed("keys_byte_pool", [P, T], U8, 76 * KIB)
+        zeros = placed("zeros", [P, 9 * T + 16], F32, 0)
+        nc.vector.memset(ekey_byte_pool[:].bitcast(I32), 0)
+        nc.vector.memset(zeros[:, 0:P], 0.0)
+        nc.vector.memset(keys_byte_pool[:].bitcast(I32), 0)
         identity = sbuf("identity", [P, P], F32)
-        make_identity(nc, identity[:])
+        nc.gpsimd.affine_select(out=identity[:], in_=zeros[:, 0:P], compare_op=ALU.not_equal, fill=1.0, base=0, pattern=[[-1, P]], channel_multiplier=1)
 
+        for q in range(QUADS):
+            nc.scalar.dma_start(ekey_byte_pool[q:P:32, :].bitcast(I32), ekey_scales[0, q:16:4, :].bitcast(I32))
+        for q in range(QUADS):
+            (nc.scalar, nc.gpsimd)[q // 2].dma_start(keys_byte_pool[KEPT_ROW + q : P : 32, :].bitcast(I32), keys_scales[0, q:16:4, :].bitcast(I32))
+
+        evals_rows = evals.rearrange("(p t) c -> p t c", t=PACK)
         vals_rows = vals.rearrange("(p t) c -> p t c", t=PACK)
+        evals_pool = [placed("evals_pool0", [P, T], F32, 0)]
+        nc.sync.dma_start(evals_pool[0][:], evals_rows[:, 0, :])
+        keys_word_pool = placed("keys_word_pool", [P, T], U32, 64 * KIB)
+        nc.sync.dma_start(keys_word_pool[:].bitcast(I32), keys_words[0].rearrange("p n t -> p (n t)").bitcast(I32))
+        fac_sb = placed("fac_sb", [P, PACK], F32, 72 * KIB)
+        nc.sync.dma_start(fac_sb[:], fac.rearrange("(p t) o -> p (t o)", t=PACK))
 
-        ekey_bytes = placed("ekey_bytes", [P, J], U8, 0, 0)
-        ekey_codes = sbuf("ekey_codes", [P, J], U32)
+        ekey_bytes = sbuf("ekey_bytes", [P, J], U8)
+        ekey_codes = placed("ekey_codes", [P, J], U32, 74 * KIB)
         ekey_scale = sbuf("ekey_scale", [P, J], U8)
         keys_scale = sbuf("keys_scale", [P, I], U8)
-        keys_codes = placed("keys_codes", [P, I], U32, 3, 0)
-        nc.vector.tensor_copy(ekey_codes[:].rearrange("p (t s) -> p s t", t=PACK), ekey_word_pool[:].indirect(evicted_list[:]))
+        keys_codes = placed("keys_codes", [P, I], U32, 76 * KIB)
         nc.vector.tensor_copy(ekey_bytes[:], ekey_byte_pool[:].indirect(evicted_list[:]))
+        nc.vector.tensor_copy(ekey_codes[:].rearrange("p (t s) -> p s t", t=PACK), ekey_word_pool[:].indirect(evicted_list[:]))
         nc.vector.tensor_copy(ekey_scale[:].rearrange("p (t s) -> p t s", t=PACK), ekey_bytes[:].rearrange("p (s t) -> p t s", t=PACK))
         nc.vector.tensor_copy(keys_scale[:], keys_byte_pool[:].indirect(kept_list[:]))
         nc.vector.tensor_copy(keys_codes[:], keys_word_pool[:].indirect(kept_list[:]))
 
-
-        fac_sb = placed("fac_sb", [P, PACK], F32, 0, 1)
-        nc.gpsimd.dma_start(fac_sb[:], fac.rearrange("(p t) o -> p (t o)", t=PACK))
         for t in range(1, PACK):
-            evals_pool.append(placed("evals_pool%d" % t, [P, T], F32, *((0, 3), (1, 0), (2, 0))[t - 1]))
+            evals_pool.append(placed("evals_pool%d" % t, [P, T], F32, t * 8 * KIB))
             nc.sync.dma_start(evals_pool[t][:], evals_rows[:, t, :])
-
         vals_pool = []
+        for t in range(PACK):
+            vals_pool.append(placed("vals_pool%d" % t, [P, T], F32, (4 + t) * 8 * KIB))
+            nc.sync.dma_start(vals_pool[t][:], vals_rows[:, t, :])
+
         turned = []
         vt_grouped = []
         vt_codes = [sbuf("vt_codes%d" % t, [P, P], U32) for t in range(PACK)]
         vt_scale = [sbuf("vt_scale%d" % t, [P, P], U8) for t in range(PACK)]
 
-        def load_vals(t):
-            vals_pool.append(placed("vals_pool%d" % t, [P, T], F32, *((2, 14), (3, 0), (0, 4), (1, 0))[t]))
-            nc.sync.dma_start(vals_pool[t][:], vals_rows[:, t, :])
-
         def gather_and_turn(t):
-            picked = placed("evals_picked%d" % t, [P, J], BF16, *((4, 0), (0, 3), (0, 1))[t - 1])
+            picked = placed("evals_picked%d" % t, [P, J], BF16, (74, 78, 79)[t - 1] * KIB)
             nc.vector.tensor_copy(picked[:], evals_pool[t][:].indirect(evicted_list[:]))
             turn(t, picked, "turned")
 
@@ -112,15 +110,14 @@ def tile_attend_softmerge_pl_kernel(tc, ekey_words, ekey_scales, keys_words, key
         def quantise_vt(t):
             nc.vector.quantize_mx(vt_codes[t][:].bitcast(FP8X4), vt_scale[t][:], vt_grouped[t][:])
 
-        load_vals(0)
         evals_rounded = sbuf("evals_rounded", [P, T], BF16)
         picked_first = sbuf("evals_picked0", [P, J], BF16)
         nc.scalar.activation(evals_rounded[:], evals_pool[0][:], ACT.Copy)
         nc.scalar.activation(picked_first[:], evals_rounded[:].indirect(evicted_list[:]), ACT.Copy)
 
         neg_max = sbuf("neg_max", [P, PACK], F32)
-        row_sum = sbuf("row_sum", [P, PACK], F32)
-        factor = sbuf("factor", [P, 2], F32)
+        sum_low = sbuf("sum_low", [P, 2], F32)
+        sum_high = placed("sum_high", [P, 32], F32, 79 * KIB - 64)
         prob = sbuf("prob", [P, PACK, I], F32)
         w_rows = sbuf("w_rows", [P, PACK, I], BF16)
         for t in range(PACK):
@@ -129,64 +126,67 @@ def tile_attend_softmerge_pl_kernel(tc, ekey_words, ekey_scales, keys_words, key
             nc.tensor.matmul_mx(score[:], lhsT=ekey_codes[:, cols].bitcast(FP8X4), lhsT_scale=ekey_scale[:, cols],
                                 rhs=keys_codes[:].bitcast(FP8X4), rhs_scale=keys_scale[KEPT_ROW:P, :], start=True, stop=True)
             nc.vector.tensor_reduce(neg_max[:, t : t + 1], score[:], AXIS.X, ALU.max, negate=True)
-            nc.scalar.activation(prob[:, t, :], score[:], ACT.Exp, bias=neg_max[:, t : t + 1], accum_out=row_sum[:, t : t + 1])
+            nc.scalar.activation(prob[:, t, :], score[:], ACT.Exp, bias=neg_max[:, t : t + 1], accum_out=(sum_low, sum_high)[t // 2][:, t % 2 : t % 2 + 1])
         turn(0, picked_first, "product")
-        load_vals(1)
-        inv_low = placed("inv_low", [P, 2], F32, 4, 0)
-        nc.vector.reciprocal(inv_low[:], row_sum[:, 0:2])
+        inv_low = sbuf("inv_low", [P, 2], F32)
+        factor = sbuf("factor", [P, 2], F32)
+        nc.vector.reciprocal(inv_low[:], sum_low[:])
         nc.vector.tensor_tensor(factor[:], inv_low[:], fac_sb[:, 0:2], ALU.mult)
         for t in (0, 1):
             nc.scalar.activation(w_rows[:, t, :], prob[:, t, :], ACT.Copy, scale=factor[:, t : t + 1])
         gather_and_turn(1)
-        load_vals(2)
-        inv_high = placed("inv_high", [P, 2], F32, 0, 3)
-        nc.vector.reciprocal(inv_high[:], row_sum[:, 2:4])
+        inv_high = sbuf("inv_high", [P, 2], F32)
+        nc.vector.reciprocal(inv_high[:], sum_high[:, 0:2])
         for t in (2, 3):
             nc.vector.tensor_scalar(w_rows[:, t, :], prob[:, t, :], inv_high[:, t - 2 : t - 1], fac_sb[:, t : t + 1], ALU.mult, ALU.mult)
-        w_grouped = placed("w_grouped", [P, I, PACK], BF16, 4, 2)
+        w_grouped = placed("w_grouped", [P, I, PACK], BF16, 80 * KIB)
         nc.scalar.copy(w_grouped[:], w_rows[:].rearrange("p t i -> p i t"))
-
+        group_vt(0)
+        group_vt(1)
         gather_and_turn(2)
-        load_vals(3)
+        group_vt(2)
+        quantise_vt(0)
         gather_and_turn(3)
-        for t in range(PACK):
-            group_vt(t)
-        w_codes = placed("w_codes", [P, I], U32, 2, 0)
+        group_vt(3)
+        quantise_vt(1)
+        w_codes = placed("w_codes", [P, I], U32, 24 * KIB)
         w_scale = sbuf("w_scale", [P, I], U8)
         nc.vector.quantize_mx(w_codes[:].bitcast(FP8X4), w_scale[:], w_grouped[:].rearrange("p i t -> p (i t)"))
+        quantise_vt(2)
+        quantise_vt(3)
 
         merged = []
         for t in range(PACK):
-            quantise_vt(t)
             merged.append(psum.tile([P, I], F32, name="merged", tag="product"))
             nc.tensor.matmul_mx(merged[t][:], lhsT=vt_codes[t][:].bitcast(FP8X4), lhsT_scale=vt_scale[t][:],
                                 rhs=w_codes[:].bitcast(FP8X4), rhs_scale=w_scale[:], start=True, stop=True)
-
-        kept = placed("kept", [P, I], F32, 4, 2)
+        merged_sb = sbuf("merged_sb", [P, PACK, I], F32)
+        for t in range(1, PACK):
+            nc.scalar.copy(merged_sb[:, t, :], merged[t][:])
+        kept = placed("kept", [P, I], F32, 80 * KIB)
         nc.vector.tensor_copy(kept[:], vals_pool[0][:].indirect(kept_list[:]))
+
         out_rows = out_0.rearrange("(p t) i -> p t i", t=PACK)
         y_low = sbuf("y_low", [P, 2, I], F32)
         y_high = sbuf("y_high", [P, 2, I], F32)
         y_grouped = sbuf("y_grouped", [P, I, PACK], BF16)
         y_codes = sbuf("y_codes", [P, I], U32)
         y_scale = sbuf("y_scale", [P, I], U8)
-        nc.vector.tensor_tensor(y_low[:, 0, :], merged[0][:], kept[:], ALU.add)
-        nc.sync.dma_start(out_rows[:, 0, :], y_low[:, 0, :])
-        merged_sb = sbuf("merged_sb", [P, PACK - 1, I], F32)
-        for t in range(1, PACK):
-            nc.scalar.copy(merged_sb[:, t - 1, :], merged[t][:])
-        for t in (1, 2):
+        last = PACK - 1
+        for t in range(last):
             y_t = (y_low, y_high)[t // 2][:, t % 2, :]
-            nc.vector.tensor_tensor(y_t, vals_pool[t][:].indirect(kept_list[:]), merged_sb[:, t - 1, :], ALU.add)
+            if t == 0:
+                nc.vector.tensor_tensor(y_t, merged[0][:], kept[:], ALU.add)
+            else:
+                nc.vector.tensor_tensor(y_t, vals_pool[t][:].indirect(kept_list[:]), merged_sb[:, t, :], ALU.add)
             nc.sync.dma_start(out_rows[:, t, :], y_t)
             if t == 1:
                 nc.scalar.copy(y_grouped[:, :, 0:2], y_low[:].rearrange("p t i -> p i t"))
-        last = PACK - 1
         words_out = out_1[0].rearrange("p n t -> p (n t)").bitcast(I32)
         halves = (slice(0, HALF), slice(HALF, I))
         for h, cols in enumerate(halves):
             nc.vector.tensor_tensor(y_high[:, 1, cols], vals_pool[last][:].indirect(kept_list[:, h * HALF // 16 : (h + 1) * HALF // 16]),
-                                    merged_sb[:, last - 1, cols], ALU.add)
+                                    merged_sb[:, last, cols], ALU.add)
         nc.scalar.copy(y_grouped[:, halves[0], 2:4], y_high[:, :, halves[0]].rearrange("p t i -> p i t"))
         nc.vector.tensor_copy(y_grouped[:, halves[1], 2:4], y_high[:, :, halves[1]].rearrange("p t i -> p i t"))
         nc.sync.dma_start(out_rows[:, last, :], y_high[:, 1, :])

@@ -59,12 +59,12 @@ def tile_attend_softmerge_pl_kernel(tc, ekey_words, ekey_scales, keys_words, key
         for q in range(QUADS):
             (nc.scalar, nc.gpsimd)[q // 2].dma_start(keys_byte_pool[KEPT_ROW + q : P : 32, :].bitcast(I32), keys_scales[0, q:16:4, :].bitcast(I32))
 
+        keys_word_pool = placed("keys_word_pool", [P, T], U32, 64 * KIB)
+        nc.sync.dma_start(keys_word_pool[:].bitcast(I32), keys_words[0].rearrange("p n t -> p (n t)").bitcast(I32))
         evals_rows = evals.rearrange("(p t) c -> p t c", t=PACK)
         vals_rows = vals.rearrange("(p t) c -> p t c", t=PACK)
         evals_pool = [placed("evals_pool0", [P, T], F32, 0)]
         nc.sync.dma_start(evals_pool[0][:], evals_rows[:, 0, :])
-        keys_word_pool = placed("keys_word_pool", [P, T], U32, 64 * KIB)
-        nc.sync.dma_start(keys_word_pool[:].bitcast(I32), keys_words[0].rearrange("p n t -> p (n t)").bitcast(I32))
         fac_sb = placed("fac_sb", [P, PACK], F32, 72 * KIB)
         nc.sync.dma_start(fac_sb[:], fac.rearrange("(p t) o -> p (t o)", t=PACK))
 
@@ -72,7 +72,7 @@ def tile_attend_softmerge_pl_kernel(tc, ekey_words, ekey_scales, keys_words, key
         ekey_codes = placed("ekey_codes", [P, J], U32, 74 * KIB)
         ekey_scale = sbuf("ekey_scale", [P, J], U8)
         keys_scale = sbuf("keys_scale", [P, I], U8)
-        keys_codes = placed("keys_codes", [P, I], U32, 76 * KIB)
+        keys_codes = placed("keys_codes", [P, I], U32, 77 * KIB)
         nc.vector.tensor_copy(ekey_bytes[:], ekey_byte_pool[:].indirect(evicted_list[:]))
         nc.vector.tensor_copy(ekey_codes[:].rearrange("p (t s) -> p s t", t=PACK), ekey_word_pool[:].indirect(evicted_list[:]))
         nc.vector.tensor_copy(ekey_scale[:].rearrange("p (t s) -> p t s", t=PACK), ekey_bytes[:].rearrange("p (s t) -> p t s", t=PACK))
@@ -89,13 +89,13 @@ def tile_attend_softmerge_pl_kernel(tc, ekey_words, ekey_scales, keys_words, key
 
         turned = []
         vt_grouped = []
-        vt_codes = [sbuf("vt_codes%d" % t, [P, P], U32) for t in range(PACK)]
+        vt_codes = []
         vt_scale = [sbuf("vt_scale%d" % t, [P, P], U8) for t in range(PACK)]
 
-        def gather_and_turn(t):
-            picked = placed("evals_picked%d" % t, [P, J], BF16, (74, 78, 79)[t - 1] * KIB)
+        def gather_evals(t):
+            picked = placed("evals_picked%d" % t, [P, J], BF16, (76, 74, 96, 97)[t] * KIB)
             nc.vector.tensor_copy(picked[:], evals_pool[t][:].indirect(evicted_list[:]))
-            turn(t, picked, "turned")
+            return picked
 
         def turn(t, picked, banks):
             pairs = picked[:].bitcast(F32)
@@ -104,55 +104,54 @@ def tile_attend_softmerge_pl_kernel(tc, ekey_words, ekey_scales, keys_words, key
                 nc.tensor.transpose(turned[t][:, u, :], pairs[:, u : J // 2 : 2], identity[:])
 
         def group_vt(t):
-            vt_grouped.append(sbuf("vt_grouped%d" % t, [P, P * PACK], BF16))
+            vt_grouped.append(placed("vt_grouped%d" % t, [P, P * PACK], BF16, (85 + t) * KIB))
             nc.scalar.copy(vt_grouped[t][:].bitcast(F32).rearrange("p (e u) -> p e u", u=2), turned[t][:].rearrange("p u e -> p e u"))
 
         def quantise_vt(t):
+            vt_codes.append(placed("vt_codes%d" % t, [P, P], U32, (90, 26, 27, 28)[t] * KIB))
             nc.vector.quantize_mx(vt_codes[t][:].bitcast(FP8X4), vt_scale[t][:], vt_grouped[t][:])
 
-        evals_rounded = sbuf("evals_rounded", [P, T], BF16)
-        picked_first = sbuf("evals_picked0", [P, J], BF16)
-        nc.scalar.activation(evals_rounded[:], evals_pool[0][:], ACT.Copy)
-        nc.scalar.activation(picked_first[:], evals_rounded[:].indirect(evicted_list[:]), ACT.Copy)
+        picked_first = gather_evals(0)
 
         neg_max = sbuf("neg_max", [P, PACK], F32)
         sum_low = sbuf("sum_low", [P, 2], F32)
-        sum_high = placed("sum_high", [P, 32], F32, 79 * KIB - 64)
-        prob = sbuf("prob", [P, PACK, I], F32)
-        w_rows = sbuf("w_rows", [P, PACK, I], BF16)
+        sum_high = sbuf("sum_high", [P, 2], F32)
+        prob = [placed("prob%d" % t, [P, I], F32, (92 + 2 * t) * KIB) for t in range(PACK)]
+        w_rows = placed("w_rows", [P, PACK, I], BF16, 86 * KIB)
         for t in range(PACK):
             cols = slice(t * P, (t + 1) * P)
             score = psum.tile([P, I], F32, name="score", tag="product")
             nc.tensor.matmul_mx(score[:], lhsT=ekey_codes[:, cols].bitcast(FP8X4), lhsT_scale=ekey_scale[:, cols],
                                 rhs=keys_codes[:].bitcast(FP8X4), rhs_scale=keys_scale[KEPT_ROW:P, :], start=True, stop=True)
             nc.vector.tensor_reduce(neg_max[:, t : t + 1], score[:], AXIS.X, ALU.max, negate=True)
-            nc.scalar.activation(prob[:, t, :], score[:], ACT.Exp, bias=neg_max[:, t : t + 1], accum_out=(sum_low, sum_high)[t // 2][:, t % 2 : t % 2 + 1])
+            nc.scalar.activation(prob[t][:], score[:], ACT.Exp, bias=neg_max[:, t : t + 1], accum_out=(sum_low, sum_high)[t // 2][:, t % 2 : t % 2 + 1])
         turn(0, picked_first, "product")
         inv_low = sbuf("inv_low", [P, 2], F32)
+        inv_high = sbuf("inv_high", [P, 2], F32)
         factor = sbuf("factor", [P, 2], F32)
         nc.vector.reciprocal(inv_low[:], sum_low[:])
+        group_vt(0)
+        turn(1, gather_evals(1), "turned")
+        nc.vector.reciprocal(inv_high[:], sum_high[:])
         nc.vector.tensor_tensor(factor[:], inv_low[:], fac_sb[:, 0:2], ALU.mult)
         for t in (0, 1):
-            nc.scalar.activation(w_rows[:, t, :], prob[:, t, :], ACT.Copy, scale=factor[:, t : t + 1])
-        gather_and_turn(1)
-        inv_high = sbuf("inv_high", [P, 2], F32)
-        nc.vector.reciprocal(inv_high[:], sum_high[:, 0:2])
+            nc.scalar.activation(w_rows[:, t, :], prob[t][:], ACT.Copy, scale=factor[:, t : t + 1])
         for t in (2, 3):
-            nc.vector.tensor_scalar(w_rows[:, t, :], prob[:, t, :], inv_high[:, t - 2 : t - 1], fac_sb[:, t : t + 1], ALU.mult, ALU.mult)
+            nc.vector.tensor_scalar(w_rows[:, t, :], prob[t][:], inv_high[:, t - 2 : t - 1], fac_sb[:, t : t + 1], ALU.mult, ALU.mult)
         w_grouped = placed("w_grouped", [P, I, PACK], BF16, 80 * KIB)
-        nc.scalar.copy(w_grouped[:], w_rows[:].rearrange("p t i -> p i t"))
-        group_vt(0)
-        group_vt(1)
-        gather_and_turn(2)
-        group_vt(2)
+        nc.scalar.copy(w_grouped[:].rearrange("p (c i) t -> p c t i", i=4), w_rows[:].rearrange("p t (c i) -> p c t i", i=4))
+        turn(2, gather_evals(2), "turned")
+        turn(3, gather_evals(3), "turned")
+        for t in range(1, PACK):
+            group_vt(t)
         quantise_vt(0)
-        gather_and_turn(3)
-        group_vt(3)
-        quantise_vt(1)
         w_codes = placed("w_codes", [P, I], U32, 24 * KIB)
         w_scale = sbuf("w_scale", [P, I], U8)
         nc.vector.quantize_mx(w_codes[:].bitcast(FP8X4), w_scale[:], w_grouped[:].rearrange("p i t -> p (i t)"))
+        quantise_vt(1)
         quantise_vt(2)
+        kept = placed("kept", [P, I], F32, 80 * KIB)
+        nc.vector.tensor_copy(kept[:], vals_pool[0][:].indirect(kept_list[:]))
         quantise_vt(3)
 
         merged = []
@@ -163,8 +162,6 @@ def tile_attend_softmerge_pl_kernel(tc, ekey_words, ekey_scales, keys_words, key
         merged_sb = sbuf("merged_sb", [P, PACK, I], F32)
         for t in range(1, PACK):
             nc.scalar.copy(merged_sb[:, t, :], merged[t][:])
-        kept = placed("kept", [P, I], F32, 80 * KIB)
-        nc.vector.tensor_copy(kept[:], vals_pool[0][:].indirect(kept_list[:]))
 
         out_rows = out_0.rearrange("(p t) i -> p t i", t=PACK)
         y_low = sbuf("y_low", [P, 2, I], F32)

@@ -20,6 +20,8 @@ P = 128
 PACK = 4
 QUADS = 4
 HALF = I // 2
+PIECES = 4
+PIECE = I // PIECES
 KEPT_ROW = 4
 KIB = 1024
 
@@ -39,79 +41,90 @@ def tile_attend_softmerge_pl_kernel(tc, ekey_words, ekey_scales, keys_words, key
 
         kept_list = held.tile([P, I // 16], U16, name="kept_list")
         evicted_list = held.tile([P, J // 16], U16, name="evicted_list")
+        ekey_word_pool = sbuf("ekey_word_pool", [P, T], U32)
+        nc.sync.dma_start(ekey_word_pool[:].bitcast(I32), ekey_words[0].rearrange("p n t -> p (n t)").bitcast(I32))
         nc.sync.dma_start(evicted_list[:], offs2)
         nc.sync.dma_start(kept_list[:], offs)
 
-        ekey_word_pool = sbuf("ekey_word_pool", [P, T], U32)
-        nc.sync.dma_start(ekey_word_pool[:].bitcast(I32), ekey_words[0].rearrange("p n t -> p (n t)").bitcast(I32))
-
-        ekey_byte_pool = placed("ekey_byte_pool", [P, T], U8, 74 * KIB)
-        keys_byte_pool = placed("keys_byte_pool", [P, T], U8, 76 * KIB)
-        zeros = placed("zeros", [P, 9 * T + 16], F32, 0)
-        nc.vector.memset(ekey_byte_pool[:].bitcast(I32), 0)
-        nc.vector.memset(zeros[:, 0:P], 0.0)
-        nc.vector.memset(keys_byte_pool[:].bitcast(I32), 0)
+        ekey_byte_pool = sbuf("ekey_byte_pool", [P, T], U8)
         identity = sbuf("identity", [P, P], F32)
-        nc.gpsimd.affine_select(out=identity[:], in_=zeros[:, 0:P], compare_op=ALU.not_equal, fill=1.0, base=0, pattern=[[-1, P]], channel_multiplier=1)
-
+        zeros_left = placed("zeros_left", [P, (10 * KIB + 64) // 4], F32, 0)
+        nc.vector.memset(ekey_byte_pool[:].bitcast(I32), 0)
+        nc.vector.memset(zeros_left[:, 0 : P // 2], 0.0)
+        nc.gpsimd.affine_select(out=identity[:, 0 : P // 2], in_=zeros_left[:, 0 : P // 2], compare_op=ALU.not_equal, fill=1.0, base=0,
+                                pattern=[[-1, P // 2]], channel_multiplier=1)
         for q in range(QUADS):
             nc.scalar.dma_start(ekey_byte_pool[q:P:32, :].bitcast(I32), ekey_scales[0, q:16:4, :].bitcast(I32))
-        for q in range(QUADS):
-            (nc.scalar, nc.gpsimd)[q // 2].dma_start(keys_byte_pool[KEPT_ROW + q : P : 32, :].bitcast(I32), keys_scales[0, q:16:4, :].bitcast(I32))
 
-        keys_word_pool = placed("keys_word_pool", [P, T], U32, 64 * KIB)
-        nc.sync.dma_start(keys_word_pool[:].bitcast(I32), keys_words[0].rearrange("p n t -> p (n t)").bitcast(I32))
         evals_rows = evals.rearrange("(p t) c -> p t c", t=PACK)
         vals_rows = vals.rearrange("(p t) c -> p t c", t=PACK)
         evals_pool = [placed("evals_pool0", [P, T], F32, 0)]
         nc.sync.dma_start(evals_pool[0][:], evals_rows[:, 0, :])
-        fac_sb = placed("fac_sb", [P, PACK], F32, 72 * KIB)
+
+        keys_byte_pool = placed("keys_byte_pool", [P, T], U8, 8 * KIB)
+        zeros_right = placed("zeros_right", [P, 69 * KIB // 4], F32, 10 * KIB)
+        nc.vector.memset(keys_byte_pool[:].bitcast(I32), 0)
+        nc.vector.memset(zeros_right[:, 0 : P // 2], 0.0)
+        nc.gpsimd.affine_select(out=identity[:, P // 2 : P], in_=zeros_right[:, 0 : P // 2], compare_op=ALU.not_equal, fill=1.0, base=-(P // 2),
+                                pattern=[[-1, P // 2]], channel_multiplier=1)
+        for q in range(QUADS):
+            nc.sync.dma_start(keys_byte_pool[KEPT_ROW + q : P : 32, :].bitcast(I32), keys_scales[0, q:16:4, :].bitcast(I32))
+        keys_word_pool = placed("keys_word_pool", [P, T], U32, 10 * KIB)
+        nc.sync.dma_start(keys_word_pool[:].bitcast(I32), keys_words[0].rearrange("p n t -> p (n t)").bitcast(I32))
+        fac_sb = placed("fac_sb", [P, PACK], F32, 74 * KIB)
         nc.sync.dma_start(fac_sb[:], fac.rearrange("(p t) o -> p (t o)", t=PACK))
 
-        ekey_bytes = sbuf("ekey_bytes", [P, J], U8)
-        ekey_codes = placed("ekey_codes", [P, J], U32, 74 * KIB)
+        ekey_bytes = placed("ekey_bytes", [P, J], U8, 78 * KIB)
+        ekey_codes = placed("ekey_codes", [P, J], U32, 76 * KIB)
         ekey_scale = sbuf("ekey_scale", [P, J], U8)
         keys_scale = sbuf("keys_scale", [P, I], U8)
-        keys_codes = placed("keys_codes", [P, I], U32, 77 * KIB)
-        nc.vector.tensor_copy(ekey_bytes[:], ekey_byte_pool[:].indirect(evicted_list[:]))
+        keys_codes = sbuf("keys_codes", [P, I], U32)
         nc.vector.tensor_copy(ekey_codes[:].rearrange("p (t s) -> p s t", t=PACK), ekey_word_pool[:].indirect(evicted_list[:]))
-        nc.vector.tensor_copy(ekey_scale[:].rearrange("p (t s) -> p t s", t=PACK), ekey_bytes[:].rearrange("p (s t) -> p t s", t=PACK))
+        nc.vector.tensor_copy(ekey_bytes[:], ekey_byte_pool[:].indirect(evicted_list[:]))
         nc.vector.tensor_copy(keys_scale[:], keys_byte_pool[:].indirect(kept_list[:]))
-        nc.vector.tensor_copy(keys_codes[:], keys_word_pool[:].indirect(kept_list[:]))
+        nc.vector.tensor_copy(ekey_scale[:].rearrange("p (t s) -> p t s", t=PACK), ekey_bytes[:].rearrange("p (s t) -> p t s", t=PACK))
+        halves = (slice(0, HALF), slice(HALF, I))
+        for cols in halves:
+            nc.vector.tensor_copy(keys_codes[:, cols], keys_word_pool[:].indirect(kept_list[:, cols.start // 16 : cols.stop // 16]))
 
         for t in range(1, PACK):
-            evals_pool.append(placed("evals_pool%d" % t, [P, T], F32, t * 8 * KIB))
+            evals_pool.append(placed("evals_pool%d" % t, [P, T], F32, (10 + 8 * t) * KIB))
             nc.sync.dma_start(evals_pool[t][:], evals_rows[:, t, :])
         vals_pool = []
         for t in range(PACK):
-            vals_pool.append(placed("vals_pool%d" % t, [P, T], F32, (4 + t) * 8 * KIB))
+            vals_pool.append(placed("vals_pool%d" % t, [P, T], F32, (42 + 8 * t) * KIB))
             nc.sync.dma_start(vals_pool[t][:], vals_rows[:, t, :])
 
-        turned = []
-        vt_grouped = []
-        vt_codes = []
-        vt_scale = [sbuf("vt_scale%d" % t, [P, P], U8) for t in range(PACK)]
+        vt_operand = {}
 
         def gather_evals(t):
-            picked = placed("evals_picked%d" % t, [P, J], BF16, (76, 74, 96, 97)[t] * KIB)
+            picked = placed("evals_picked%d" % t, [P, J], BF16, (76, 96, 97)[t - 1] * KIB)
             nc.vector.tensor_copy(picked[:], evals_pool[t][:].indirect(evicted_list[:]))
             return picked
 
-        def turn(t, picked, banks):
+        def turn(picked, turned):
             pairs = picked[:].bitcast(F32)
-            turned.append(psum.tile([P, 2, P], F32, name="turned", tag=banks))
             for u in range(2):
-                nc.tensor.transpose(turned[t][:, u, :], pairs[:, u : J // 2 : 2], identity[:])
+                nc.tensor.transpose(turned[:, u, :], pairs[:, u : J // 2 : 2], identity[:])
 
-        def group_vt(t):
-            vt_grouped.append(placed("vt_grouped%d" % t, [P, P * PACK], BF16, (85 + t) * KIB))
-            nc.scalar.copy(vt_grouped[t][:].bitcast(F32).rearrange("p (e u) -> p e u", u=2), turned[t][:].rearrange("p u e -> p e u"))
+        def group_vt(first, turned, kib):
+            planes = turned.shape[1]
+            grouped = placed("vt_grouped%d" % first, [P, planes * P * PACK], BF16, kib * KIB)
+            nc.scalar.copy(grouped[:].bitcast(F32).rearrange("p (t e u) -> p t e u", t=planes, u=2), turned[:].rearrange("p t u e -> p t e u"))
+            return grouped
 
-        def quantise_vt(t):
-            vt_codes.append(placed("vt_codes%d" % t, [P, P], U32, (90, 26, 27, 28)[t] * KIB))
-            nc.vector.quantize_mx(vt_codes[t][:].bitcast(FP8X4), vt_scale[t][:], vt_grouped[t][:])
+        def quantise_vt(first, grouped, kib):
+            width = grouped.shape[1] // PACK
+            codes = placed("vt_codes%d" % first, [P, width], U32, kib * KIB)
+            scale = sbuf("vt_scale%d" % first, [P, width], U8)
+            nc.vector.quantize_mx(codes[:].bitcast(FP8X4), scale[:], grouped[:])
+            for n in range(width // P):
+                vt_operand[first + n] = (codes[:, n * P : (n + 1) * P], scale[:, n * P : (n + 1) * P])
 
-        picked_first = gather_evals(0)
+        evals_rounded = sbuf("evals_rounded", [P, T], BF16)
+        picked_first = sbuf("evals_picked0", [P, J], BF16)
+        nc.scalar.activation(evals_rounded[:], evals_pool[0][:], ACT.Copy)
+        nc.scalar.activation(picked_first[:], evals_rounded[:].indirect(evicted_list[:]), ACT.Copy)
 
         neg_max = sbuf("neg_max", [P, PACK], F32)
         sum_low = sbuf("sum_low", [P, 2], F32)
@@ -119,19 +132,23 @@ def tile_attend_softmerge_pl_kernel(tc, ekey_words, ekey_scales, keys_words, key
         prob = [placed("prob%d" % t, [P, I], F32, (92 + 2 * t) * KIB) for t in range(PACK)]
         w_rows = placed("w_rows", [P, PACK, I], BF16, 86 * KIB)
         for t in range(PACK):
-            cols = slice(t * P, (t + 1) * P)
+            rows = slice(t * P, (t + 1) * P)
             score = psum.tile([P, I], F32, name="score", tag="product")
-            nc.tensor.matmul_mx(score[:], lhsT=ekey_codes[:, cols].bitcast(FP8X4), lhsT_scale=ekey_scale[:, cols],
-                                rhs=keys_codes[:].bitcast(FP8X4), rhs_scale=keys_scale[KEPT_ROW:P, :], start=True, stop=True)
+            for cols in halves if t == 0 else (slice(0, I),):
+                nc.tensor.matmul_mx(score[:, cols], lhsT=ekey_codes[:, rows].bitcast(FP8X4), lhsT_scale=ekey_scale[:, rows],
+                                    rhs=keys_codes[:, cols].bitcast(FP8X4), rhs_scale=keys_scale[KEPT_ROW:P, cols], start=True, stop=True)
             nc.vector.tensor_reduce(neg_max[:, t : t + 1], score[:], AXIS.X, ALU.max, negate=True)
             nc.scalar.activation(prob[t][:], score[:], ACT.Exp, bias=neg_max[:, t : t + 1], accum_out=(sum_low, sum_high)[t // 2][:, t % 2 : t % 2 + 1])
-        turn(0, picked_first, "product")
+        turned_first = psum.tile([P, 1, 2, P], F32, name="turned_first", tag="product")
+        turned_middle = psum.tile([P, 2, 2, P], F32, name="turned_middle", tag="turned")
+        turned_last = psum.tile([P, 1, 2, P], F32, name="turned_last", tag="turned")
+        turn(picked_first, turned_first[:, 0])
         inv_low = sbuf("inv_low", [P, 2], F32)
         inv_high = sbuf("inv_high", [P, 2], F32)
         factor = sbuf("factor", [P, 2], F32)
         nc.vector.reciprocal(inv_low[:], sum_low[:])
-        group_vt(0)
-        turn(1, gather_evals(1), "turned")
+        grouped_first = group_vt(0, turned_first, 85)
+        turn(gather_evals(1), turned_middle[:, 0])
         nc.vector.reciprocal(inv_high[:], sum_high[:])
         nc.vector.tensor_tensor(factor[:], inv_low[:], fac_sb[:, 0:2], ALU.mult)
         for t in (0, 1):
@@ -140,24 +157,23 @@ def tile_attend_softmerge_pl_kernel(tc, ekey_words, ekey_scales, keys_words, key
             nc.vector.tensor_scalar(w_rows[:, t, :], prob[t][:], inv_high[:, t - 2 : t - 1], fac_sb[:, t : t + 1], ALU.mult, ALU.mult)
         w_grouped = placed("w_grouped", [P, I, PACK], BF16, 80 * KIB)
         nc.scalar.copy(w_grouped[:].rearrange("p (c i) t -> p c t i", i=4), w_rows[:].rearrange("p t (c i) -> p c t i", i=4))
-        turn(2, gather_evals(2), "turned")
-        turn(3, gather_evals(3), "turned")
-        for t in range(1, PACK):
-            group_vt(t)
-        quantise_vt(0)
-        w_codes = placed("w_codes", [P, I], U32, 24 * KIB)
+        turn(gather_evals(2), turned_middle[:, 1])
+        turn(gather_evals(3), turned_last[:, 0])
+        grouped_middle = group_vt(1, turned_middle, 86)
+        grouped_last = group_vt(3, turned_last, 88)
+        quantise_vt(0, grouped_first, 90)
+        w_codes = placed("w_codes", [P, I], U32, 34 * KIB)
         w_scale = sbuf("w_scale", [P, I], U8)
         nc.vector.quantize_mx(w_codes[:].bitcast(FP8X4), w_scale[:], w_grouped[:].rearrange("p i t -> p (i t)"))
-        quantise_vt(1)
-        quantise_vt(2)
+        quantise_vt(1, grouped_middle, 36)
         kept = placed("kept", [P, I], F32, 80 * KIB)
         nc.vector.tensor_copy(kept[:], vals_pool[0][:].indirect(kept_list[:]))
-        quantise_vt(3)
+        quantise_vt(3, grouped_last, 38)
 
         merged = []
         for t in range(PACK):
             merged.append(psum.tile([P, I], F32, name="merged", tag="product"))
-            nc.tensor.matmul_mx(merged[t][:], lhsT=vt_codes[t][:].bitcast(FP8X4), lhsT_scale=vt_scale[t][:],
+            nc.tensor.matmul_mx(merged[t][:], lhsT=vt_operand[t][0].bitcast(FP8X4), lhsT_scale=vt_operand[t][1],
                                 rhs=w_codes[:].bitcast(FP8X4), rhs_scale=w_scale[:], start=True, stop=True)
         merged_sb = sbuf("merged_sb", [P, PACK, I], F32)
         for t in range(1, PACK):
@@ -180,16 +196,16 @@ def tile_attend_softmerge_pl_kernel(tc, ekey_words, ekey_scales, keys_words, key
             if t == 1:
                 nc.scalar.copy(y_grouped[:, :, 0:2], y_low[:].rearrange("p t i -> p i t"))
         words_out = out_1[0].rearrange("p n t -> p (n t)").bitcast(I32)
-        halves = (slice(0, HALF), slice(HALF, I))
-        for h, cols in enumerate(halves):
-            nc.vector.tensor_tensor(y_high[:, 1, cols], vals_pool[last][:].indirect(kept_list[:, h * HALF // 16 : (h + 1) * HALF // 16]),
+        for piece in range(PIECES):
+            cols = slice(piece * PIECE, (piece + 1) * PIECE)
+            nc.vector.tensor_tensor(y_high[:, 1, cols], vals_pool[last][:].indirect(kept_list[:, piece * PIECE // 16 : (piece + 1) * PIECE // 16]),
                                     merged_sb[:, last, cols], ALU.add)
-        nc.scalar.copy(y_grouped[:, halves[0], 2:4], y_high[:, :, halves[0]].rearrange("p t i -> p i t"))
-        nc.vector.tensor_copy(y_grouped[:, halves[1], 2:4], y_high[:, :, halves[1]].rearrange("p t i -> p i t"))
+            (nc.scalar.copy if piece < PIECES - 1 else nc.vector.tensor_copy)(y_grouped[:, cols, 2:4], y_high[:, :, cols].rearrange("p t i -> p i t"))
         nc.sync.dma_start(out_rows[:, last, :], y_high[:, 1, :])
         for cols in halves:
             nc.vector.quantize_mx(y_codes[:, cols].bitcast(FP8X4), y_scale[:, cols], y_grouped[:, cols, :].rearrange("p i t -> p (i t)"))
-            nc.sync.dma_start(words_out[:, cols], y_codes[:, cols].bitcast(I32))
+            if cols.stop % HALF == 0:
+                nc.sync.dma_start(words_out[:, cols.stop - HALF : cols.stop], y_codes[:, cols.stop - HALF : cols.stop].bitcast(I32))
         for q in range(QUADS):
             queue = (nc.sync, nc.scalar)[q % 2]
             queue.dma_start(out_2[0, 4 * q : 4 * q + 4, :].bitcast(I32), y_scale[32 * q : 32 * q + 4, :].bitcast(I32))

@@ -37,7 +37,7 @@ def tile_attend_softmerge_pl_kernel(tc, ekey_words, ekey_scales, keys_words, key
             return held.tile(shape, dtype, name=name, align_bytes=64)
 
         def placed(name, shape, dtype, offset):
-            return shared.tile(shape, dtype, name=name, align_bytes=64, offset=offset)
+            return shared.tile(shape, dtype, name=name, align_bytes=64, offset=offset + 4 * KIB)
 
         kept_list = held.tile([P, I // 16], U16, name="kept_list")
         evicted_list = held.tile([P, J // 16], U16, name="evicted_list")
@@ -48,7 +48,7 @@ def tile_attend_softmerge_pl_kernel(tc, ekey_words, ekey_scales, keys_words, key
 
         ekey_byte_pool = sbuf("ekey_byte_pool", [P, T], U8)
         identity = sbuf("identity", [P, P], F32)
-        zeros_left = placed("zeros_left", [P, (10 * KIB + 64) // 4], F32, 0)
+        zeros_left = placed("zeros_left", [P, (14 * KIB + 64) // 4], F32, -4 * KIB)
         nc.vector.memset(ekey_byte_pool[:].bitcast(I32), 0)
         nc.vector.memset(zeros_left[:, 0 : P // 2], 0.0)
         nc.gpsimd.affine_select(out=identity[:, 0 : P // 2], in_=zeros_left[:, 0 : P // 2], compare_op=ALU.not_equal, fill=1.0, base=0,
@@ -62,27 +62,27 @@ def tile_attend_softmerge_pl_kernel(tc, ekey_words, ekey_scales, keys_words, key
         nc.sync.dma_start(evals_pool[0][:], evals_rows[:, 0, :])
 
         keys_byte_pool = placed("keys_byte_pool", [P, T], U8, 8 * KIB)
-        zeros_right = placed("zeros_right", [P, 69 * KIB // 4], F32, 10 * KIB)
+        zeros_right = placed("zeros_right", [P, 65 * KIB // 4], F32, 10 * KIB)
         nc.vector.memset(keys_byte_pool[:].bitcast(I32), 0)
         nc.vector.memset(zeros_right[:, 0 : P // 2], 0.0)
+        for q in range(QUADS):
+            (nc.sync, nc.gpsimd)[q // 2].dma_start(keys_byte_pool[KEPT_ROW + q : P : 32, :].bitcast(I32), keys_scales[0, q:16:4, :].bitcast(I32))
         nc.gpsimd.affine_select(out=identity[:, P // 2 : P], in_=zeros_right[:, 0 : P // 2], compare_op=ALU.not_equal, fill=1.0, base=-(P // 2),
                                 pattern=[[-1, P // 2]], channel_multiplier=1)
-        for q in range(QUADS):
-            nc.sync.dma_start(keys_byte_pool[KEPT_ROW + q : P : 32, :].bitcast(I32), keys_scales[0, q:16:4, :].bitcast(I32))
         keys_word_pool = placed("keys_word_pool", [P, T], U32, 10 * KIB)
         nc.sync.dma_start(keys_word_pool[:].bitcast(I32), keys_words[0].rearrange("p n t -> p (n t)").bitcast(I32))
         fac_sb = placed("fac_sb", [P, PACK], F32, 74 * KIB)
         nc.sync.dma_start(fac_sb[:], fac.rearrange("(p t) o -> p (t o)", t=PACK))
 
-        ekey_bytes = placed("ekey_bytes", [P, J], U8, 78 * KIB)
-        ekey_codes = placed("ekey_codes", [P, J], U32, 76 * KIB)
+        ekey_bytes = placed("ekey_bytes", [P, J], U8, -KIB)
+        ekey_codes = placed("ekey_codes", [P, J], U32, -4 * KIB)
         ekey_scale = sbuf("ekey_scale", [P, J], U8)
         keys_scale = sbuf("keys_scale", [P, I], U8)
-        keys_codes = sbuf("keys_codes", [P, I], U32)
+        keys_codes = placed("keys_codes", [P, I], U32, 8 * KIB)
         nc.vector.tensor_copy(ekey_codes[:].rearrange("p (t s) -> p s t", t=PACK), ekey_word_pool[:].indirect(evicted_list[:]))
         nc.vector.tensor_copy(ekey_bytes[:], ekey_byte_pool[:].indirect(evicted_list[:]))
-        nc.vector.tensor_copy(keys_scale[:], keys_byte_pool[:].indirect(kept_list[:]))
         nc.vector.tensor_copy(ekey_scale[:].rearrange("p (t s) -> p t s", t=PACK), ekey_bytes[:].rearrange("p (s t) -> p t s", t=PACK))
+        nc.vector.tensor_copy(keys_scale[:], keys_byte_pool[:].indirect(kept_list[:]))
         halves = (slice(0, HALF), slice(HALF, I))
         for cols in halves:
             nc.vector.tensor_copy(keys_codes[:, cols], keys_word_pool[:].indirect(kept_list[:, cols.start // 16 : cols.stop // 16]))
@@ -98,7 +98,7 @@ def tile_attend_softmerge_pl_kernel(tc, ekey_words, ekey_scales, keys_words, key
         vt_operand = {}
 
         def gather_evals(t):
-            picked = placed("evals_picked%d" % t, [P, J], BF16, (76, 96, 97)[t - 1] * KIB)
+            picked = placed("evals_picked%d" % t, [P, J], BF16, (-4, 96, 97)[t - 1] * KIB)
             nc.vector.tensor_copy(picked[:], evals_pool[t][:].indirect(evicted_list[:]))
             return picked
 

@@ -18,12 +18,30 @@ AXIS = mybir.AxisListType
 
 P = 128
 PACK = 4
-QUADS = 4
+QUADRANT = 32
+SCALE_ROWS = 16
+LIST_ROWS = 16
+KEYS_SCALE_ROW = 4
 HALF = I // 2
+EARLY = 3 * T // 4
 PIECES = 4
 PIECE = I // PIECES
-KEPT_ROW = 4
+RUN = 4
+
 KIB = 1024
+POOL_BYTES = 4 * T
+AT_EKEY_CODES = 0
+AT_EKEY_BYTES = 3 * KIB
+AT_FIRST_EVALS = 4 * KIB
+AT_KEYS_BYTES = AT_FIRST_EVALS + POOL_BYTES
+AT_LATE_LOADS = AT_KEYS_BYTES + T
+AT_LAST_EVALS = AT_LATE_LOADS + (PACK - 1) * POOL_BYTES
+AT_FAC = AT_LATE_LOADS + 2 * PACK * POOL_BYTES
+AT_W_GROUPED = 84 * KIB
+AT_FIRST_VT = 89 * KIB
+AT_W_ROWS = 90 * KIB
+AT_FIRST_VT_CODES = 94 * KIB
+AT_PROB = 96 * KIB
 
 
 def tile_attend_softmerge_pl_kernel(tc, ekey_words, ekey_scales, keys_words, keys_scales, fac, evals, vals, offs, offs2, out_0, out_1, out_2):
@@ -31,16 +49,19 @@ def tile_attend_softmerge_pl_kernel(tc, ekey_words, ekey_scales, keys_words, key
     with ExitStack() as ctx:
         held = ctx.enter_context(tc.tile_pool(name="held", bufs=1))
         shared = ctx.enter_context(tc.tile_pool(name="shared", bufs=1))
-        psum = ctx.enter_context(tc.psum_pool(name="psum", bufs=4))
+        psum = ctx.enter_context(tc.psum_pool(name="psum", bufs=PACK))
 
         def sbuf(name, shape, dtype):
             return held.tile(shape, dtype, name=name, align_bytes=64)
 
         def placed(name, shape, dtype, offset):
-            return shared.tile(shape, dtype, name=name, align_bytes=64, offset=offset + 4 * KIB)
+            return shared.tile(shape, dtype, name=name, align_bytes=64, offset=offset)
 
-        kept_list = held.tile([P, I // 16], U16, name="kept_list")
-        evicted_list = held.tile([P, J // 16], U16, name="evicted_list")
+        def entries(listed, cols):
+            return listed[:, cols.start // LIST_ROWS : cols.stop // LIST_ROWS]
+
+        kept_list = held.tile([P, I // LIST_ROWS], U16, name="kept_list")
+        evicted_list = held.tile([P, J // LIST_ROWS], U16, name="evicted_list")
         ekey_word_pool = sbuf("ekey_word_pool", [P, T], U32)
         nc.sync.dma_start(ekey_word_pool[:].bitcast(I32), ekey_words[0].rearrange("p n t -> p (n t)").bitcast(I32))
         nc.sync.dma_start(evicted_list[:], offs2)
@@ -48,57 +69,60 @@ def tile_attend_softmerge_pl_kernel(tc, ekey_words, ekey_scales, keys_words, key
 
         ekey_byte_pool = sbuf("ekey_byte_pool", [P, T], U8)
         identity = sbuf("identity", [P, P], F32)
-        zeros_left = placed("zeros_left", [P, (14 * KIB + 64) // 4], F32, -4 * KIB)
+        zeros_left = placed("zeros_left", [P, (AT_LATE_LOADS + 64) // 4], F32, 0)
         nc.vector.memset(ekey_byte_pool[:].bitcast(I32), 0)
         nc.vector.memset(zeros_left[:, 0 : P // 2], 0.0)
         nc.gpsimd.affine_select(out=identity[:, 0 : P // 2], in_=zeros_left[:, 0 : P // 2], compare_op=ALU.not_equal, fill=1.0, base=0,
                                 pattern=[[-1, P // 2]], channel_multiplier=1)
-        for q in range(QUADS):
-            nc.scalar.dma_start(ekey_byte_pool[q:P:32, :].bitcast(I32), ekey_scales[0, q:16:4, :].bitcast(I32))
+        for r in range(PACK):
+            nc.scalar.dma_start(ekey_byte_pool[r:P:QUADRANT, :].bitcast(I32), ekey_scales[0, r:SCALE_ROWS:PACK, :].bitcast(I32))
 
         evals_rows = evals.rearrange("(p t) c -> p t c", t=PACK)
         vals_rows = vals.rearrange("(p t) c -> p t c", t=PACK)
-        evals_pool = [placed("evals_pool0", [P, T], F32, 0)]
-        nc.sync.dma_start(evals_pool[0][:], evals_rows[:, 0, :])
+        evals_pool = [placed("evals_pool0", [P, EARLY], F32, AT_FIRST_EVALS)]
+        nc.sync.dma_start(evals_pool[0][:], evals_rows[:, 0, 0:EARLY])
 
-        keys_byte_pool = placed("keys_byte_pool", [P, T], U8, 8 * KIB)
-        zeros_right = placed("zeros_right", [P, 65 * KIB // 4], F32, 10 * KIB)
+        keys_byte_pool = placed("keys_byte_pool", [P, T], U8, AT_KEYS_BYTES)
+        zeros_right = placed("zeros_right", [P, (AT_FAC + 3 * KIB - AT_LATE_LOADS) // 4], F32, AT_LATE_LOADS)
         nc.vector.memset(keys_byte_pool[:].bitcast(I32), 0)
         nc.vector.memset(zeros_right[:, 0 : P // 2], 0.0)
-        for q in range(QUADS):
-            (nc.sync, nc.gpsimd)[q // 2].dma_start(keys_byte_pool[KEPT_ROW + q : P : 32, :].bitcast(I32), keys_scales[0, q:16:4, :].bitcast(I32))
+        for r in range(PACK):
+            queue = (nc.sync, nc.gpsimd)[r // 2]
+            queue.dma_start(keys_byte_pool[KEYS_SCALE_ROW + r : P : QUADRANT, :].bitcast(I32), keys_scales[0, r:SCALE_ROWS:PACK, :].bitcast(I32))
         nc.gpsimd.affine_select(out=identity[:, P // 2 : P], in_=zeros_right[:, 0 : P // 2], compare_op=ALU.not_equal, fill=1.0, base=-(P // 2),
                                 pattern=[[-1, P // 2]], channel_multiplier=1)
-        keys_word_pool = placed("keys_word_pool", [P, T], U32, 10 * KIB)
+        keys_word_pool = placed("keys_word_pool", [P, T], U32, AT_LATE_LOADS)
         nc.sync.dma_start(keys_word_pool[:].bitcast(I32), keys_words[0].rearrange("p n t -> p (n t)").bitcast(I32))
-        fac_sb = placed("fac_sb", [P, PACK], F32, 74 * KIB)
+        evals_rest = placed("evals_rest", [P, T - EARLY], F32, AT_FAC + KIB)
+        nc.sync.dma_start(evals_rest[:], evals_rows[:, 0, EARLY:T])
+        fac_sb = placed("fac_sb", [P, PACK], F32, AT_FAC)
         nc.sync.dma_start(fac_sb[:], fac.rearrange("(p t) o -> p (t o)", t=PACK))
 
-        ekey_bytes = placed("ekey_bytes", [P, J], U8, -KIB)
-        ekey_codes = placed("ekey_codes", [P, J], U32, -4 * KIB)
-        ekey_scale = sbuf("ekey_scale", [P, J], U8)
+        ekey_bytes = placed("ekey_bytes", [P, J], U8, AT_EKEY_BYTES)
+        ekey_codes = placed("ekey_codes", [P, J], U32, AT_EKEY_CODES)
+        ekey_scale = placed("ekey_scale", [P, J], U8, AT_KEYS_BYTES + KIB)
         keys_scale = sbuf("keys_scale", [P, I], U8)
-        keys_codes = placed("keys_codes", [P, I], U32, 8 * KIB)
+        keys_codes = placed("keys_codes", [P, I], U32, AT_KEYS_BYTES - 3 * KIB // 2)
         nc.vector.tensor_copy(ekey_codes[:].rearrange("p (t s) -> p s t", t=PACK), ekey_word_pool[:].indirect(evicted_list[:]))
         nc.vector.tensor_copy(ekey_bytes[:], ekey_byte_pool[:].indirect(evicted_list[:]))
-        nc.vector.tensor_copy(ekey_scale[:].rearrange("p (t s) -> p t s", t=PACK), ekey_bytes[:].rearrange("p (s t) -> p t s", t=PACK))
         nc.vector.tensor_copy(keys_scale[:], keys_byte_pool[:].indirect(kept_list[:]))
+        nc.vector.tensor_copy(ekey_scale[:].rearrange("p (t s) -> p t s", t=PACK), ekey_bytes[:].rearrange("p (s t) -> p t s", t=PACK))
         halves = (slice(0, HALF), slice(HALF, I))
         for cols in halves:
-            nc.vector.tensor_copy(keys_codes[:, cols], keys_word_pool[:].indirect(kept_list[:, cols.start // 16 : cols.stop // 16]))
+            nc.vector.tensor_copy(keys_codes[:, cols], keys_word_pool[:].indirect(entries(kept_list, cols)))
 
         for t in range(1, PACK):
-            evals_pool.append(placed("evals_pool%d" % t, [P, T], F32, (10 + 8 * t) * KIB))
+            evals_pool.append(placed("evals_pool%d" % t, [P, T], F32, AT_LATE_LOADS + t * POOL_BYTES))
             nc.sync.dma_start(evals_pool[t][:], evals_rows[:, t, :])
         vals_pool = []
         for t in range(PACK):
-            vals_pool.append(placed("vals_pool%d" % t, [P, T], F32, (42 + 8 * t) * KIB))
+            vals_pool.append(placed("vals_pool%d" % t, [P, T], F32, AT_LATE_LOADS + (PACK + t) * POOL_BYTES))
             nc.sync.dma_start(vals_pool[t][:], vals_rows[:, t, :])
 
         vt_operand = {}
 
-        def gather_evals(t):
-            picked = placed("evals_picked%d" % t, [P, J], BF16, (-4, 96, 97)[t - 1] * KIB)
+        def gather_evals(t, offset):
+            picked = placed("evals_picked%d" % t, [P, J], BF16, offset)
             nc.vector.tensor_copy(picked[:], evals_pool[t][:].indirect(evicted_list[:]))
             return picked
 
@@ -107,15 +131,15 @@ def tile_attend_softmerge_pl_kernel(tc, ekey_words, ekey_scales, keys_words, key
             for u in range(2):
                 nc.tensor.transpose(turned[:, u, :], pairs[:, u : J // 2 : 2], identity[:])
 
-        def group_vt(first, turned, kib):
+        def group_vt(first, turned, offset):
             planes = turned.shape[1]
-            grouped = placed("vt_grouped%d" % first, [P, planes * P * PACK], BF16, kib * KIB)
+            grouped = placed("vt_grouped%d" % first, [P, planes * P * PACK], BF16, offset)
             nc.scalar.copy(grouped[:].bitcast(F32).rearrange("p (t e u) -> p t e u", t=planes, u=2), turned[:].rearrange("p t u e -> p t e u"))
             return grouped
 
-        def quantise_vt(first, grouped, kib):
+        def quantise_vt(first, grouped, offset):
             width = grouped.shape[1] // PACK
-            codes = placed("vt_codes%d" % first, [P, width], U32, kib * KIB)
+            codes = placed("vt_codes%d" % first, [P, width], U32, offset)
             scale = sbuf("vt_scale%d" % first, [P, width], U8)
             nc.vector.quantize_mx(codes[:].bitcast(FP8X4), scale[:], grouped[:])
             for n in range(width // P):
@@ -123,20 +147,21 @@ def tile_attend_softmerge_pl_kernel(tc, ekey_words, ekey_scales, keys_words, key
 
         evals_rounded = sbuf("evals_rounded", [P, T], BF16)
         picked_first = sbuf("evals_picked0", [P, J], BF16)
-        nc.scalar.activation(evals_rounded[:], evals_pool[0][:], ACT.Copy)
+        nc.scalar.activation(evals_rounded[:, 0:EARLY], evals_pool[0][:], ACT.Copy)
+        nc.scalar.activation(evals_rounded[:, EARLY:T], evals_rest[:], ACT.Copy)
         nc.scalar.activation(picked_first[:], evals_rounded[:].indirect(evicted_list[:]), ACT.Copy)
 
         neg_max = sbuf("neg_max", [P, PACK], F32)
         sum_low = sbuf("sum_low", [P, 2], F32)
         sum_high = sbuf("sum_high", [P, 2], F32)
-        prob = [placed("prob%d" % t, [P, I], F32, (92 + 2 * t) * KIB) for t in range(PACK)]
-        w_rows = placed("w_rows", [P, PACK, I], BF16, 86 * KIB)
+        prob = [placed("prob%d" % t, [P, I], F32, AT_PROB + t * 4 * I) for t in range(PACK)]
+        w_rows = placed("w_rows", [P, PACK, I], BF16, AT_W_ROWS)
         for t in range(PACK):
             rows = slice(t * P, (t + 1) * P)
             score = psum.tile([P, I], F32, name="score", tag="product")
             for cols in halves if t == 0 else (slice(0, I),):
                 nc.tensor.matmul_mx(score[:, cols], lhsT=ekey_codes[:, rows].bitcast(FP8X4), lhsT_scale=ekey_scale[:, rows],
-                                    rhs=keys_codes[:, cols].bitcast(FP8X4), rhs_scale=keys_scale[KEPT_ROW:P, cols], start=True, stop=True)
+                                    rhs=keys_codes[:, cols].bitcast(FP8X4), rhs_scale=keys_scale[KEYS_SCALE_ROW:P, cols], start=True, stop=True)
             nc.vector.tensor_reduce(neg_max[:, t : t + 1], score[:], AXIS.X, ALU.max, negate=True)
             nc.scalar.activation(prob[t][:], score[:], ACT.Exp, bias=neg_max[:, t : t + 1], accum_out=(sum_low, sum_high)[t // 2][:, t % 2 : t % 2 + 1])
         turned_first = psum.tile([P, 1, 2, P], F32, name="turned_first", tag="product")
@@ -147,28 +172,29 @@ def tile_attend_softmerge_pl_kernel(tc, ekey_words, ekey_scales, keys_words, key
         inv_high = sbuf("inv_high", [P, 2], F32)
         factor = sbuf("factor", [P, 2], F32)
         nc.vector.reciprocal(inv_low[:], sum_low[:])
-        grouped_first = group_vt(0, turned_first, 85)
-        turn(gather_evals(1), turned_middle[:, 0])
+        grouped_first = group_vt(0, turned_first, AT_FIRST_VT)
+        turn(gather_evals(1, AT_EKEY_CODES), turned_middle[:, 0])
         nc.vector.reciprocal(inv_high[:], sum_high[:])
         nc.vector.tensor_tensor(factor[:], inv_low[:], fac_sb[:, 0:2], ALU.mult)
         for t in (0, 1):
             nc.scalar.activation(w_rows[:, t, :], prob[t][:], ACT.Copy, scale=factor[:, t : t + 1])
         for t in (2, 3):
             nc.vector.tensor_scalar(w_rows[:, t, :], prob[t][:], inv_high[:, t - 2 : t - 1], fac_sb[:, t : t + 1], ALU.mult, ALU.mult)
-        w_grouped = placed("w_grouped", [P, I, PACK], BF16, 80 * KIB)
-        nc.scalar.copy(w_grouped[:].rearrange("p (c i) t -> p c t i", i=4), w_rows[:].rearrange("p t (c i) -> p c t i", i=4))
-        turn(gather_evals(2), turned_middle[:, 1])
-        turn(gather_evals(3), turned_last[:, 0])
-        grouped_middle = group_vt(1, turned_middle, 86)
-        grouped_last = group_vt(3, turned_last, 88)
-        quantise_vt(0, grouped_first, 90)
-        w_codes = placed("w_codes", [P, I], U32, 34 * KIB)
+        w_grouped = placed("w_grouped", [P, I, PACK], BF16, AT_W_GROUPED)
+        nc.scalar.copy(w_grouped[:].rearrange("p (c i) t -> p c t i", i=RUN), w_rows[:].rearrange("p t (c i) -> p c t i", i=RUN))
+        at_scaled = AT_PROB + 2 * 4 * I
+        turn(gather_evals(2, at_scaled), turned_middle[:, 1])
+        turn(gather_evals(3, at_scaled + 2 * J), turned_last[:, 0])
+        grouped_middle = group_vt(1, turned_middle, AT_W_ROWS)
+        grouped_last = group_vt(3, turned_last, AT_W_ROWS + 2 * KIB)
+        quantise_vt(0, grouped_first, AT_FIRST_VT_CODES)
+        w_codes = placed("w_codes", [P, I], U32, AT_LAST_EVALS)
         w_scale = sbuf("w_scale", [P, I], U8)
         nc.vector.quantize_mx(w_codes[:].bitcast(FP8X4), w_scale[:], w_grouped[:].rearrange("p i t -> p (i t)"))
-        quantise_vt(1, grouped_middle, 36)
-        kept = placed("kept", [P, I], F32, 80 * KIB)
+        quantise_vt(1, grouped_middle, AT_LAST_EVALS + 2 * KIB)
+        kept = placed("kept", [P, I], F32, AT_W_GROUPED)
         nc.vector.tensor_copy(kept[:], vals_pool[0][:].indirect(kept_list[:]))
-        quantise_vt(3, grouped_last, 38)
+        quantise_vt(3, grouped_last, AT_LAST_EVALS + 4 * KIB)
 
         merged = []
         for t in range(PACK):
@@ -186,26 +212,24 @@ def tile_attend_softmerge_pl_kernel(tc, ekey_words, ekey_scales, keys_words, key
         y_codes = sbuf("y_codes", [P, I], U32)
         y_scale = sbuf("y_scale", [P, I], U8)
         last = PACK - 1
-        for t in range(last):
-            y_t = (y_low, y_high)[t // 2][:, t % 2, :]
-            if t == 0:
-                nc.vector.tensor_tensor(y_t, merged[0][:], kept[:], ALU.add)
-            else:
-                nc.vector.tensor_tensor(y_t, vals_pool[t][:].indirect(kept_list[:]), merged_sb[:, t, :], ALU.add)
-            nc.sync.dma_start(out_rows[:, t, :], y_t)
-            if t == 1:
-                nc.scalar.copy(y_grouped[:, :, 0:2], y_low[:].rearrange("p t i -> p i t"))
+        nc.vector.tensor_tensor(y_low[:, 0, :], merged[0][:], kept[:], ALU.add)
+        nc.sync.dma_start(out_rows[:, 0, :], y_low[:, 0, :])
+        nc.vector.tensor_tensor(y_low[:, 1, :], vals_pool[1][:].indirect(kept_list[:]), merged_sb[:, 1, :], ALU.add)
+        nc.sync.dma_start(out_rows[:, 1, :], y_low[:, 1, :])
+        nc.scalar.copy(y_grouped[:, :, 0:2], y_low[:].rearrange("p t i -> p i t"))
+        nc.vector.tensor_tensor(y_high[:, 0, :], vals_pool[2][:].indirect(kept_list[:]), merged_sb[:, 2, :], ALU.add)
+        nc.sync.dma_start(out_rows[:, 2, :], y_high[:, 0, :])
         words_out = out_1[0].rearrange("p n t -> p (n t)").bitcast(I32)
         for piece in range(PIECES):
             cols = slice(piece * PIECE, (piece + 1) * PIECE)
-            nc.vector.tensor_tensor(y_high[:, 1, cols], vals_pool[last][:].indirect(kept_list[:, piece * PIECE // 16 : (piece + 1) * PIECE // 16]),
-                                    merged_sb[:, last, cols], ALU.add)
-            (nc.scalar.copy if piece < PIECES - 1 else nc.vector.tensor_copy)(y_grouped[:, cols, 2:4], y_high[:, :, cols].rearrange("p t i -> p i t"))
+            nc.vector.tensor_tensor(y_high[:, 1, cols], vals_pool[last][:].indirect(entries(kept_list, cols)), merged_sb[:, last, cols], ALU.add)
+            interleave = nc.scalar.copy if piece < PIECES - 1 else nc.vector.tensor_copy
+            interleave(y_grouped[:, cols, 2:4], y_high[:, :, cols].rearrange("p t i -> p i t"))
         nc.sync.dma_start(out_rows[:, last, :], y_high[:, 1, :])
         for cols in halves:
             nc.vector.quantize_mx(y_codes[:, cols].bitcast(FP8X4), y_scale[:, cols], y_grouped[:, cols, :].rearrange("p i t -> p (i t)"))
-            if cols.stop % HALF == 0:
-                nc.sync.dma_start(words_out[:, cols.stop - HALF : cols.stop], y_codes[:, cols.stop - HALF : cols.stop].bitcast(I32))
-        for q in range(QUADS):
-            queue = (nc.sync, nc.scalar)[q % 2]
-            queue.dma_start(out_2[0, 4 * q : 4 * q + 4, :].bitcast(I32), y_scale[32 * q : 32 * q + 4, :].bitcast(I32))
+            nc.sync.dma_start(words_out[:, cols], y_codes[:, cols].bitcast(I32))
+        for quadrant in range(P // QUADRANT):
+            queue = (nc.sync, nc.scalar)[quadrant % 2]
+            queue.dma_start(out_2[0, PACK * quadrant : PACK * quadrant + PACK, :].bitcast(I32),
+                            y_scale[QUADRANT * quadrant : QUADRANT * quadrant + PACK, :].bitcast(I32))

@@ -23,25 +23,20 @@ SCALE_ROWS = 16
 LIST_ROWS = 16
 KEYS_SCALE_ROW = 4
 HALF = I // 2
-EARLY = 3 * T // 4
-PIECES = 4
-PIECE = I // PIECES
 RUN = 4
-
 KIB = 1024
 POOL_BYTES = 4 * T
+
 AT_EKEY_CODES = 0
-AT_EKEY_BYTES = 3 * KIB
-AT_FIRST_EVALS = 4 * KIB
-AT_KEYS_BYTES = AT_FIRST_EVALS + POOL_BYTES
+AT_EKEY_SCALE = 2 * KIB
+AT_KEYS_WORDS = 3 * KIB
+AT_KEYS_BYTES = AT_KEYS_WORDS + POOL_BYTES
 AT_LATE_LOADS = AT_KEYS_BYTES + T
-AT_LAST_EVALS = AT_LATE_LOADS + (PACK - 1) * POOL_BYTES
 AT_FAC = AT_LATE_LOADS + 2 * PACK * POOL_BYTES
-AT_W_GROUPED = 84 * KIB
-AT_FIRST_VT = 89 * KIB
-AT_W_ROWS = 90 * KIB
-AT_FIRST_VT_CODES = 94 * KIB
-AT_PROB = 96 * KIB
+AT_LAST_EVALS = AT_LATE_LOADS + (PACK - 1) * POOL_BYTES
+AT_NEG_MAX = 80 * KIB
+AT_W_ROWS = 83 * KIB
+AT_LAST_VT = 87 * KIB
 
 
 def tile_attend_softmerge_pl_kernel(tc, ekey_words, ekey_scales, keys_words, keys_scales, fac, evals, vals, offs, offs2, out_0, out_1, out_2):
@@ -69,92 +64,54 @@ def tile_attend_softmerge_pl_kernel(tc, ekey_words, ekey_scales, keys_words, key
 
         ekey_byte_pool = sbuf("ekey_byte_pool", [P, T], U8)
         identity = sbuf("identity", [P, P], F32)
-        zeros_left = placed("zeros_left", [P, (AT_LATE_LOADS + 64) // 4], F32, 0)
+        offset = placed("offset", [P, AT_LATE_LOADS // 4], F32, 0)
+        distance = placed("distance", [P, (AT_FAC + 64 - AT_LATE_LOADS) // 4], F32, AT_LATE_LOADS)
         nc.vector.memset(ekey_byte_pool[:].bitcast(I32), 0)
-        nc.vector.memset(zeros_left[:, 0 : P // 2], 0.0)
-        nc.gpsimd.affine_select(out=identity[:, 0 : P // 2], in_=zeros_left[:, 0 : P // 2], compare_op=ALU.not_equal, fill=1.0, base=0,
-                                pattern=[[-1, P // 2]], channel_multiplier=1)
+        nc.gpsimd.iota(offset[:, 0:P], pattern=[[-1, P]], base=0, channel_multiplier=1, allow_small_or_imprecise_dtypes=True)
+        nc.scalar.activation(distance[:, 0:P], offset[:, 0:P], ACT.Abs)
         for r in range(PACK):
-            nc.scalar.dma_start(ekey_byte_pool[r:P:QUADRANT, :].bitcast(I32), ekey_scales[0, r:SCALE_ROWS:PACK, :].bitcast(I32))
+            nc.sync.dma_start(ekey_byte_pool[r:P:QUADRANT, :].bitcast(I32), ekey_scales[0, r:SCALE_ROWS:PACK, :].bitcast(I32))
+
+        keys_word_pool = placed("keys_word_pool", [P, T], U32, AT_KEYS_WORDS)
+        nc.sync.dma_start(keys_word_pool[:].bitcast(I32), keys_words[0].rearrange("p n t -> p (n t)").bitcast(I32))
+        keys_byte_pool = placed("keys_byte_pool", [P, T], U8, AT_KEYS_BYTES)
+        one = placed("one", [P, 1], F32, AT_KEYS_WORDS - 64)
+        nc.vector.memset(keys_byte_pool[:].bitcast(I32), 0)
+        nc.vector.memset(one[:], 1.0)
+        for r in range(PACK):
+            nc.sync.dma_start(keys_byte_pool[KEYS_SCALE_ROW + r : P : QUADRANT, :].bitcast(I32), keys_scales[0, r:SCALE_ROWS:PACK, :].bitcast(I32))
+        nc.scalar.activation(identity[:], distance[:, 0:P], ACT.Relu, bias=one[:], scale=-1.0)
 
         evals_rows = evals.rearrange("(p t) c -> p t c", t=PACK)
         vals_rows = vals.rearrange("(p t) c -> p t c", t=PACK)
-        evals_pool = [placed("evals_pool0", [P, EARLY], F32, AT_FIRST_EVALS)]
-        nc.sync.dma_start(evals_pool[0][:], evals_rows[:, 0, 0:EARLY])
-
-        keys_byte_pool = placed("keys_byte_pool", [P, T], U8, AT_KEYS_BYTES)
-        zeros_right = placed("zeros_right", [P, (AT_FAC + 3 * KIB - AT_LATE_LOADS) // 4], F32, AT_LATE_LOADS)
-        nc.vector.memset(keys_byte_pool[:].bitcast(I32), 0)
-        nc.vector.memset(zeros_right[:, 0 : P // 2], 0.0)
-        for r in range(PACK):
-            queue = (nc.sync, nc.gpsimd)[r // 2]
-            queue.dma_start(keys_byte_pool[KEYS_SCALE_ROW + r : P : QUADRANT, :].bitcast(I32), keys_scales[0, r:SCALE_ROWS:PACK, :].bitcast(I32))
-        nc.gpsimd.affine_select(out=identity[:, P // 2 : P], in_=zeros_right[:, 0 : P // 2], compare_op=ALU.not_equal, fill=1.0, base=-(P // 2),
-                                pattern=[[-1, P // 2]], channel_multiplier=1)
-        keys_word_pool = placed("keys_word_pool", [P, T], U32, AT_LATE_LOADS)
-        nc.sync.dma_start(keys_word_pool[:].bitcast(I32), keys_words[0].rearrange("p n t -> p (n t)").bitcast(I32))
-        evals_rest = placed("evals_rest", [P, T - EARLY], F32, AT_FAC + KIB)
-        nc.sync.dma_start(evals_rest[:], evals_rows[:, 0, EARLY:T])
+        evals_pool, vals_pool = [], []
         fac_sb = placed("fac_sb", [P, PACK], F32, AT_FAC)
-        nc.sync.dma_start(fac_sb[:], fac.rearrange("(p t) o -> p (t o)", t=PACK))
-
-        ekey_bytes = placed("ekey_bytes", [P, J], U8, AT_EKEY_BYTES)
-        ekey_codes = placed("ekey_codes", [P, J], U32, AT_EKEY_CODES)
-        ekey_scale = placed("ekey_scale", [P, J], U8, AT_KEYS_BYTES + KIB)
-        keys_scale = sbuf("keys_scale", [P, I], U8)
-        keys_codes = placed("keys_codes", [P, I], U32, AT_KEYS_BYTES - 3 * KIB // 2)
-        nc.vector.tensor_copy(ekey_codes[:].rearrange("p (t s) -> p s t", t=PACK), ekey_word_pool[:].indirect(evicted_list[:]))
-        nc.vector.tensor_copy(ekey_bytes[:], ekey_byte_pool[:].indirect(evicted_list[:]))
-        nc.vector.tensor_copy(keys_scale[:], keys_byte_pool[:].indirect(kept_list[:]))
-        nc.vector.tensor_copy(ekey_scale[:].rearrange("p (t s) -> p t s", t=PACK), ekey_bytes[:].rearrange("p (s t) -> p t s", t=PACK))
-        halves = (slice(0, HALF), slice(HALF, I))
-        for cols in halves:
-            nc.vector.tensor_copy(keys_codes[:, cols], keys_word_pool[:].indirect(entries(kept_list, cols)))
-
-        for t in range(1, PACK):
+        for t in range(PACK):
             evals_pool.append(placed("evals_pool%d" % t, [P, T], F32, AT_LATE_LOADS + t * POOL_BYTES))
             nc.sync.dma_start(evals_pool[t][:], evals_rows[:, t, :])
-        vals_pool = []
+            if t == 0:
+                nc.sync.dma_start(fac_sb[:], fac.rearrange("(p t) o -> p (t o)", t=PACK))
         for t in range(PACK):
             vals_pool.append(placed("vals_pool%d" % t, [P, T], F32, AT_LATE_LOADS + (PACK + t) * POOL_BYTES))
             nc.sync.dma_start(vals_pool[t][:], vals_rows[:, t, :])
 
-        vt_operand = {}
+        ekey_codes = placed("ekey_codes", [P, J], U32, AT_EKEY_CODES)
+        ekey_scale = placed("ekey_scale", [P, J], U8, AT_EKEY_SCALE)
+        keys_scale = sbuf("keys_scale", [P, I], U8)
+        keys_codes = sbuf("keys_codes", [P, I], U32)
+        nc.vector.tensor_copy(ekey_codes[:].rearrange("p (t s) -> p s t", t=PACK), ekey_word_pool[:].indirect(evicted_list[:]))
+        nc.vector.tensor_copy(ekey_scale[:].rearrange("p (t s) -> p s t", t=PACK), ekey_byte_pool[:].indirect(evicted_list[:]))
+        nc.vector.tensor_copy(keys_codes[:], keys_word_pool[:].indirect(kept_list[:]))
+        halves = (slice(0, HALF), slice(HALF, I))
+        for cols in halves:
+            nc.vector.tensor_copy(keys_scale[:, cols], keys_byte_pool[:].indirect(entries(kept_list, cols)))
 
-        def gather_evals(t, offset):
-            picked = placed("evals_picked%d" % t, [P, J], BF16, offset)
-            nc.vector.tensor_copy(picked[:], evals_pool[t][:].indirect(evicted_list[:]))
-            return picked
-
-        def turn(picked, turned):
-            pairs = picked[:].bitcast(F32)
-            for u in range(2):
-                nc.tensor.transpose(turned[:, u, :], pairs[:, u : J // 2 : 2], identity[:])
-
-        def group_vt(first, turned, offset):
-            planes = turned.shape[1]
-            grouped = placed("vt_grouped%d" % first, [P, planes * P * PACK], BF16, offset)
-            nc.scalar.copy(grouped[:].bitcast(F32).rearrange("p (t e u) -> p t e u", t=planes, u=2), turned[:].rearrange("p t u e -> p t e u"))
-            return grouped
-
-        def quantise_vt(first, grouped, offset):
-            width = grouped.shape[1] // PACK
-            codes = placed("vt_codes%d" % first, [P, width], U32, offset)
-            scale = sbuf("vt_scale%d" % first, [P, width], U8)
-            nc.vector.quantize_mx(codes[:].bitcast(FP8X4), scale[:], grouped[:])
-            for n in range(width // P):
-                vt_operand[first + n] = (codes[:, n * P : (n + 1) * P], scale[:, n * P : (n + 1) * P])
-
-        evals_rounded = sbuf("evals_rounded", [P, T], BF16)
-        picked_first = sbuf("evals_picked0", [P, J], BF16)
-        nc.scalar.activation(evals_rounded[:, 0:EARLY], evals_pool[0][:], ACT.Copy)
-        nc.scalar.activation(evals_rounded[:, EARLY:T], evals_rest[:], ACT.Copy)
-        nc.scalar.activation(picked_first[:], evals_rounded[:].indirect(evicted_list[:]), ACT.Copy)
-
-        neg_max = sbuf("neg_max", [P, PACK], F32)
-        sum_low = sbuf("sum_low", [P, 2], F32)
-        sum_high = sbuf("sum_high", [P, 2], F32)
-        prob = [placed("prob%d" % t, [P, I], F32, AT_PROB + t * 4 * I) for t in range(PACK)]
+        first_picked = sbuf("first_picked", [P, J], BF16)
+        nc.scalar.activation(first_picked[:], evals_pool[0][:].indirect(evicted_list[:]), ACT.Copy)
+        neg_max = placed("neg_max", [P, PACK], F32, AT_NEG_MAX)
+        sums = [sbuf("sum%d" % h, [P, 2], F32) for h in range(2)]
+        invs = [sbuf("inv%d" % h, [P, 2], F32) for h in range(2)]
+        prob = [placed("prob%d" % t, [P, I], F32, AT_LATE_LOADS + t * 4 * I) for t in range(PACK)]
         w_rows = placed("w_rows", [P, PACK, I], BF16, AT_W_ROWS)
         for t in range(PACK):
             rows = slice(t * P, (t + 1) * P)
@@ -163,70 +120,79 @@ def tile_attend_softmerge_pl_kernel(tc, ekey_words, ekey_scales, keys_words, key
                 nc.tensor.matmul_mx(score[:, cols], lhsT=ekey_codes[:, rows].bitcast(FP8X4), lhsT_scale=ekey_scale[:, rows],
                                     rhs=keys_codes[:, cols].bitcast(FP8X4), rhs_scale=keys_scale[KEYS_SCALE_ROW:P, cols], start=True, stop=True)
             nc.vector.tensor_reduce(neg_max[:, t : t + 1], score[:], AXIS.X, ALU.max, negate=True)
-            nc.scalar.activation(prob[t][:], score[:], ACT.Exp, bias=neg_max[:, t : t + 1], accum_out=(sum_low, sum_high)[t // 2][:, t % 2 : t % 2 + 1])
-        turned_first = psum.tile([P, 1, 2, P], F32, name="turned_first", tag="product")
-        turned_middle = psum.tile([P, 2, 2, P], F32, name="turned_middle", tag="turned")
-        turned_last = psum.tile([P, 1, 2, P], F32, name="turned_last", tag="turned")
-        turn(picked_first, turned_first[:, 0])
-        inv_low = sbuf("inv_low", [P, 2], F32)
-        inv_high = sbuf("inv_high", [P, 2], F32)
-        factor = sbuf("factor", [P, 2], F32)
-        nc.vector.reciprocal(inv_low[:], sum_low[:])
-        grouped_first = group_vt(0, turned_first, AT_FIRST_VT)
-        turn(gather_evals(1, AT_EKEY_CODES), turned_middle[:, 0])
-        nc.vector.reciprocal(inv_high[:], sum_high[:])
-        nc.vector.tensor_tensor(factor[:], inv_low[:], fac_sb[:, 0:2], ALU.mult)
-        for t in (0, 1):
-            nc.scalar.activation(w_rows[:, t, :], prob[t][:], ACT.Copy, scale=factor[:, t : t + 1])
-        for t in (2, 3):
-            nc.vector.tensor_scalar(w_rows[:, t, :], prob[t][:], inv_high[:, t - 2 : t - 1], fac_sb[:, t : t + 1], ALU.mult, ALU.mult)
-        w_grouped = placed("w_grouped", [P, I, PACK], BF16, AT_W_GROUPED)
-        nc.scalar.copy(w_grouped[:].rearrange("p (c i) t -> p c t i", i=RUN), w_rows[:].rearrange("p t (c i) -> p c t i", i=RUN))
-        at_scaled = AT_PROB + 2 * 4 * I
-        turn(gather_evals(2, at_scaled), turned_middle[:, 1])
-        turn(gather_evals(3, at_scaled + 2 * J), turned_last[:, 0])
-        grouped_middle = group_vt(1, turned_middle, AT_W_ROWS)
-        grouped_last = group_vt(3, turned_last, AT_W_ROWS + 2 * KIB)
-        quantise_vt(0, grouped_first, AT_FIRST_VT_CODES)
-        w_codes = placed("w_codes", [P, I], U32, AT_LAST_EVALS)
+            nc.scalar.activation(prob[t][:], score[:], ACT.Exp, bias=neg_max[:, t : t + 1], accum_out=sums[t // 2][:, t % 2 : t % 2 + 1])
+        for h in range(2):
+            nc.vector.reciprocal(invs[h][:], sums[h][:])
+            for t in (2 * h, 2 * h + 1):
+                nc.vector.tensor_scalar(w_rows[:, t, :], prob[t][:], invs[h][:, t % 2 : t % 2 + 1], fac_sb[:, t : t + 1], ALU.mult, ALU.mult)
+        w_grouped = sbuf("w_grouped", [P, I, PACK], BF16)
+        w_codes = sbuf("w_codes", [P, I], U32)
         w_scale = sbuf("w_scale", [P, I], U8)
-        nc.vector.quantize_mx(w_codes[:].bitcast(FP8X4), w_scale[:], w_grouped[:].rearrange("p i t -> p (i t)"))
-        quantise_vt(1, grouped_middle, AT_LAST_EVALS + 2 * KIB)
-        kept = placed("kept", [P, I], F32, AT_W_GROUPED)
-        nc.vector.tensor_copy(kept[:], vals_pool[0][:].indirect(kept_list[:]))
-        quantise_vt(3, grouped_last, AT_LAST_EVALS + 4 * KIB)
+        for cols in halves:
+            nc.vector.tensor_copy(w_grouped[:, cols, :].rearrange("p (c i) t -> p c t i", i=RUN), w_rows[:, :, cols].rearrange("p t (c i) -> p c t i", i=RUN))
+        for cols in halves:
+            nc.vector.quantize_mx(w_codes[:, cols].bitcast(FP8X4), w_scale[:, cols], w_grouped[:, cols, :].rearrange("p i t -> p (i t)"))
 
         merged = []
-        for t in range(PACK):
-            merged.append(psum.tile([P, I], F32, name="merged", tag="product"))
-            nc.tensor.matmul_mx(merged[t][:], lhsT=vt_operand[t][0].bitcast(FP8X4), lhsT_scale=vt_operand[t][1],
-                                rhs=w_codes[:].bitcast(FP8X4), rhs_scale=w_scale[:], start=True, stop=True)
-        merged_sb = sbuf("merged_sb", [P, PACK, I], F32)
+        merged_sb = placed("merged_sb", [P, PACK, I], F32, AT_LAST_EVALS + POOL_BYTES)
+        last = PACK - 1
+        late_picked = placed("late_picked", [P, 3 * J], BF16, AT_NEG_MAX)
+        turned_pairs = []
+        for h in range(2):
+            turned_pairs.append(psum.tile([P, 2, 2, P], F32, name="turned", tag="turned"))
+            for n in range(2):
+                t = 2 * h + n
+                if t == 0:
+                    picked = first_picked[:]
+                else:
+                    picked = late_picked[:, (t - 1) * J : t * J]
+                    nc.scalar.activation(picked, evals_pool[t][:].indirect(evicted_list[:]), ACT.Copy)
+                pairs = picked.bitcast(F32)
+                for u in range(2):
+                    nc.tensor.transpose(turned_pairs[h][:, n, u, :], pairs[:, u : J // 2 : 2], identity[:])
+        for h in range(2):
+            turned = turned_pairs[h]
+            grouped = placed("vt_grouped%d" % h, [P, 2 * P * PACK], BF16, (AT_W_ROWS, AT_LAST_VT)[h])
+            nc.vector.tensor_copy(grouped[:].bitcast(F32).rearrange("p (t e u) -> p t e u", t=2, u=2), turned[:].rearrange("p t u e -> p t e u"))
+            codes = placed("vt_codes%d" % h, [P, 2 * P], U32, (AT_NEG_MAX, AT_LAST_VT + 4 * KIB)[h])
+            scale = sbuf("vt_scale%d" % h, [P, 2 * P], U8)
+            nc.vector.quantize_mx(codes[:].bitcast(FP8X4), scale[:], grouped[:])
+            for n in range(2):
+                t = 2 * h + n
+                merged.append(psum.tile([P, I], F32, name="merged", tag="product"))
+                nc.tensor.matmul_mx(merged[t][:], lhsT=codes[:, n * P : (n + 1) * P].bitcast(FP8X4), lhsT_scale=scale[:, n * P : (n + 1) * P],
+                                    rhs=w_codes[:].bitcast(FP8X4), rhs_scale=w_scale[:], start=True, stop=True)
+        kept_first = sbuf("kept_first", [P, I], F32)
+        nc.scalar.activation(kept_first[:], vals_pool[0][:].indirect(kept_list[:]), ACT.Copy)
         for t in range(1, PACK):
-            nc.scalar.copy(merged_sb[:, t, :], merged[t][:])
+            cols = slice(0, I) if t < last else halves[0]
+            nc.scalar.copy(merged_sb[:, t, cols], merged[t][:, cols])
 
         out_rows = out_0.rearrange("(p t) i -> p t i", t=PACK)
-        y_low = sbuf("y_low", [P, 2, I], F32)
+        y_low = placed("y_low", [P, 2, I], F32, AT_LAST_VT)
         y_high = sbuf("y_high", [P, 2, I], F32)
         y_grouped = sbuf("y_grouped", [P, I, PACK], BF16)
         y_codes = sbuf("y_codes", [P, I], U32)
         y_scale = sbuf("y_scale", [P, I], U8)
-        last = PACK - 1
-        nc.vector.tensor_tensor(y_low[:, 0, :], merged[0][:], kept[:], ALU.add)
-        nc.sync.dma_start(out_rows[:, 0, :], y_low[:, 0, :])
-        nc.vector.tensor_tensor(y_low[:, 1, :], vals_pool[1][:].indirect(kept_list[:]), merged_sb[:, 1, :], ALU.add)
-        nc.sync.dma_start(out_rows[:, 1, :], y_low[:, 1, :])
-        nc.scalar.copy(y_grouped[:, :, 0:2], y_low[:].rearrange("p t i -> p i t"))
-        nc.vector.tensor_tensor(y_high[:, 0, :], vals_pool[2][:].indirect(kept_list[:]), merged_sb[:, 2, :], ALU.add)
-        nc.sync.dma_start(out_rows[:, 2, :], y_high[:, 0, :])
+        for t in range(last):
+            y = (y_low, y_high)[t // 2][:, t % 2, :]
+            if t == 0:
+                nc.vector.tensor_tensor(y, merged[t][:], kept_first[:], ALU.add)
+            else:
+                nc.vector.tensor_tensor(y, vals_pool[t][:].indirect(kept_list[:]), merged_sb[:, t, :], ALU.add)
+            nc.sync.dma_start(out_rows[:, t, :], y)
+            if t == 1:
+                nc.scalar.copy(y_grouped[:, :, 0:2], y_low[:].rearrange("p t i -> p i t"))
         words_out = out_1[0].rearrange("p n t -> p (n t)").bitcast(I32)
-        for piece in range(PIECES):
-            cols = slice(piece * PIECE, (piece + 1) * PIECE)
-            nc.vector.tensor_tensor(y_high[:, 1, cols], vals_pool[last][:].indirect(entries(kept_list, cols)), merged_sb[:, last, cols], ALU.add)
-            interleave = nc.scalar.copy if piece < PIECES - 1 else nc.vector.tensor_copy
-            interleave(y_grouped[:, cols, 2:4], y_high[:, :, cols].rearrange("p t i -> p i t"))
+        kept = sbuf("kept", [P, HALF], F32)
+        low, high = halves
+        nc.vector.tensor_tensor(y_high[:, 1, low], vals_pool[last][:].indirect(entries(kept_list, low)), merged_sb[:, last, low], ALU.add)
+        nc.scalar.activation(kept[:], vals_pool[last][:].indirect(entries(kept_list, high)), ACT.Copy)
+        nc.vector.tensor_tensor(y_high[:, 1, high], merged[last][:, high], kept[:], ALU.add)
         nc.sync.dma_start(out_rows[:, last, :], y_high[:, 1, :])
-        for cols in halves:
+        nc.scalar.copy(y_grouped[:, low, 2:4], y_high[:, :, low].rearrange("p t i -> p i t"))
+        nc.vector.tensor_copy(y_grouped[:, high, 2:4], y_high[:, :, high].rearrange("p t i -> p i t"))
+        for cols in (high, low):
             nc.vector.quantize_mx(y_codes[:, cols].bitcast(FP8X4), y_scale[:, cols], y_grouped[:, cols, :].rearrange("p i t -> p (i t)"))
             nc.sync.dma_start(words_out[:, cols], y_codes[:, cols].bitcast(I32))
         for quadrant in range(P // QUADRANT):

@@ -21,22 +21,21 @@ PACK = 4
 QUADRANT = 32
 SCALE_ROWS = 16
 LIST_ROWS = 16
-KEYS_SCALE_ROW = 4
 HALF = I // 2
 RUN = 4
+SCALAR_SHARE = 192
 KIB = 1024
 POOL_BYTES = 4 * T
 
-AT_EKEY_CODES = 0
-AT_EKEY_SCALE = 2 * KIB
-AT_KEYS_WORDS = 3 * KIB
-AT_KEYS_BYTES = AT_KEYS_WORDS + POOL_BYTES
-AT_LATE_LOADS = AT_KEYS_BYTES + T
-AT_FAC = AT_LATE_LOADS + 2 * PACK * POOL_BYTES
-AT_LAST_EVALS = AT_LATE_LOADS + (PACK - 1) * POOL_BYTES
-AT_NEG_MAX = 80 * KIB
-AT_W_ROWS = 83 * KIB
-AT_LAST_VT = 87 * KIB
+EDGE = 64
+AT_EVALS = (0, POOL_BYTES, 2 * POOL_BYTES, 4 * POOL_BYTES - 2 * EDGE)
+AT_EKEY_WORDS = 3 * POOL_BYTES - EDGE
+AT_VALS = (5 * POOL_BYTES, 7 * POOL_BYTES - 2 * EDGE, 8 * POOL_BYTES, 9 * POOL_BYTES + 4 * I - 2 * EDGE)
+AT_KEYS_WORDS = 6 * POOL_BYTES - EDGE
+AT_KEYS_CODES = 9 * POOL_BYTES - EDGE
+ROW_STEP = P // SCALE_ROWS
+AT_NEG_MAX = 90 * KIB
+AT_W_ROWS = 93 * KIB
 
 
 def tile_attend_softmerge_pl_kernel(tc, ekey_words, ekey_scales, keys_words, keys_scales, fac, evals, vals, offs, offs2, out_0, out_1, out_2):
@@ -57,70 +56,75 @@ def tile_attend_softmerge_pl_kernel(tc, ekey_words, ekey_scales, keys_words, key
 
         kept_list = held.tile([P, I // LIST_ROWS], U16, name="kept_list")
         evicted_list = held.tile([P, J // LIST_ROWS], U16, name="evicted_list")
-        ekey_word_pool = sbuf("ekey_word_pool", [P, T], U32)
-        nc.sync.dma_start(ekey_word_pool[:].bitcast(I32), ekey_words[0].rearrange("p n t -> p (n t)").bitcast(I32))
         nc.sync.dma_start(evicted_list[:], offs2)
         nc.sync.dma_start(kept_list[:], offs)
-
-        ekey_byte_pool = sbuf("ekey_byte_pool", [P, T], U8)
-        identity = sbuf("identity", [P, P], F32)
-        offset = placed("offset", [P, AT_LATE_LOADS // 4], F32, 0)
-        distance = placed("distance", [P, (AT_FAC + 64 - AT_LATE_LOADS) // 4], F32, AT_LATE_LOADS)
-        nc.vector.memset(ekey_byte_pool[:].bitcast(I32), 0)
-        nc.gpsimd.iota(offset[:, 0:P], pattern=[[-1, P]], base=0, channel_multiplier=1, allow_small_or_imprecise_dtypes=True)
-        nc.scalar.activation(distance[:, 0:P], offset[:, 0:P], ACT.Abs)
-        for r in range(PACK):
-            nc.sync.dma_start(ekey_byte_pool[r:P:QUADRANT, :].bitcast(I32), ekey_scales[0, r:SCALE_ROWS:PACK, :].bitcast(I32))
-
+        ekey_word_pool = placed("ekey_word_pool", [P, T], U32, AT_EKEY_WORDS)
         keys_word_pool = placed("keys_word_pool", [P, T], U32, AT_KEYS_WORDS)
+        nc.sync.dma_start(ekey_word_pool[:].bitcast(I32), ekey_words[0].rearrange("p n t -> p (n t)").bitcast(I32))
         nc.sync.dma_start(keys_word_pool[:].bitcast(I32), keys_words[0].rearrange("p n t -> p (n t)").bitcast(I32))
-        keys_byte_pool = placed("keys_byte_pool", [P, T], U8, AT_KEYS_BYTES)
-        one = placed("one", [P, 1], F32, AT_KEYS_WORDS - 64)
-        nc.vector.memset(keys_byte_pool[:].bitcast(I32), 0)
-        nc.vector.memset(one[:], 1.0)
-        for r in range(PACK):
-            nc.sync.dma_start(keys_byte_pool[KEYS_SCALE_ROW + r : P : QUADRANT, :].bitcast(I32), keys_scales[0, r:SCALE_ROWS:PACK, :].bitcast(I32))
-        nc.scalar.activation(identity[:], distance[:, 0:P], ACT.Relu, bias=one[:], scale=-1.0)
+        ekey_byte_pool = sbuf("ekey_byte_pool", [P, T], U8)
+        keys_byte_pool = sbuf("keys_byte_pool", [P, T], U8)
+        for pool, rows in ((ekey_byte_pool, ekey_scales), (keys_byte_pool, keys_scales)):
+            nc.vector.memset(pool[:].bitcast(I32), 0)
+            nc.scalar.dma_start(pool[0:P:ROW_STEP, :].bitcast(I32), rows[0].bitcast(I32))
+
+        fac_sb = sbuf("fac_sb", [P, PACK], F32)
+        nc.gpsimd.dma_start(fac_sb[:], fac.rearrange("(p t) o -> p (t o)", t=PACK))
+        offset = sbuf("offset", [P, P], F32)
+        distance = sbuf("distance", [P, P], F32)
+        identity = sbuf("identity", [P, P], F32)
+        nc.gpsimd.iota(offset[:], pattern=[[-1, P]], base=0, channel_multiplier=1, allow_small_or_imprecise_dtypes=True)
+        nc.scalar.activation(distance[:], offset[:], ACT.Abs)
+        nc.scalar.activation(identity[:], distance[:], ACT.Relu, bias=1.0, scale=-1.0)
 
         evals_rows = evals.rearrange("(p t) c -> p t c", t=PACK)
         vals_rows = vals.rearrange("(p t) c -> p t c", t=PACK)
         evals_pool, vals_pool = [], []
-        fac_sb = placed("fac_sb", [P, PACK], F32, AT_FAC)
-        for t in range(PACK):
-            evals_pool.append(placed("evals_pool%d" % t, [P, T], F32, AT_LATE_LOADS + t * POOL_BYTES))
-            nc.sync.dma_start(evals_pool[t][:], evals_rows[:, t, :])
-            if t == 0:
-                nc.sync.dma_start(fac_sb[:], fac.rearrange("(p t) o -> p (t o)", t=PACK))
-        for t in range(PACK):
-            vals_pool.append(placed("vals_pool%d" % t, [P, T], F32, AT_LATE_LOADS + (PACK + t) * POOL_BYTES))
-            nc.sync.dma_start(vals_pool[t][:], vals_rows[:, t, :])
 
-        ekey_codes = placed("ekey_codes", [P, J], U32, AT_EKEY_CODES)
-        ekey_scale = placed("ekey_scale", [P, J], U8, AT_EKEY_SCALE)
-        keys_scale = sbuf("keys_scale", [P, I], U8)
-        keys_codes = sbuf("keys_codes", [P, I], U32)
+        def load(pools, name, rows, t, at):
+            pools.append(placed("%s%d" % (name, t), [P, T], F32, at[t]))
+            nc.sync.dma_start(pools[t][:], rows[:, t, :])
+
+        for t in range(2):
+            load(evals_pool, "evals_pool", evals_rows, t, AT_EVALS)
+
+        ekey_bytes = sbuf("ekey_bytes", [P, J], U8)
+        keys_bytes = sbuf("keys_bytes", [P, I], U8)
+        key_scales = sbuf("key_scales", [P, J + I], U8)
+        ekey_codes = sbuf("ekey_codes", [P, J], U32)
+        keys_codes = placed("keys_codes", [P, I], U32, AT_KEYS_CODES)
+        nc.vector.tensor_copy(ekey_bytes[:].rearrange("p (t s) -> p s t", t=PACK), ekey_byte_pool[:].indirect(evicted_list[:]))
+        nc.vector.tensor_copy(keys_bytes[:], keys_byte_pool[:].indirect(kept_list[:]))
+        nc.vector.tensor_copy(key_scales[:, 0:J].bitcast(I32), ekey_bytes[:].bitcast(I32))
+        nc.vector.tensor_copy(key_scales[:, J:].bitcast(I32), keys_bytes[:].bitcast(I32))
+        for r in range(1, PACK):
+            nc.scalar.dma_start(key_scales[r:P:QUADRANT, :].bitcast(I32), key_scales[r * ROW_STEP : P : QUADRANT, :].bitcast(I32))
+        ekey_scale, keys_scale = key_scales[:, 0:J], key_scales[:, J:]
         nc.vector.tensor_copy(ekey_codes[:].rearrange("p (t s) -> p s t", t=PACK), ekey_word_pool[:].indirect(evicted_list[:]))
-        nc.vector.tensor_copy(ekey_scale[:].rearrange("p (t s) -> p s t", t=PACK), ekey_byte_pool[:].indirect(evicted_list[:]))
-        nc.vector.tensor_copy(keys_codes[:], keys_word_pool[:].indirect(kept_list[:]))
         halves = (slice(0, HALF), slice(HALF, I))
         for cols in halves:
-            nc.vector.tensor_copy(keys_scale[:, cols], keys_byte_pool[:].indirect(entries(kept_list, cols)))
+            nc.vector.tensor_copy(keys_codes[:, cols], keys_word_pool[:].indirect(entries(kept_list, cols)))
+
+        for t in range(2, PACK):
+            load(evals_pool, "evals_pool", evals_rows, t, AT_EVALS)
 
         first_picked = sbuf("first_picked", [P, J], BF16)
         nc.scalar.activation(first_picked[:], evals_pool[0][:].indirect(evicted_list[:]), ACT.Copy)
         neg_max = placed("neg_max", [P, PACK], F32, AT_NEG_MAX)
         sums = [sbuf("sum%d" % h, [P, 2], F32) for h in range(2)]
         invs = [sbuf("inv%d" % h, [P, 2], F32) for h in range(2)]
-        prob = [placed("prob%d" % t, [P, I], F32, AT_LATE_LOADS + t * 4 * I) for t in range(PACK)]
+        prob = [placed("prob%d" % t, [P, I], F32, AT_EVALS[0] + t * 4 * I) for t in range(PACK)]
         w_rows = placed("w_rows", [P, PACK, I], BF16, AT_W_ROWS)
         for t in range(PACK):
             rows = slice(t * P, (t + 1) * P)
             score = psum.tile([P, I], F32, name="score", tag="product")
             for cols in halves if t == 0 else (slice(0, I),):
                 nc.tensor.matmul_mx(score[:, cols], lhsT=ekey_codes[:, rows].bitcast(FP8X4), lhsT_scale=ekey_scale[:, rows],
-                                    rhs=keys_codes[:, cols].bitcast(FP8X4), rhs_scale=keys_scale[KEYS_SCALE_ROW:P, cols], start=True, stop=True)
+                                    rhs=keys_codes[:, cols].bitcast(FP8X4), rhs_scale=keys_scale[:, cols], start=True, stop=True)
             nc.vector.tensor_reduce(neg_max[:, t : t + 1], score[:], AXIS.X, ALU.max, negate=True)
             nc.scalar.activation(prob[t][:], score[:], ACT.Exp, bias=neg_max[:, t : t + 1], accum_out=sums[t // 2][:, t % 2 : t % 2 + 1])
+        for t in range(PACK):
+            load(vals_pool, "vals_pool", vals_rows, t, AT_VALS)
         for h in range(2):
             nc.vector.reciprocal(invs[h][:], sums[h][:])
             for t in (2 * h, 2 * h + 1):
@@ -134,14 +138,14 @@ def tile_attend_softmerge_pl_kernel(tc, ekey_words, ekey_scales, keys_words, key
             nc.vector.quantize_mx(w_codes[:, cols].bitcast(FP8X4), w_scale[:, cols], w_grouped[:, cols, :].rearrange("p i t -> p (i t)"))
 
         merged = []
-        merged_sb = placed("merged_sb", [P, PACK, I], F32, AT_LAST_EVALS + POOL_BYTES)
+        merged_sb = placed("merged_sb", [P, PACK - 1, I], F32, AT_VALS[0] + KIB)
         last = PACK - 1
         late_picked = placed("late_picked", [P, 3 * J], BF16, AT_NEG_MAX)
-        turned_pairs = []
-        for h in range(2):
-            turned_pairs.append(psum.tile([P, 2, 2, P], F32, name="turned", tag="turned"))
-            for n in range(2):
-                t = 2 * h + n
+        turned = []
+        for first, planes in ((0, 2), (2, 1), (3, 1)):
+            turned.append(psum.tile([P, planes, 2, P], F32, name="turned", tag="turned"))
+            for n in range(planes):
+                t = first + n
                 if t == 0:
                     picked = first_picked[:]
                 else:
@@ -149,27 +153,31 @@ def tile_attend_softmerge_pl_kernel(tc, ekey_words, ekey_scales, keys_words, key
                     nc.scalar.activation(picked, evals_pool[t][:].indirect(evicted_list[:]), ACT.Copy)
                 pairs = picked.bitcast(F32)
                 for u in range(2):
-                    nc.tensor.transpose(turned_pairs[h][:, n, u, :], pairs[:, u : J // 2 : 2], identity[:])
-        for h in range(2):
-            turned = turned_pairs[h]
-            grouped = placed("vt_grouped%d" % h, [P, 2 * P * PACK], BF16, (AT_W_ROWS, AT_LAST_VT)[h])
-            nc.vector.tensor_copy(grouped[:].bitcast(F32).rearrange("p (t e u) -> p t e u", t=2, u=2), turned[:].rearrange("p t u e -> p t e u"))
-            codes = placed("vt_codes%d" % h, [P, 2 * P], U32, (AT_NEG_MAX, AT_LAST_VT + 4 * KIB)[h])
-            scale = sbuf("vt_scale%d" % h, [P, 2 * P], U8)
+                    nc.tensor.transpose(turned[-1][:, n, u, :], pairs[:, u : J // 2 : 2], identity[:])
+
+        def group(copy, grouped, bank):
+            copy(grouped.bitcast(F32).rearrange("p (t e u) -> p t e u", e=P, u=2), bank[:].rearrange("p t u e -> p t e u"))
+
+        def multiply(codes, scale, grouped):
             nc.vector.quantize_mx(codes[:].bitcast(FP8X4), scale[:], grouped[:])
-            for n in range(2):
-                t = 2 * h + n
+            for n in range(codes.shape[1] // P):
                 merged.append(psum.tile([P, I], F32, name="merged", tag="product"))
-                nc.tensor.matmul_mx(merged[t][:], lhsT=codes[:, n * P : (n + 1) * P].bitcast(FP8X4), lhsT_scale=scale[:, n * P : (n + 1) * P],
+                nc.tensor.matmul_mx(merged[-1][:], lhsT=codes[:, n * P : (n + 1) * P].bitcast(FP8X4), lhsT_scale=scale[:, n * P : (n + 1) * P],
                                     rhs=w_codes[:].bitcast(FP8X4), rhs_scale=w_scale[:], start=True, stop=True)
+
+        early_grouped = placed("early_grouped", [P, last * P * PACK], BF16, AT_W_ROWS)
+        group(nc.vector.tensor_copy, early_grouped[:, 0 : 2 * P * PACK], turned[0])
+        group(nc.vector.tensor_copy, early_grouped[:, 2 * P * PACK :], turned[1])
+        multiply(sbuf("early_codes", [P, last * P], U32), sbuf("early_scale", [P, last * P], U8), early_grouped)
         kept_first = sbuf("kept_first", [P, I], F32)
         nc.scalar.activation(kept_first[:], vals_pool[0][:].indirect(kept_list[:]), ACT.Copy)
-        for t in range(1, PACK):
-            cols = slice(0, I) if t < last else halves[0]
-            nc.scalar.copy(merged_sb[:, t, cols], merged[t][:, cols])
+        for t in range(1, last):
+            nc.scalar.copy(merged_sb[:, t - 1, :], merged[t][:])
+        last_grouped = placed("last_grouped", [P, P * PACK], BF16, AT_VALS[0])
+        group(nc.scalar.copy, last_grouped[:], turned[2])
 
         out_rows = out_0.rearrange("(p t) i -> p t i", t=PACK)
-        y_low = placed("y_low", [P, 2, I], F32, AT_LAST_VT)
+        y_low = sbuf("y_low", [P, 2, I], F32)
         y_high = sbuf("y_high", [P, 2, I], F32)
         y_grouped = sbuf("y_grouped", [P, I, PACK], BF16)
         y_codes = sbuf("y_codes", [P, I], U32)
@@ -179,20 +187,22 @@ def tile_attend_softmerge_pl_kernel(tc, ekey_words, ekey_scales, keys_words, key
             if t == 0:
                 nc.vector.tensor_tensor(y, merged[t][:], kept_first[:], ALU.add)
             else:
-                nc.vector.tensor_tensor(y, vals_pool[t][:].indirect(kept_list[:]), merged_sb[:, t, :], ALU.add)
+                nc.vector.tensor_tensor(y, vals_pool[t][:].indirect(kept_list[:]), merged_sb[:, t - 1, :], ALU.add)
             nc.sync.dma_start(out_rows[:, t, :], y)
             if t == 1:
                 nc.scalar.copy(y_grouped[:, :, 0:2], y_low[:].rearrange("p t i -> p i t"))
+                multiply(placed("last_codes", [P, P], U32, AT_VALS[1] + KIB), sbuf("last_scale", [P, P], U8), last_grouped)
+                nc.scalar.copy(merged_sb[:, last - 1, halves[0]], merged[last][:, halves[0]])
         words_out = out_1[0].rearrange("p n t -> p (n t)").bitcast(I32)
         kept = sbuf("kept", [P, HALF], F32)
         low, high = halves
-        nc.vector.tensor_tensor(y_high[:, 1, low], vals_pool[last][:].indirect(entries(kept_list, low)), merged_sb[:, last, low], ALU.add)
+        nc.vector.tensor_tensor(y_high[:, 1, low], vals_pool[last][:].indirect(entries(kept_list, low)), merged_sb[:, last - 1, low], ALU.add)
         nc.scalar.activation(kept[:], vals_pool[last][:].indirect(entries(kept_list, high)), ACT.Copy)
         nc.vector.tensor_tensor(y_high[:, 1, high], merged[last][:, high], kept[:], ALU.add)
         nc.sync.dma_start(out_rows[:, last, :], y_high[:, 1, :])
-        nc.scalar.copy(y_grouped[:, low, 2:4], y_high[:, :, low].rearrange("p t i -> p i t"))
-        nc.vector.tensor_copy(y_grouped[:, high, 2:4], y_high[:, :, high].rearrange("p t i -> p i t"))
-        for cols in (high, low):
+        for interleave, cols in ((nc.scalar.copy, slice(0, SCALAR_SHARE)), (nc.vector.tensor_copy, slice(SCALAR_SHARE, HALF)), (nc.vector.tensor_copy, high)):
+            interleave(y_grouped[:, cols, 2:4], y_high[:, :, cols].rearrange("p t i -> p i t"))
+        for cols in halves:
             nc.vector.quantize_mx(y_codes[:, cols].bitcast(FP8X4), y_scale[:, cols], y_grouped[:, cols, :].rearrange("p i t -> p (i t)"))
             nc.sync.dma_start(words_out[:, cols], y_codes[:, cols].bitcast(I32))
         for quadrant in range(P // QUADRANT):

@@ -28,14 +28,16 @@ KIB = 1024
 POOL_BYTES = 4 * T
 
 EDGE = 64
-AT_EVALS = (0, POOL_BYTES, 2 * POOL_BYTES, 4 * POOL_BYTES - 2 * EDGE)
-AT_EKEY_WORDS = 3 * POOL_BYTES - EDGE
-AT_VALS = (5 * POOL_BYTES, 7 * POOL_BYTES - 2 * EDGE, 8 * POOL_BYTES, 9 * POOL_BYTES + 4 * I - 2 * EDGE)
-AT_KEYS_WORDS = 6 * POOL_BYTES - EDGE
-AT_KEYS_CODES = 9 * POOL_BYTES - EDGE
+AT_EVALS = (0, POOL_BYTES, 2 * POOL_BYTES + I - 2 * EDGE, 4 * POOL_BYTES)
+AT_KEYS_BYTES = 2 * POOL_BYTES - EDGE
+AT_EKEY_WORDS = 5 * POOL_BYTES - EDGE
+AT_VALS = (6 * POOL_BYTES - 2 * EDGE, 7 * POOL_BYTES, 9 * POOL_BYTES - 2 * EDGE, 10 * POOL_BYTES)
+AT_KEYS_WORDS = 8 * POOL_BYTES - EDGE
+AT_KEYS_CODES = 11 * POOL_BYTES - EDGE
 ROW_STEP = P // SCALE_ROWS
-AT_NEG_MAX = 90 * KIB
-AT_W_ROWS = 93 * KIB
+AT_NEG_MAX = 92 * KIB
+AT_W_ROWS = 95 * KIB
+AT_Y_LOW = 100 * KIB
 
 
 def tile_attend_softmerge_pl_kernel(tc, ekey_words, ekey_scales, keys_words, keys_scales, fac, evals, vals, offs, offs2, out_0, out_1, out_2):
@@ -56,20 +58,22 @@ def tile_attend_softmerge_pl_kernel(tc, ekey_words, ekey_scales, keys_words, key
 
         kept_list = held.tile([P, I // LIST_ROWS], U16, name="kept_list")
         evicted_list = held.tile([P, J // LIST_ROWS], U16, name="evicted_list")
-        nc.sync.dma_start(evicted_list[:], offs2)
-        nc.sync.dma_start(kept_list[:], offs)
         ekey_word_pool = placed("ekey_word_pool", [P, T], U32, AT_EKEY_WORDS)
         keys_word_pool = placed("keys_word_pool", [P, T], U32, AT_KEYS_WORDS)
-        nc.sync.dma_start(ekey_word_pool[:].bitcast(I32), ekey_words[0].rearrange("p n t -> p (n t)").bitcast(I32))
-        nc.sync.dma_start(keys_word_pool[:].bitcast(I32), keys_words[0].rearrange("p n t -> p (n t)").bitcast(I32))
+        ekey_word_rows = ekey_words[0].rearrange("p n t -> p (n t)").bitcast(I32)
+        nc.sync.dma_start(ekey_word_pool[:, 0 : T // 2].bitcast(I32), ekey_word_rows[:, 0 : T // 2])
+        nc.sync.dma_start(evicted_list[:], offs2)
+        nc.sync.dma_start(kept_list[:], offs)
+        fac_sb = sbuf("fac_sb", [P, PACK], F32)
+        nc.sync.dma_start(fac_sb[:], fac.rearrange("(p t) o -> p (t o)", t=PACK))
         ekey_byte_pool = sbuf("ekey_byte_pool", [P, T], U8)
         keys_byte_pool = sbuf("keys_byte_pool", [P, T], U8)
         for pool, rows in ((ekey_byte_pool, ekey_scales), (keys_byte_pool, keys_scales)):
             nc.vector.memset(pool[:].bitcast(I32), 0)
-            nc.scalar.dma_start(pool[0:P:ROW_STEP, :].bitcast(I32), rows[0].bitcast(I32))
+            nc.sync.dma_start(pool[0:P:ROW_STEP, :].bitcast(I32), rows[0].bitcast(I32))
+        nc.sync.dma_start(ekey_word_pool[:, T // 2 :].bitcast(I32), ekey_word_rows[:, T // 2 :])
+        nc.sync.dma_start(keys_word_pool[:].bitcast(I32), keys_words[0].rearrange("p n t -> p (n t)").bitcast(I32))
 
-        fac_sb = sbuf("fac_sb", [P, PACK], F32)
-        nc.gpsimd.dma_start(fac_sb[:], fac.rearrange("(p t) o -> p (t o)", t=PACK))
         offset = sbuf("offset", [P, P], F32)
         distance = sbuf("distance", [P, P], F32)
         identity = sbuf("identity", [P, P], F32)
@@ -85,11 +89,10 @@ def tile_attend_softmerge_pl_kernel(tc, ekey_words, ekey_scales, keys_words, key
             pools.append(placed("%s%d" % (name, t), [P, T], F32, at[t]))
             nc.sync.dma_start(pools[t][:], rows[:, t, :])
 
-        for t in range(2):
-            load(evals_pool, "evals_pool", evals_rows, t, AT_EVALS)
+        load(evals_pool, "evals_pool", evals_rows, 0, AT_EVALS)
 
         ekey_bytes = sbuf("ekey_bytes", [P, J], U8)
-        keys_bytes = sbuf("keys_bytes", [P, I], U8)
+        keys_bytes = placed("keys_bytes", [P, I], U8, AT_KEYS_BYTES)
         key_scales = sbuf("key_scales", [P, J + I], U8)
         ekey_codes = sbuf("ekey_codes", [P, J], U32)
         keys_codes = placed("keys_codes", [P, I], U32, AT_KEYS_CODES)
@@ -98,14 +101,13 @@ def tile_attend_softmerge_pl_kernel(tc, ekey_words, ekey_scales, keys_words, key
         nc.vector.tensor_copy(key_scales[:, 0:J].bitcast(I32), ekey_bytes[:].bitcast(I32))
         nc.vector.tensor_copy(key_scales[:, J:].bitcast(I32), keys_bytes[:].bitcast(I32))
         for r in range(1, PACK):
-            nc.scalar.dma_start(key_scales[r:P:QUADRANT, :].bitcast(I32), key_scales[r * ROW_STEP : P : QUADRANT, :].bitcast(I32))
+            nc.sync.dma_start(key_scales[r:P:QUADRANT, :].bitcast(I32), key_scales[r * ROW_STEP : P : QUADRANT, :].bitcast(I32))
         ekey_scale, keys_scale = key_scales[:, 0:J], key_scales[:, J:]
         nc.vector.tensor_copy(ekey_codes[:].rearrange("p (t s) -> p s t", t=PACK), ekey_word_pool[:].indirect(evicted_list[:]))
         halves = (slice(0, HALF), slice(HALF, I))
-        for cols in halves:
-            nc.vector.tensor_copy(keys_codes[:, cols], keys_word_pool[:].indirect(entries(kept_list, cols)))
+        nc.vector.tensor_copy(keys_codes[:], keys_word_pool[:].indirect(kept_list[:]))
 
-        for t in range(2, PACK):
+        for t in range(1, PACK):
             load(evals_pool, "evals_pool", evals_rows, t, AT_EVALS)
 
         first_picked = sbuf("first_picked", [P, J], BF16)
@@ -118,9 +120,8 @@ def tile_attend_softmerge_pl_kernel(tc, ekey_words, ekey_scales, keys_words, key
         for t in range(PACK):
             rows = slice(t * P, (t + 1) * P)
             score = psum.tile([P, I], F32, name="score", tag="product")
-            for cols in halves if t == 0 else (slice(0, I),):
-                nc.tensor.matmul_mx(score[:, cols], lhsT=ekey_codes[:, rows].bitcast(FP8X4), lhsT_scale=ekey_scale[:, rows],
-                                    rhs=keys_codes[:, cols].bitcast(FP8X4), rhs_scale=keys_scale[:, cols], start=True, stop=True)
+            nc.tensor.matmul_mx(score[:], lhsT=ekey_codes[:, rows].bitcast(FP8X4), lhsT_scale=ekey_scale[:, rows],
+                                rhs=keys_codes[:].bitcast(FP8X4), rhs_scale=keys_scale, start=True, stop=True)
             nc.vector.tensor_reduce(neg_max[:, t : t + 1], score[:], AXIS.X, ALU.max, negate=True)
             nc.scalar.activation(prob[t][:], score[:], ACT.Exp, bias=neg_max[:, t : t + 1], accum_out=sums[t // 2][:, t % 2 : t % 2 + 1])
         for t in range(PACK):
@@ -142,10 +143,10 @@ def tile_attend_softmerge_pl_kernel(tc, ekey_words, ekey_scales, keys_words, key
         last = PACK - 1
         late_picked = placed("late_picked", [P, 3 * J], BF16, AT_NEG_MAX)
         turned = []
-        for first, planes in ((0, 2), (2, 1), (3, 1)):
-            turned.append(psum.tile([P, planes, 2, P], F32, name="turned", tag="turned"))
-            for n in range(planes):
-                t = first + n
+        for h in range(2):
+            turned.append(psum.tile([P, 2, 2, P], F32, name="turned", tag=("product", "turned")[h]))
+            for n in range(2):
+                t = 2 * h + n
                 if t == 0:
                     picked = first_picked[:]
                 else:
@@ -153,31 +154,25 @@ def tile_attend_softmerge_pl_kernel(tc, ekey_words, ekey_scales, keys_words, key
                     nc.scalar.activation(picked, evals_pool[t][:].indirect(evicted_list[:]), ACT.Copy)
                 pairs = picked.bitcast(F32)
                 for u in range(2):
-                    nc.tensor.transpose(turned[-1][:, n, u, :], pairs[:, u : J // 2 : 2], identity[:])
-
-        def group(copy, grouped, bank):
-            copy(grouped.bitcast(F32).rearrange("p (t e u) -> p t e u", e=P, u=2), bank[:].rearrange("p t u e -> p t e u"))
-
-        def multiply(codes, scale, grouped):
+                    nc.tensor.transpose(turned[h][:, n, u, :], pairs[:, u : J // 2 : 2], identity[:])
+        for h in range(2):
+            grouped = placed("vt_grouped%d" % h, [P, 2 * P * PACK], BF16, (AT_W_ROWS, AT_Y_LOW)[h])
+            nc.vector.tensor_copy(grouped[:].bitcast(F32).rearrange("p (t e u) -> p t e u", t=2, u=2), turned[h][:].rearrange("p t u e -> p t e u"))
+            codes = placed("vt_codes%d" % h, [P, 2 * P], U32, AT_EVALS[last] + h * KIB)
+            scale = sbuf("vt_scale%d" % h, [P, 2 * P], U8)
             nc.vector.quantize_mx(codes[:].bitcast(FP8X4), scale[:], grouped[:])
-            for n in range(codes.shape[1] // P):
+            for n in range(2):
                 merged.append(psum.tile([P, I], F32, name="merged", tag="product"))
                 nc.tensor.matmul_mx(merged[-1][:], lhsT=codes[:, n * P : (n + 1) * P].bitcast(FP8X4), lhsT_scale=scale[:, n * P : (n + 1) * P],
                                     rhs=w_codes[:].bitcast(FP8X4), rhs_scale=w_scale[:], start=True, stop=True)
-
-        early_grouped = placed("early_grouped", [P, last * P * PACK], BF16, AT_W_ROWS)
-        group(nc.vector.tensor_copy, early_grouped[:, 0 : 2 * P * PACK], turned[0])
-        group(nc.vector.tensor_copy, early_grouped[:, 2 * P * PACK :], turned[1])
-        multiply(sbuf("early_codes", [P, last * P], U32), sbuf("early_scale", [P, last * P], U8), early_grouped)
         kept_first = sbuf("kept_first", [P, I], F32)
         nc.scalar.activation(kept_first[:], vals_pool[0][:].indirect(kept_list[:]), ACT.Copy)
-        for t in range(1, last):
-            nc.scalar.copy(merged_sb[:, t - 1, :], merged[t][:])
-        last_grouped = placed("last_grouped", [P, P * PACK], BF16, AT_VALS[0])
-        group(nc.scalar.copy, last_grouped[:], turned[2])
+        for t in range(1, PACK):
+            cols = slice(0, I) if t < last else halves[0]
+            nc.scalar.copy(merged_sb[:, t - 1, cols], merged[t][:, cols])
 
         out_rows = out_0.rearrange("(p t) i -> p t i", t=PACK)
-        y_low = sbuf("y_low", [P, 2, I], F32)
+        y_low = placed("y_low", [P, 2, I], F32, AT_Y_LOW)
         y_high = sbuf("y_high", [P, 2, I], F32)
         y_grouped = sbuf("y_grouped", [P, I, PACK], BF16)
         y_codes = sbuf("y_codes", [P, I], U32)
@@ -191,8 +186,6 @@ def tile_attend_softmerge_pl_kernel(tc, ekey_words, ekey_scales, keys_words, key
             nc.sync.dma_start(out_rows[:, t, :], y)
             if t == 1:
                 nc.scalar.copy(y_grouped[:, :, 0:2], y_low[:].rearrange("p t i -> p i t"))
-                multiply(placed("last_codes", [P, P], U32, AT_VALS[1] + KIB), sbuf("last_scale", [P, P], U8), last_grouped)
-                nc.scalar.copy(merged_sb[:, last - 1, halves[0]], merged[last][:, halves[0]])
         words_out = out_1[0].rearrange("p n t -> p (n t)").bitcast(I32)
         kept = sbuf("kept", [P, HALF], F32)
         low, high = halves

@@ -23,7 +23,6 @@ SCALE_ROWS = 16
 LIST_ROWS = 16
 HALF = I // 2
 RUN = 4
-SCALAR_SHARE = 192
 KIB = 1024
 POOL_BYTES = 4 * T
 
@@ -36,7 +35,6 @@ AT_KEYS_WORDS = 8 * POOL_BYTES - EDGE
 AT_KEYS_CODES = 11 * POOL_BYTES - EDGE
 ROW_STEP = P // SCALE_ROWS
 AT_NEG_MAX = 92 * KIB
-AT_W_ROWS = 95 * KIB
 AT_Y_LOW = 100 * KIB
 
 
@@ -116,7 +114,6 @@ def tile_attend_softmerge_pl_kernel(tc, ekey_words, ekey_scales, keys_words, key
         sums = [sbuf("sum%d" % h, [P, 2], F32) for h in range(2)]
         invs = [sbuf("inv%d" % h, [P, 2], F32) for h in range(2)]
         prob = [placed("prob%d" % t, [P, I], F32, AT_EVALS[0] + t * 4 * I) for t in range(PACK)]
-        w_rows = placed("w_rows", [P, PACK, I], BF16, AT_W_ROWS)
         for t in range(PACK):
             rows = slice(t * P, (t + 1) * P)
             score = psum.tile([P, I], F32, name="score", tag="product")
@@ -126,6 +123,9 @@ def tile_attend_softmerge_pl_kernel(tc, ekey_words, ekey_scales, keys_words, key
             nc.scalar.activation(prob[t][:], score[:], ACT.Exp, bias=neg_max[:, t : t + 1], accum_out=sums[t // 2][:, t % 2 : t % 2 + 1])
         for t in range(PACK):
             load(vals_pool, "vals_pool", vals_rows, t, AT_VALS)
+        second_picked = placed("second_picked", [P, J], BF16, AT_KEYS_CODES + 2 * EDGE)
+        nc.vector.tensor_copy(second_picked[:], evals_pool[1][:].indirect(evicted_list[:]))
+        w_rows = placed("w_rows", [P, PACK, I], BF16, AT_EVALS[1])
         for h in range(2):
             nc.vector.reciprocal(invs[h][:], sums[h][:])
             for t in (2 * h, 2 * h + 1):
@@ -141,7 +141,7 @@ def tile_attend_softmerge_pl_kernel(tc, ekey_words, ekey_scales, keys_words, key
         merged = []
         merged_sb = placed("merged_sb", [P, PACK - 1, I], F32, AT_VALS[0] + KIB)
         last = PACK - 1
-        late_picked = placed("late_picked", [P, 3 * J], BF16, AT_NEG_MAX)
+        late_picked = placed("late_picked", [P, 2 * J], BF16, AT_NEG_MAX)
         turned = []
         for h in range(2):
             turned.append(psum.tile([P, 2, 2, P], F32, name="turned", tag=("product", "turned")[h]))
@@ -149,15 +149,17 @@ def tile_attend_softmerge_pl_kernel(tc, ekey_words, ekey_scales, keys_words, key
                 t = 2 * h + n
                 if t == 0:
                     picked = first_picked[:]
+                elif t == 1:
+                    picked = second_picked[:]
                 else:
-                    picked = late_picked[:, (t - 1) * J : t * J]
+                    picked = late_picked[:, (t - 2) * J : (t - 1) * J]
                     nc.scalar.activation(picked, evals_pool[t][:].indirect(evicted_list[:]), ACT.Copy)
                 pairs = picked.bitcast(F32)
                 for u in range(2):
                     nc.tensor.transpose(turned[h][:, n, u, :], pairs[:, u : J // 2 : 2], identity[:])
         for h in range(2):
-            grouped = placed("vt_grouped%d" % h, [P, 2 * P * PACK], BF16, (AT_W_ROWS, AT_Y_LOW)[h])
-            nc.vector.tensor_copy(grouped[:].bitcast(F32).rearrange("p (t e u) -> p t e u", t=2, u=2), turned[h][:].rearrange("p t u e -> p t e u"))
+            grouped = placed("vt_grouped%d" % h, [P, 2 * P * PACK], BF16, (AT_EVALS[2], AT_Y_LOW)[h])
+            (nc.scalar.copy, nc.vector.tensor_copy)[h](grouped[:].bitcast(F32).rearrange("p (t e u) -> p t e u", t=2, u=2), turned[h][:].rearrange("p t u e -> p t e u"))
             codes = placed("vt_codes%d" % h, [P, 2 * P], U32, AT_EVALS[last] + h * KIB)
             scale = sbuf("vt_scale%d" % h, [P, 2 * P], U8)
             nc.vector.quantize_mx(codes[:].bitcast(FP8X4), scale[:], grouped[:])
@@ -189,11 +191,15 @@ def tile_attend_softmerge_pl_kernel(tc, ekey_words, ekey_scales, keys_words, key
         words_out = out_1[0].rearrange("p n t -> p (n t)").bitcast(I32)
         kept = sbuf("kept", [P, HALF], F32)
         low, high = halves
-        nc.vector.tensor_tensor(y_high[:, 1, low], vals_pool[last][:].indirect(entries(kept_list, low)), merged_sb[:, last - 1, low], ALU.add)
+        pieces = [slice(n * P, (n + 1) * P) for n in range(I // P)]
+        for cols in pieces[:2]:
+            nc.vector.tensor_tensor(y_high[:, 1, cols], vals_pool[last][:].indirect(entries(kept_list, cols)), merged_sb[:, last - 1, cols], ALU.add)
         nc.scalar.activation(kept[:], vals_pool[last][:].indirect(entries(kept_list, high)), ACT.Copy)
-        nc.vector.tensor_tensor(y_high[:, 1, high], merged[last][:, high], kept[:], ALU.add)
+        for cols in pieces[2:]:
+            nc.vector.tensor_tensor(y_high[:, 1, cols], merged[last][:, cols], kept[:, cols.start - HALF : cols.stop - HALF], ALU.add)
         nc.sync.dma_start(out_rows[:, last, :], y_high[:, 1, :])
-        for interleave, cols in ((nc.scalar.copy, slice(0, SCALAR_SHARE)), (nc.vector.tensor_copy, slice(SCALAR_SHARE, HALF)), (nc.vector.tensor_copy, high)):
+        for n, cols in enumerate(pieces):
+            interleave = (nc.scalar.copy, nc.vector.tensor_copy)[n // 2]
             interleave(y_grouped[:, cols, 2:4], y_high[:, :, cols].rearrange("p t i -> p i t"))
         for cols in halves:
             nc.vector.quantize_mx(y_codes[:, cols].bitcast(FP8X4), y_scale[:, cols], y_grouped[:, cols, :].rearrange("p i t -> p (i t)"))

@@ -27,7 +27,7 @@ KIB = 1024
 POOL_BYTES = 4 * T
 
 EDGE = 64
-AT_EVALS = (0, POOL_BYTES, 2 * POOL_BYTES + I - 2 * EDGE, 4 * POOL_BYTES)
+AT_EVALS = (0, POOL_BYTES, 2 * POOL_BYTES + T - 2 * EDGE, 4 * POOL_BYTES)
 AT_KEYS_BYTES = 2 * POOL_BYTES - EDGE
 AT_EKEY_WORDS = 5 * POOL_BYTES - EDGE
 AT_VALS = (6 * POOL_BYTES - 2 * EDGE, 7 * POOL_BYTES, 9 * POOL_BYTES - 2 * EDGE, 10 * POOL_BYTES)
@@ -62,10 +62,8 @@ def tile_attend_softmerge_pl_kernel(tc, ekey_words, ekey_scales, keys_words, key
         nc.sync.dma_start(ekey_word_pool[:, 0 : T // 2].bitcast(I32), ekey_word_rows[:, 0 : T // 2])
         nc.sync.dma_start(evicted_list[:], offs2)
         nc.sync.dma_start(kept_list[:], offs)
-        fac_sb = sbuf("fac_sb", [P, PACK], F32)
-        nc.sync.dma_start(fac_sb[:], fac.rearrange("(p t) o -> p (t o)", t=PACK))
         ekey_byte_pool = sbuf("ekey_byte_pool", [P, T], U8)
-        keys_byte_pool = sbuf("keys_byte_pool", [P, T], U8)
+        keys_byte_pool = placed("keys_byte_pool", [P, T], U8, AT_KEYS_BYTES)
         for pool, rows in ((ekey_byte_pool, ekey_scales), (keys_byte_pool, keys_scales)):
             nc.vector.memset(pool[:].bitcast(I32), 0)
             nc.sync.dma_start(pool[0:P:ROW_STEP, :].bitcast(I32), rows[0].bitcast(I32))
@@ -88,24 +86,25 @@ def tile_attend_softmerge_pl_kernel(tc, ekey_words, ekey_scales, keys_words, key
             nc.sync.dma_start(pools[t][:], rows[:, t, :])
 
         load(evals_pool, "evals_pool", evals_rows, 0, AT_EVALS)
+        fac_sb = placed("fac_sb", [P, PACK], F32, AT_KEYS_BYTES + KIB)
 
-        ekey_bytes = sbuf("ekey_bytes", [P, J], U8)
-        keys_bytes = placed("keys_bytes", [P, I], U8, AT_KEYS_BYTES)
+        picked_bytes = sbuf("picked_bytes", [P, J + I], U8)
         key_scales = sbuf("key_scales", [P, J + I], U8)
+        nc.vector.memset(key_scales[:].bitcast(I32), 0)
         ekey_codes = sbuf("ekey_codes", [P, J], U32)
         keys_codes = placed("keys_codes", [P, I], U32, AT_KEYS_CODES)
-        nc.vector.tensor_copy(ekey_bytes[:].rearrange("p (t s) -> p s t", t=PACK), ekey_byte_pool[:].indirect(evicted_list[:]))
-        nc.vector.tensor_copy(keys_bytes[:], keys_byte_pool[:].indirect(kept_list[:]))
-        nc.vector.tensor_copy(key_scales[:, 0:J].bitcast(I32), ekey_bytes[:].bitcast(I32))
-        nc.vector.tensor_copy(key_scales[:, J:].bitcast(I32), keys_bytes[:].bitcast(I32))
-        for r in range(1, PACK):
-            nc.sync.dma_start(key_scales[r:P:QUADRANT, :].bitcast(I32), key_scales[r * ROW_STEP : P : QUADRANT, :].bitcast(I32))
+        nc.vector.tensor_copy(picked_bytes[:, 0:J].rearrange("p (t s) -> p s t", t=PACK), ekey_byte_pool[:].indirect(evicted_list[:]))
+        nc.vector.tensor_copy(picked_bytes[:, J:], keys_byte_pool[:].indirect(kept_list[:]))
+        for r in range(PACK):
+            nc.sync.dma_start(key_scales[r:P:QUADRANT, :].bitcast(I32), picked_bytes[r * ROW_STEP : P : QUADRANT, :].bitcast(I32))
         ekey_scale, keys_scale = key_scales[:, 0:J], key_scales[:, J:]
         nc.vector.tensor_copy(ekey_codes[:].rearrange("p (t s) -> p s t", t=PACK), ekey_word_pool[:].indirect(evicted_list[:]))
         halves = (slice(0, HALF), slice(HALF, I))
         nc.vector.tensor_copy(keys_codes[:], keys_word_pool[:].indirect(kept_list[:]))
 
-        for t in range(1, PACK):
+        load(evals_pool, "evals_pool", evals_rows, 1, AT_EVALS)
+        nc.sync.dma_start(fac_sb[:], fac.rearrange("(p t) o -> p (t o)", t=PACK))
+        for t in range(2, PACK):
             load(evals_pool, "evals_pool", evals_rows, t, AT_EVALS)
 
         first_picked = sbuf("first_picked", [P, J], BF16)

@@ -26,7 +26,7 @@ RUN = 4
 KIB = 1024
 POOL_BYTES = 4 * T
 
-EDGE = 64
+EDGE = 256
 AT_EVALS = (0, POOL_BYTES, 2 * POOL_BYTES + T - 2 * EDGE, 4 * POOL_BYTES)
 AT_KEYS_BYTES = 2 * POOL_BYTES - EDGE
 AT_EKEY_WORDS = 5 * POOL_BYTES - EDGE
@@ -46,10 +46,10 @@ def tile_attend_softmerge_pl_kernel(tc, ekey_words, ekey_scales, keys_words, key
         psum = ctx.enter_context(tc.psum_pool(name="psum", bufs=PACK))
 
         def sbuf(name, shape, dtype):
-            return held.tile(shape, dtype, name=name, align_bytes=64)
+            return held.tile(shape, dtype, name=name, align_bytes=EDGE)
 
         def placed(name, shape, dtype, offset):
-            return shared.tile(shape, dtype, name=name, align_bytes=64, offset=offset)
+            return shared.tile(shape, dtype, name=name, align_bytes=EDGE, offset=offset)
 
         def entries(listed, cols):
             return listed[:, cols.start // LIST_ROWS : cols.stop // LIST_ROWS]

@@ -23,6 +23,7 @@ SCALE_ROWS = 16
 LIST_ROWS = 16
 HALF = I // 2
 RUN = 4
+FRONT = T // 4
 KIB = 1024
 POOL_BYTES = 4 * T
 
@@ -59,7 +60,7 @@ def tile_attend_softmerge_pl_kernel(tc, ekey_words, ekey_scales, keys_words, key
         ekey_word_pool = placed("ekey_word_pool", [P, T], U32, AT_EKEY_WORDS)
         keys_word_pool = placed("keys_word_pool", [P, T], U32, AT_KEYS_WORDS)
         ekey_word_rows = ekey_words[0].rearrange("p n t -> p (n t)").bitcast(I32)
-        nc.sync.dma_start(ekey_word_pool[:, 0 : T // 2].bitcast(I32), ekey_word_rows[:, 0 : T // 2])
+        nc.sync.dma_start(ekey_word_pool[:, 0:FRONT].bitcast(I32), ekey_word_rows[:, 0:FRONT])
         nc.sync.dma_start(evicted_list[:], offs2)
         nc.sync.dma_start(kept_list[:], offs)
         ekey_byte_pool = sbuf("ekey_byte_pool", [P, T], U8)
@@ -67,7 +68,7 @@ def tile_attend_softmerge_pl_kernel(tc, ekey_words, ekey_scales, keys_words, key
         for pool, rows in ((ekey_byte_pool, ekey_scales), (keys_byte_pool, keys_scales)):
             nc.vector.memset(pool[:].bitcast(I32), 0)
             nc.sync.dma_start(pool[0:P:ROW_STEP, :].bitcast(I32), rows[0].bitcast(I32))
-        nc.sync.dma_start(ekey_word_pool[:, T // 2 :].bitcast(I32), ekey_word_rows[:, T // 2 :])
+        nc.sync.dma_start(ekey_word_pool[:, FRONT:].bitcast(I32), ekey_word_rows[:, FRONT:])
         nc.sync.dma_start(keys_word_pool[:].bitcast(I32), keys_words[0].rearrange("p n t -> p (n t)").bitcast(I32))
 
         offset = sbuf("offset", [P, P], F32)
@@ -90,12 +91,12 @@ def tile_attend_softmerge_pl_kernel(tc, ekey_words, ekey_scales, keys_words, key
 
         picked_bytes = sbuf("picked_bytes", [P, J + I], U8)
         key_scales = sbuf("key_scales", [P, J + I], U8)
-        nc.vector.memset(key_scales[:].bitcast(I32), 0)
         ekey_codes = sbuf("ekey_codes", [P, J], U32)
         keys_codes = placed("keys_codes", [P, I], U32, AT_KEYS_CODES)
         nc.vector.tensor_copy(picked_bytes[:, 0:J].rearrange("p (t s) -> p s t", t=PACK), ekey_byte_pool[:].indirect(evicted_list[:]))
         nc.vector.tensor_copy(picked_bytes[:, J:], keys_byte_pool[:].indirect(kept_list[:]))
-        for r in range(PACK):
+        nc.vector.tensor_copy(key_scales[:].bitcast(I32), picked_bytes[:].bitcast(I32))
+        for r in range(1, PACK):
             nc.sync.dma_start(key_scales[r:P:QUADRANT, :].bitcast(I32), picked_bytes[r * ROW_STEP : P : QUADRANT, :].bitcast(I32))
         ekey_scale, keys_scale = key_scales[:, 0:J], key_scales[:, J:]
         nc.vector.tensor_copy(ekey_codes[:].rearrange("p (t s) -> p s t", t=PACK), ekey_word_pool[:].indirect(evicted_list[:]))

@@ -23,7 +23,7 @@ SCALE_ROWS = 16
 LIST_ROWS = 16
 HALF = I // 2
 RUN = 4
-FRONT = T // 4
+FRONT = 3 * T // 8
 KIB = 1024
 POOL_BYTES = 4 * T
 

@@ -139,7 +139,6 @@ def tile_attend_softmerge_pl_kernel(tc, ekey_words, ekey_scales, keys_words, key
             nc.vector.quantize_mx(w_codes[:, cols].bitcast(FP8X4), w_scale[:, cols], w_grouped[:, cols, :].rearrange("p i t -> p (i t)"))
 
         merged = []
-        merged_sb = placed("merged_sb", [P, PACK - 1, I], F32, AT_VALS[0] + KIB)
         last = PACK - 1
         late_picked = placed("late_picked", [P, 2 * J], BF16, AT_NEG_MAX)
         turned = []
@@ -169,9 +168,11 @@ def tile_attend_softmerge_pl_kernel(tc, ekey_words, ekey_scales, keys_words, key
                                     rhs=w_codes[:].bitcast(FP8X4), rhs_scale=w_scale[:], start=True, stop=True)
         kept_first = sbuf("kept_first", [P, I], F32)
         nc.scalar.activation(kept_first[:], vals_pool[0][:].indirect(kept_list[:]), ACT.Copy)
-        for t in range(1, PACK):
-            cols = slice(0, I) if t < last else halves[0]
-            nc.scalar.copy(merged_sb[:, t - 1, cols], merged[t][:, cols])
+        kept_second = placed("kept_second", [P, I], F32, AT_VALS[0])
+        nc.scalar.activation(kept_second[:], vals_pool[1][:].indirect(kept_list[:]), ACT.Copy)
+        merged2 = placed("merged2", [P, I], F32, AT_VALS[1])
+        nc.scalar.copy(merged2[:], merged[2][:])
+        merged3 = sbuf("merged3", [P, HALF], F32)
 
         out_rows = out_0.rearrange("(p t) i -> p t i", t=PACK)
         y_low = placed("y_low", [P, 2, I], F32, AT_Y_LOW)
@@ -183,17 +184,23 @@ def tile_attend_softmerge_pl_kernel(tc, ekey_words, ekey_scales, keys_words, key
             y = (y_low, y_high)[t // 2][:, t % 2, :]
             if t == 0:
                 nc.vector.tensor_tensor(y, merged[t][:], kept_first[:], ALU.add)
+            elif t == 1:
+                for cols in halves:
+                    nc.vector.tensor_tensor(y[:, cols], merged[t][:, cols], kept_second[:, cols], ALU.add)
             else:
-                nc.vector.tensor_tensor(y, vals_pool[t][:].indirect(kept_list[:]), merged_sb[:, t - 1, :], ALU.add)
+                nc.vector.tensor_tensor(y, vals_pool[t][:].indirect(kept_list[:]), merged2[:], ALU.add)
+            if t == 0:
+                nc.vector.tensor_copy(merged3[:], merged[last][:, halves[0]])
             nc.sync.dma_start(out_rows[:, t, :], y)
             if t == 1:
-                nc.scalar.copy(y_grouped[:, :, 0:2], y_low[:].rearrange("p t i -> p i t"))
+                for cols in halves:
+                    nc.scalar.copy(y_grouped[:, cols, 0:2], y_low[:, :, cols].rearrange("p t i -> p i t"))
         words_out = out_1[0].rearrange("p n t -> p (n t)").bitcast(I32)
         kept = sbuf("kept", [P, HALF], F32)
         low, high = halves
         pieces = [slice(n * P, (n + 1) * P) for n in range(I // P)]
         for cols in pieces[:2]:
-            nc.vector.tensor_tensor(y_high[:, 1, cols], vals_pool[last][:].indirect(entries(kept_list, cols)), merged_sb[:, last - 1, cols], ALU.add)
+            nc.vector.tensor_tensor(y_high[:, 1, cols], vals_pool[last][:].indirect(entries(kept_list, cols)), merged3[:, cols], ALU.add)
         nc.scalar.activation(kept[:], vals_pool[last][:].indirect(entries(kept_list, high)), ACT.Copy)
         for cols in pieces[2:]:
             nc.vector.tensor_tensor(y_high[:, 1, cols], merged[last][:, cols], kept[:, cols.start - HALF : cols.stop - HALF], ALU.add)

from contextlib import ExitStack

import concourse.mybir as mybir

D, T, J, I, E = 512, 2048, 512, 512, 512
FLOPS = 2 * D * J * I + 2 * J * E * I

F32 = mybir.dt.float32
BF16 = mybir.dt.bfloat16
I32 = mybir.dt.int32
U32 = mybir.dt.uint32
U16 = mybir.dt.uint16
U8 = mybir.dt.uint8
FP8X4 = mybir.dt.float8_e4m3fn_x4
ALU = mybir.AluOpType
ACT = mybir.ActivationFunctionType
AXIS = mybir.AxisListType

P = 128
PACK = 4
QUADRANT = 32
SCALE_ROWS = 16
LIST_ROWS = 16
HALF = I // 2
RUN = 4
FRONT = 3 * T // 8
KIB = 1024
POOL_BYTES = 4 * T

EDGE = 256
AT_EVALS = (0, POOL_BYTES, 2 * POOL_BYTES + T - 2 * EDGE, 4 * POOL_BYTES)
AT_KEYS_BYTES = 2 * POOL_BYTES - EDGE
AT_EKEY_WORDS = 5 * POOL_BYTES - EDGE
AT_VALS = (6 * POOL_BYTES - 2 * EDGE, 7 * POOL_BYTES, 9 * POOL_BYTES - 2 * EDGE, 10 * POOL_BYTES)
AT_KEYS_WORDS = 8 * POOL_BYTES - EDGE
AT_KEYS_CODES = 11 * POOL_BYTES - EDGE
ROW_STEP = P // SCALE_ROWS
AT_NEG_MAX = 92 * KIB
AT_Y_LOW = 100 * KIB


def tile_attend_softmerge_pl_kernel(tc, ekey_words, ekey_scales, keys_words, keys_scales, fac, evals, vals, offs, offs2, out_0, out_1, out_2):
    nc = tc.nc
    with ExitStack() as ctx:
        held = ctx.enter_context(tc.tile_pool(name="held", bufs=1))
        shared = ctx.enter_context(tc.tile_pool(name="shared", bufs=1))
        psum = ctx.enter_context(tc.psum_pool(name="psum", bufs=PACK))

        def sbuf(name, shape, dtype):
            return held.tile(shape, dtype, name=name, align_bytes=EDGE)

        def placed(name, shape, dtype, offset):
            return shared.tile(shape, dtype, name=name, align_bytes=EDGE, offset=offset)

        def entries(listed, cols):
            return listed[:, cols.start // LIST_ROWS : cols.stop // LIST_ROWS]

        kept_list = held.tile([P, I // LIST_ROWS], U16, name="kept_list")
        evicted_list = held.tile([P, J // LIST_ROWS], U16, name="evicted_list")
        ekey_word_pool = placed("ekey_word_pool", [P, T], U32, AT_EKEY_WORDS)
        keys_word_pool = placed("keys_word_pool", [P, T], U32, AT_KEYS_WORDS)
        ekey_word_rows = ekey_words[0].rearrange("p n t -> p (n t)").bitcast(I32)
        nc.sync.dma_start(ekey_word_pool[:, 0:FRONT].bitcast(I32), ekey_word_rows[:, 0:FRONT])
        nc.sync.dma_start(evicted_list[:], offs2)
        nc.sync.dma_start(kept_list[:], offs)
        ekey_byte_pool = sbuf("ekey_byte_pool", [P, T], U8)
        keys_byte_pool = placed("keys_byte_pool", [P, T], U8, AT_KEYS_BYTES)
        for pool, rows in ((ekey_byte_pool, ekey_scales), (keys_byte_pool, keys_scales)):
            nc.vector.memset(pool[:].bitcast(I32), 0)
            nc.sync.dma_start(pool[0:P:ROW_STEP, :].bitcast(I32), rows[0].bitcast(I32))
        nc.sync.dma_start(ekey_word_pool[:, FRONT:].bitcast(I32), ekey_word_rows[:, FRONT:])
        nc.sync.dma_start(keys_word_pool[:].bitcast(I32), keys_words[0].rearrange("p n t -> p (n t)").bitcast(I32))

        offset = sbuf("offset", [P, P], F32)
        distance = sbuf("distance", [P, P], F32)
        identity = sbuf("identity", [P, P], F32)
        nc.gpsimd.iota(offset[:], pattern=[[-1, P]], base=0, channel_multiplier=1, allow_small_or_imprecise_dtypes=True)
        nc.scalar.activation(distance[:], offset[:], ACT.Abs)
        nc.scalar.activation(identity[:], distance[:], ACT.Relu, bias=1.0, scale=-1.0)

        evals_rows = evals.rearrange("(p t) c -> p t c", t=PACK)
        vals_rows = vals.rearrange("(p t) c -> p t c", t=PACK)
        evals_pool, vals_pool = [], []

        def load(pools, name, rows, t, at):
            pools.append(placed("%s%d" % (name, t), [P, T], F32, at[t]))
            nc.sync.dma_start(pools[t][:], rows[:, t, :])

        load(evals_pool, "evals_pool", evals_rows, 0, AT_EVALS)
        fac_sb = placed("fac_sb", [P, PACK], F32, AT_KEYS_BYTES + KIB)

        picked_bytes = sbuf("picked_bytes", [P, J + I], U8)
        key_scales = sbuf("key_scales", [P, J + I], U8)
        ekey_codes = sbuf("ekey_codes", [P, J], U32)
        keys_codes = placed("keys_codes", [P, I], U32, AT_KEYS_CODES)
        nc.vector.tensor_copy(picked_bytes[:, 0:J].rearrange("p (t s) -> p s t", t=PACK), ekey_byte_pool[:].indirect(evicted_list[:]))
        nc.vector.tensor_copy(picked_bytes[:, J:], keys_byte_pool[:].indirect(kept_list[:]))
        nc.vector.tensor_copy(key_scales[:].bitcast(I32), picked_bytes[:].bitcast(I32))
        for r in range(1, PACK):
            nc.sync.dma_start(key_scales[r:P:QUADRANT, :].bitcast(I32), picked_bytes[r * ROW_STEP : P : QUADRANT, :].bitcast(I32))
        ekey_scale, keys_scale = key_scales[:, 0:J], key_scales[:, J:]
        nc.vector.tensor_copy(ekey_codes[:].rearrange("p (t s) -> p s t", t=PACK), ekey_word_pool[:].indirect(evicted_list[:]))
        halves = (slice(0, HALF), slice(HALF, I))
        nc.vector.tensor_copy(keys_codes[:], keys_word_pool[:].indirect(kept_list[:]))

        load(evals_pool, "evals_pool", evals_rows, 1, AT_EVALS)
        nc.sync.dma_start(fac_sb[:], fac.rearrange("(p t) o -> p (t o)", t=PACK))
        for t in range(2, PACK):
            load(evals_pool, "evals_pool", evals_rows, t, AT_EVALS)

        first_picked = sbuf("first_picked", [P, J], BF16)
        nc.scalar.activation(first_picked[:], evals_pool[0][:].indirect(evicted_list[:]), ACT.Copy)
        neg_max = placed("neg_max", [P, PACK], F32, AT_NEG_MAX)
        sums = [sbuf("sum%d" % h, [P, 2], F32) for h in range(2)]
        invs = [sbuf("inv%d" % h, [P, 2], F32) for h in range(2)]
        prob = [placed("prob%d" % t, [P, I], F32, AT_EVALS[0] + t * 4 * I) for t in range(PACK)]
        for t in range(PACK):
            rows = slice(t * P, (t + 1) * P)
            score = psum.tile([P, I], F32, name="score", tag="product")
            nc.tensor.matmul_mx(score[:], lhsT=ekey_codes[:, rows].bitcast(FP8X4), lhsT_scale=ekey_scale[:, rows],
                                rhs=keys_codes[:].bitcast(FP8X4), rhs_scale=keys_scale, start=True, stop=True)
            nc.vector.tensor_reduce(neg_max[:, t : t + 1], score[:], AXIS.X, ALU.max, negate=True)
            nc.scalar.activation(prob[t][:], score[:], ACT.Exp, bias=neg_max[:, t : t + 1], accum_out=sums[t // 2][:, t % 2 : t % 2 + 1])
        for t in range(PACK):
            load(vals_pool, "vals_pool", vals_rows, t, AT_VALS)
        second_picked = placed("second_picked", [P, J], BF16, AT_KEYS_CODES + 2 * EDGE)
        nc.vector.tensor_copy(second_picked[:], evals_pool[1][:].indirect(evicted_list[:]))
        w_rows = placed("w_rows", [P, PACK, I], BF16, AT_EVALS[1])
        for h in range(2):
            nc.vector.reciprocal(invs[h][:], sums[h][:])
            for t in (2 * h, 2 * h + 1):
                nc.vector.tensor_scalar(w_rows[:, t, :], prob[t][:], invs[h][:, t % 2 : t % 2 + 1], fac_sb[:, t : t + 1], ALU.mult, ALU.mult)
        w_grouped = sbuf("w_grouped", [P, I, PACK], BF16)
        w_codes = sbuf("w_codes", [P, I], U32)
        w_scale = sbuf("w_scale", [P, I], U8)
        for cols in halves:
            nc.vector.tensor_copy(w_grouped[:, cols, :].rearrange("p (c i) t -> p c t i", i=RUN), w_rows[:, :, cols].rearrange("p t (c i) -> p c t i", i=RUN))
        for cols in halves:
            nc.vector.quantize_mx(w_codes[:, cols].bitcast(FP8X4), w_scale[:, cols], w_grouped[:, cols, :].rearrange("p i t -> p (i t)"))

        merged = []
        last = PACK - 1
        late_picked = placed("late_picked", [P, 2 * J], BF16, AT_NEG_MAX)
        turned = []
        for h in range(2):
            turned.append(psum.tile([P, 2, 2, P], F32, name="turned", tag=("product", "turned")[h]))
            for n in range(2):
                t = 2 * h + n
                if t == 0:
                    picked = first_picked[:]
                elif t == 1:
                    picked = second_picked[:]
                else:
                    picked = late_picked[:, (t - 2) * J : (t - 1) * J]
                    nc.scalar.activation(picked, evals_pool[t][:].indirect(evicted_list[:]), ACT.Copy)
                pairs = picked.bitcast(F32)
                for u in range(2):
                    nc.tensor.transpose(turned[h][:, n, u, :], pairs[:, u : J // 2 : 2], identity[:])
        for h in range(2):
            grouped = placed("vt_grouped%d" % h, [P, 2 * P * PACK], BF16, (AT_EVALS[2], AT_Y_LOW)[h])
            (nc.scalar.copy, nc.vector.tensor_copy)[h](grouped[:].bitcast(F32).rearrange("p (t e u) -> p t e u", t=2, u=2), turned[h][:].rearrange("p t u e -> p t e u"))
            codes = placed("vt_codes%d" % h, [P, 2 * P], U32, AT_EVALS[last] + h * KIB)
            scale = sbuf("vt_scale%d" % h, [P, 2 * P], U8)
            nc.vector.quantize_mx(codes[:].bitcast(FP8X4), scale[:], grouped[:])
            for n in range(2):
                merged.append(psum.tile([P, I], F32, name="merged", tag="product"))
                nc.tensor.matmul_mx(merged[-1][:], lhsT=codes[:, n * P : (n + 1) * P].bitcast(FP8X4), lhsT_scale=scale[:, n * P : (n + 1) * P],
                                    rhs=w_codes[:].bitcast(FP8X4), rhs_scale=w_scale[:], start=True, stop=True)
        kept_first = sbuf("kept_first", [P, I], F32)
        nc.scalar.activation(kept_first[:], vals_pool[0][:].indirect(kept_list[:]), ACT.Copy)
        kept_second = placed("kept_second", [P, I], F32, AT_VALS[0])
        nc.scalar.activation(kept_second[:], vals_pool[1][:].indirect(kept_list[:]), ACT.Copy)
        merged2 = placed("merged2", [P, I], F32, AT_VALS[1])
        nc.scalar.copy(merged2[:], merged[2][:])
        merged3 = sbuf("merged3", [P, HALF], F32)

        out_rows = out_0.rearrange("(p t) i -> p t i", t=PACK)
        y_low = placed("y_low", [P, 2, I], F32, AT_Y_LOW)
        y_high = sbuf("y_high", [P, 2, I], F32)
        y_grouped = sbuf("y_grouped", [P, I, PACK], BF16)
        y_codes = sbuf("y_codes", [P, I], U32)
        y_scale = sbuf("y_scale", [P, I], U8)
        for t in range(last):
            y = (y_low, y_high)[t // 2][:, t % 2, :]
            if t == 0:
                nc.vector.tensor_tensor(y, merged[t][:], kept_first[:], ALU.add)
            elif t == 1:
                for cols in halves:
                    nc.vector.tensor_tensor(y[:, cols], merged[t][:, cols], kept_second[:, cols], ALU.add)
            else:
                nc.vector.tensor_tensor(y, vals_pool[t][:].indirect(kept_list[:]), merged2[:], ALU.add)
            if t == 0:
                nc.vector.tensor_copy(merged3[:], merged[last][:, halves[0]])
            nc.sync.dma_start(out_rows[:, t, :], y)
            if t == 1:
                for cols in halves:
                    nc.scalar.copy(y_grouped[:, cols, 0:2], y_low[:, :, cols].rearrange("p t i -> p i t"))
        words_out = out_1[0].rearrange("p n t -> p (n t)").bitcast(I32)
        kept = sbuf("kept", [P, HALF], F32)
        low, high = halves
        pieces = [slice(n * P, (n + 1) * P) for n in range(I // P)]
        for cols in pieces[:2]:
            nc.vector.tensor_tensor(y_high[:, 1, cols], vals_pool[last][:].indirect(entries(kept_list, cols)), merged3[:, cols], ALU.add)
        nc.scalar.activation(kept[:], vals_pool[last][:].indirect(entries(kept_list, high)), ACT.Copy)
        for cols in pieces[2:]:
            nc.vector.tensor_tensor(y_high[:, 1, cols], merged[last][:, cols], kept[:, cols.start - HALF : cols.stop - HALF], ALU.add)
        nc.sync.dma_start(out_rows[:, last, :], y_high[:, 1, :])
        for n, cols in enumerate(pieces):
            interleave = (nc.scalar.copy, nc.vector.tensor_copy)[n // 2]
            interleave(y_grouped[:, cols, 2:4], y_high[:, :, cols].rearrange("p t i -> p i t"))
        for cols in halves:
            nc.vector.quantize_mx(y_codes[:, cols].bitcast(FP8X4), y_scale[:, cols], y_grouped[:, cols, :].rearrange("p i t -> p (i t)"))
            nc.sync.dma_start(words_out[:, cols], y_codes[:, cols].bitcast(I32))
        for quadrant in range(P // QUADRANT):
            queue = (nc.sync, nc.scalar)[quadrant % 2]
            queue.dma_start(out_2[0, PACK * quadrant : PACK * quadrant + PACK, :].bitcast(I32),
                            y_scale[QUADRANT * quadrant : QUADRANT * quadrant + PACK, :].bitcast(I32))
